import numpy as np, ml_dtypes
CORES = [23,119,17,113]
N = 4
BF = ml_dtypes.bfloat16
def gentries(a):
    return np.ascontiguousarray(a.reshape(8, 16, -1).transpose(0, 2, 1)).reshape(8, -1)
def gtable(e):
    e = np.asarray(e); return np.ascontiguousarray(e.reshape(8, -1, 16).transpose(0, 2, 1)).reshape(128, -1).astype(np.int32)
W, C, S, L0, K, CAP, RO = 4096, 128, 32, 21, 32, 256, 3
U = C * L0
def orders(rng):
    return np.argsort(rng.random((N, 8, U)), axis=-1)
def aim(z, want):
    s = np.add.reduce(z, axis=2)[:, :, 0::2]
    ends = np.stack([s[..., 0], s[..., L0 - 1]], -1).reshape(N, 8, C)
    return (want - 61 * np.roll(ends, 1, axis=0)[..., None]) & (W - 1)
def pack(z, o, cn):
    a = np.take_along_axis(z.reshape(N, 8, 16, U), np.argsort(o, axis=-1)[:, :, None, :], 3)
    return {"x": a.reshape(N, 128, U).astype(np.float32).astype(BF), "oc": np.stack([gtable(v) for v in o]), "cd": np.stack([gtable(v.reshape(8, C * K)) for v in cn])}
def setup_inputs(rng):
    o = orders(rng); z = rng.integers(0, 16, (N, 8, 16, C, L0))
    share = rng.choice(np.array([0.0, 0.0, 0.25, 0.5]), (N, 8, 1, 1, 1))
    walk = np.clip(z[..., :1] + np.add.accumulate(rng.integers(-1, 2, z.shape), axis=-1), 0, 15)
    z = np.where(rng.random((N, 8, 1, C, 1)) < share, walk, z)
    return pack(z, o, rng.integers(0, W, (N, 8, C, K)))
def setup_inputs_room(rng):
    o = orders(rng); H = C // 2; mx = (L0 + 1) // 2; lo = CAP // H + 1
    z = rng.integers(0, 4, (N, 8, 16, C, L0)) + 12 * rng.integers(0, 2, (N, 8, 16, C, L0))
    z[:, :, :, 0::2] = rng.integers(0, 16, (N, 8, 16, H, L0))
    z[:, :, :, 0::2, 0] = rng.integers(7, 9, (N, 8, 16, H)); z[:, :, :, 0::2, L0 - 1] = rng.integers(7, 9, (N, 8, 16, H))
    want = np.zeros((N, 8, C, K), np.int64); many, huge = [int(v) for v in rng.permutation(8)[:2]]
    for q in range(N):
        for g in range(8):
            oo = o[q, g].reshape(C, L0)
            pool = np.concatenate([oo[0::2].reshape(-1), oo[1::2, 0], oo[1::2, L0 - 1], np.arange(U, W)])
            want[q, g] = rng.choice(pool, (C, K))
            total = CAP + int(rng.integers(-1, 2)); more = int(rng.integers(0, H + 1))
            if q == 0: total = CAP + (0, 1, -1)[g % 3]; more = (0, H)[int(g > 0)]
            sizes = []; rem = total
            while rem > mx:
                s = int(rng.integers(lo, min(mx, rem - 2) + 1)); sizes.append(s); rem -= s
            sizes.append(rem); sizes += [2] * min(more, H - len(sizes))
            if q > 0 and g == many:
                base = CAP // H; sz = base + (np.arange(H) < CAP - base * H).astype(np.int64)
                dd = rng.integers(0, base - 1, H // 2); sz[:H // 2] += dd; sz[H // 2:2 * (H // 2)] -= dd
                sizes = [int(v) for v in rng.permutation(sz)]
            if q > 0 and g == huge:
                sizes = [int(v) for v in rng.integers(mx - 1, mx + 1, H)]
            who = np.sort(rng.permutation(H)[:len(sizes)]); whom = rng.permutation(H)[:len(sizes)]
            for w, v, s in zip(who, whom, sizes):
                c = 2 * int(v) + 1; i = s - 1 if s < mx and rng.random() < 0.5 else L0 - s
                z[q, g, :, c, i] = rng.integers(7, 9, 16)
                spot = rng.random((2, K)) < 0.5; spot[int(rng.integers(0, 2)), int(rng.integers(0, K))] = True
                want[q, g, 2 * w:2 * w + 2][spot] = oo[c, i]
    return pack(z, o, aim(z, want))
def setup_inputs_ties(rng):
    o = orders(rng); pat = rng.integers(0, 16, (4, 16)); w = rng.integers(0, 4, (N, 8, C, L0)); w[:, int(rng.integers(0, 8))] = 0
    cn = rng.integers(0, W, (N, 8, C, K)); cn[:, ::3] = cn[:, ::3, :, :1]
    return pack(np.moveaxis(pat[w], -1, 2), o, cn)
def setup_inputs_edge(rng):
    o = orders(rng); z = rng.integers(0, 16, (N, 8, 16, C, L0)); h = (L0 - 1) // 2
    at = np.where(np.arange(8)[None, :, None, None] % 2 == 0, rng.choice(np.array([0, 1, L0 - 2, L0 - 1]), (N, 8, C, K)), rng.choice(np.array([h - 1, h, h, h + 1]), (N, 8, C, K)))
    ch = 2 * rng.integers(0, C // 2, (N, 8, C, K)) + 1
    want = np.take_along_axis(o, (ch * L0 + at).reshape(N, 8, C * K), 2).reshape(N, 8, C, K)
    want = np.where(rng.random(want.shape) < 0.125, rng.integers(U, W, want.shape), want)
    two = [int(v) for v in rng.permutation(8)[:2]]
    side = (np.arange(L0) + rng.integers(0, 2, (N, 2, C, 1))) % 2
    low = rng.integers(1, 4, (N, 2, 16, C, L0)); low[:, 1] = np.where(rng.random((N, 1, C, L0)) < 0.125, 0, low[:, 1])
    v0 = 2 * rng.integers(0, C // 2, N) + 1
    i0 = 1 + np.argmin(o[:, two[0]].reshape(N, C, L0)[np.arange(N), v0][:, 1:L0 - 1], axis=1)
    side[np.arange(N), 0, v0] = (np.arange(L0) - i0[:, None] + 1) % 2
    for q in range(N): low[q, 0, :, int(v0[q]), int(i0[q]) - 1:int(i0[q]) + 2] = 0
    side[:, 0, C - 2] = (np.arange(L0) + 1) % 2; low[:, 0, :, C - 2, 0] = 0; low[:, 0, :, C - 2, L0 - 1] = 0
    z[:, two] = np.where(side[:, :, None] == 1, 15 - low, low)
    es = np.roll(np.stack([side[:, :, 0::2, 0], side[:, :, 0::2, L0 - 1]], -1).reshape(N, 2, C), 1, axis=0)[..., None]
    vic = 2 * rng.integers(0, C // 2, (N, 2, C, K)) + 1; vic[:, 0] = v0[:, None, None]
    first = np.take_along_axis(side.reshape(N, 2, U), (vic * L0 + 1).reshape(N, 2, C * K), 2).reshape(N, 2, C, K)
    pc = 1 + (first != es).astype(np.int64) + 2 * rng.integers(0, h - 1, (N, 2, C, K))
    b0 = i0[:, None, None]; last = pc[:, 0, C - 2:]
    pc[:, 0, C - 2:] = np.where(last == b0, np.where(b0 + 2 <= L0 - 2, b0 + 2, b0 - 2), last); pc[:, 0, C - 1, K - 1] = i0
    want[:, two] = np.take_along_axis(o[:, two], (vic * L0 + pc).reshape(N, 2, C * K), 2).reshape(N, 2, C, K)
    return pack(z, o, aim(z, want))
def setup_inputs_still(rng):
    o = orders(rng); z = rng.integers(0, 16, (N, 8, 16, C, L0)); s = int(rng.integers(0, N)); g, h = [int(v) for v in rng.permutation(8)[:2]]
    z[s] = z[s][..., :1].copy(); z[:, g] = z[:, g][..., :1].copy(); z[:, h, :, 1::2] = z[:, h, :, 1::2, :1].copy()
    return pack(z, o, rng.integers(0, W, (N, 8, C, K)))
def setup_inputs_spread(rng):
    o = orders(rng); top = rng.integers(1, 17, (N, 8, 1, C, L0)) * (rng.random((N, 8, 1, C, L0)) > 0.0625)
    z = np.minimum((top * rng.random((N, 8, 16, C, L0)) ** rng.choice(np.array([1.0, 2.0, 4.0]), (N, 8, 16, 1, 1))).astype(np.int64), 15)
    near = rng.integers(0, W, (N, 8, 1, 1)) + rng.integers(0, 64, (N, 8, C, K))
    return pack(z, o, np.where(rng.random((N, 8, C, 1)) < 0.5, rng.integers(0, W, (N, 8, C, K)), near) & (W - 1))
def check_inputs(d):
    bad = []; v = np.asarray(d["x"]).astype(np.float32)
    if not np.all((v >= 0) & (v <= 15) & (v == np.floor(v))): bad.append("x: whole numbers from 0 to 15")
    if not all(np.array_equal(np.sort(gentries(a), axis=-1), np.tile(np.arange(U), (8, 1))) for a in d["oc"]): bad.append("oc: every column once")
    if np.min(d["cd"]) < 0 or np.max(d["cd"]) > W - 1: bad.append("range of cd")
    return bad
def reference(x, oc, cd):
    X = np.zeros((N, 8, 16, W), np.int16); X[..., :U] = x.astype(np.float32).reshape(N, 8, 16, U).astype(np.int16)
    O = np.full((N, 8, C, S), -1, np.int64); O[..., :L0] = np.stack([gentries(a) for a in oc]).reshape(N, 8, C, L0)
    ln = np.full((N, 8, C), L0, np.int64); cn = np.stack([gentries(a) for a in cd]).astype(np.int64).reshape(N, 8, C, K)
    j = np.arange(C // 2)
    for t in range(RO):
        att = np.arange(t % 2, C, 2)
        O1, ln1 = O.copy(), ln.copy()
        for p in range(N):
            q = (p + 1 + t % (N - 1)) % N
            for g in range(8):
                o, n, xq = O[q, g], ln[q, g], X[q, g]; a, na = O[p, g][att], ln[p, g][att]
                flat = o.reshape(-1); full = np.flatnonzero(flat >= 0); pl = np.full(W, -1, np.int64); pl[flat[full]] = full
                e = np.stack([a[:, 0], a[j, na - 1]], 1).reshape(-1); xe = X[p, g][:, e]
                m = (cn[q, g] + 61 * np.add.reduce(xe, axis=0, dtype=np.int64)[:, None]) & (W - 1)
                at = pl[m]; v = at // S; i = at % S; L = n[v]
                head = 2 * i + 1 < L; size = np.where(head, i + 1, L - i)
                ok = (at >= 0) & (v % 2 != t % 2) & (i >= 1) & (i <= L - 2) & (np.repeat(na, 2)[:, None] + size <= S)
                other = flat[np.clip(at + np.where(head, 1, -1), 0, C * S - 1)]
                xm = xq[:, m]
                gain = np.add.reduce(np.abs(xm - xq[:, other]), axis=0, dtype=np.int64) - np.add.reduce(np.abs(xe[:, :, None] - xm), axis=0, dtype=np.int64)
                gain = np.where(ok, gain, 0).reshape(C // 2, 2 * K); best = np.argmax(gain, axis=1)
                b = gain[j, best]; vb, ib, hb, sb = [w.reshape(C // 2, 2 * K)[j, best] for w in (v, i, head, size)]
                s = np.lexsort((j, -b)); s = s[b[s] > 0]
                win = np.sort(s[np.unique(vb[s], return_index=True)[1]])
                win = win[np.add.accumulate(sb[win]) <= CAP]
                k = U + CAP * t
                for w in win:
                    c, vc, ic, size_w = att[w], vb[w], ib[w], sb[w]
                    if hb[w]: part, rest = o[vc, ic::-1], o[vc, ic + 1:n[vc]]
                    else: part, rest = o[vc, ic:n[vc]], o[vc, :ic]
                    own = a[w, :na[w]]
                    if best[w] < K: own = own[::-1]
                    new = np.concatenate([own, np.arange(k, k + size_w)]); X[p, g][:, k:k + size_w] = xq[:, part]; k += size_w
                    O1[p, g, c, :len(new)] = new; ln1[p, g, c] = len(new)
                    O1[q, g, vc] = -1; O1[q, g, vc, :len(rest)] = rest; ln1[q, g, vc] = len(rest)
        O, ln = O1, ln1
    ix = O.reshape(N, 8, 1, C * S); y = np.where(ix >= 0, np.take_along_axis(X, np.maximum(ix, 0), 3), 0)
    return {"y": y.reshape(N, 128, C * S).astype(np.float32).astype(BF), "yo": O.reshape(N, 8, C * S).astype(np.float32)}

@@ -1,0 +1,711 @@
+from concourse.mybir import AluOpType as A, AxisListType, ActivationFunctionType as AF
+
+U, NEWC, RO = 2688, 256, 3
+XVN = 34 * 64
+ZC = U + RO * NEWC
+H16, P25, P26 = 65536.0, 2.0 ** 25, 2.0 ** 26
+
+DIAG = {
+    "d_as": {5: 1, 8: -1, 15: 1}, "d_ra": {4: 1, 5: -1, 8: 2}, "d_rv": {6: -1, 7: 1, 9: 1}, "d_ac": {7: -1},
+    "d_ba": {14: 1}, "d_one": {6: -128},
+    "i_ba": {4: -1, 5: 1, 7: -1, 8: -2, 12: 256, 13: 256}, "i_as": {5: 1, 7: -1, 8: -1}, "i_la": {4: 1, 8: 1},
+    "i_e": {13: 1}, "i_ne": {13: -1}, "i_j": {3: 1}, "i_one": {5: -1, 7: 2, 8: 1, 10: -256},
+    "d_e": {11: 1, 13: 1}, "d_ne": {11: -1, 13: -1},
+    "i_k": {4: 1, 5: -1, 7: 1, 8: 2, 12: -256, 13: -256},
+    "c_l": {4: -1, 6: 1, 8: -1, 12: 256, 13: 256}, "c_r": {5: -1, 7: 1, 8: 1, 10: 256, 11: 256},
+}
+COLS = {
+    "s_i": {4: 1, 5: -1, 6: -1, 7: 1, 8: 2, 10: 256, 11: 256, 12: -256, 13: -256},
+    "s_e": {6: 128, 14: -64}, "s_j": {3: 1, 14: 1},
+    "s_c": {5: 20, 6: 1, 7: -19, 8: -20, 10: -5120, 11: -5120, 14: 64},
+    "kh": {0: H16, 12: -H16, 13: H16, 2: -H16, 6: -P26, 7: -P26},
+    "dh": {1: H16, 10: -H16, 11: H16, 0: -H16, 12: H16, 13: -H16},
+    "sh": {5: 1, 9: 1, 4: -1}, "ch": {4: -P25, 8: P25},
+    "kl": {5: 64, 9: -1024, 3: 1}, "dl": {9: 2048, 4: 64, 5: -64},
+}
+CN = list(COLS)
+DN = list(DIAG)
+NC_, ND = len(CN), len(DN)
+
+SIZES = {"F": {}, "B": {}, "I": {}, "U": {}}
+def _a(ar, **kw):
+    SIZES[ar].update(kw)
+_a("F", stat=16 + U, T1=16 + U + 256, T2=16 + U + 512, spos=U, iot=U, numb=ZC + 16, cp=672, YO=4096,
+   pcol=16, g8=8, x144=144, pat=288, r16=288, sgm=288, rt=16 * NC_, rt2=16 * ND, seg=16 * ND, cw=16 * NC_, dw=16 * ND, sb=8,
+   idf=128, cdf=256, cdt=256, cdT=256, pm=4 * 128, kM=256, kt=256, kk=256, kf=256, red=8, rep=128, he=64, zs=8, mf=256,
+   S1=64, S=64, jc=64, tq=4 * 80, best=4, size=64, ws=64, tot=64, ones=128, ac0=64, cnt=2, pos0=64, pj=64, j32=64, j256=64,
+   mm=128, ms=64, o1=64, o2=64, val=64, b64=64, sw0=320, sw1=320, sw2=320, Fs=256, F2=256, cap=256,
+   kw=16, kkw=16, pw=16, iv=16, w2=16, vq=4, vx=4, vm=4, cs=4, e80=8, e81=8, e82=8, e64=8, c8=8,
+   mo0=144, mo1=144, mo2=144, dl0=208, dl1=144, dl2=144, ifl=256, dy2=128, cut=64,
+   rs=3 * 128, wr=12, xa=4, xb=4, xc=4, xd=4, xe_=4, xf=4, xg=4, xh=4, xi=4, c21w=8, y1=68, xP=136, xt=136, xm=136, xu=136,
+   c21=128, bc=16, fa=128, fb=128, fc=128, fd=128, fe=128, ff=128, fg=128, fh=128, ga=64, gb=64, gd=64, ge=64, gf=64, gg=64,
+   gh=64, gi=64, gj=64, ha=64, hb=64, hc=64, hf=64, R0=192, R1=192, R2=192, C0=192, C1=192, C2=192)
+_a("B", xc_=16 + U + 512, xb_=ZC + 16, ad=U + 32, G=4096, MN=4096, Y=4096, XV=XVN + 16, sB=U, bo=128, nbo=128, idb=128, nid=128,
+   qz=144, q1=144, q14=144, dg=128 * ND, ds=3 * 128, pt=3 * 336, fR=128, fL=128, fZ=128, w0=512, w1=512, wc=1024, wf=32, wh=32, wl=32,
+   onb=128, jb=64, kb=256, eo0=256, eo1=256, eo2=256, el0=640, el1=640, el2=640, W=256, q_as=64, q_ac=64, q_ra=64, q_rv=64,
+   q_ba=64, q_gn=64, q_D=64, g2=128, g2a=64, po0=256, po1=256, po2=256, ex=128, lr=64, cb=128, rb=192, nad=272)
+_a("I", oc=168, cd=256, pi=4, mi=256, mj=256, ri=8, rj=8, Hi=64, vf=64, dm=64, g16=64, mu=64, hd=64, pl=64, d64=64,
+   Fw=16, cc=16, ww=16, bi=4, bx=4, bm=4, bd=4, e8i=8)
+_a("U", ocu=168, cl=168, ml=256, l_rep=8, l_p0=8, l_off=4, l_pos=16, wo0=16, wo1=16, wl0=16, wl1=16, l_end=8, l_xv=136, l_f=256)
+OFF = {}
+TOT = {}
+for _ar, _d in SIZES.items():
+    _o = 0
+    for _n, _s in _d.items():
+        OFF[_n] = (_ar, _o, _s)
+        _o += (_s + 15) // 16 * 16
+    TOT[_ar] = _o
+SCRATCH = {"F": ("sbuf", [128, TOT["F"]], "float32"), "B": ("sbuf", [128, TOT["B"]], "bfloat16"),
+           "I": ("sbuf", [128, TOT["I"]], "int32"), "U": ("sbuf", [128, TOT["U"]], "uint16"),
+           "TR": ("sbuf", [128, 8, 32], "float32")}
+for _b in range(8):
+    SCRATCH["P%d" % _b] = ("psum", [128, 512], "float32")
+SEMAPHORES = ["cv", "ca", "ct", "cg", "ls", "lx0", "lx1", "loc", "lcd", "so"] + \
+    ["%s%d" % (n, t) for n in ("ae", "ad", "ap", "ai") for t in range(RO)]
+
+
+def rank_program(g, core, T, topo):
+    rank = T.rank_of(core)
+    if rank is None:
+        return
+    NR = len(T.cores)
+    Q = {"v": g.vector, "a": g.scalar, "t": g.tensor, "g": g, "s": g.sync}
+    SEM = {"v": "cv", "a": "ca", "t": "ct", "g": "cg"}
+    cnt = {"cv": 0, "ca": 0, "ct": 0, "cg": 0}
+    seen = {}
+    lastw = {}
+    readers = {}
+
+    def s(n, a=0, b=None, st=None):
+        ar, o, z = OFF[n]
+        b = z if b is None else b
+        return T[ar][:, o + a:o + b] if st is None else T[ar][:, o + a:o + b:st]
+
+    def col(n, j):
+        return s(n, j, j + 1)
+
+    def P(b, a=0, e=512, st=None):
+        return T["P%d" % b][:, a:e] if st is None else T["P%d" % b][:, a:e:st]
+
+    def need(q, sem, c):
+        if q == "t" and sem == "ct":
+            return
+        if seen.get((q, sem), 0) < c:
+            Q[q].wait_ge(T.sem[sem], c)
+            seen[(q, sem)] = c
+
+    def deps(q, r, w):
+        evs = {}
+        def add(ev):
+            if ev is not None:
+                evs[ev[0]] = max(evs.get(ev[0], 0), ev[1])
+        for k in r:
+            add(lastw.get(k))
+            if k[0] == "P" and len(k) == 2:
+                for ev in readers.get(k, []):
+                    if ev[0] != SEM.get(q):
+                        add(ev)
+        for k in w:
+            add(lastw.get(k))
+            for ev in readers.get(k, []):
+                add(ev)
+        for sem, c in evs.items():
+            need(q, sem, c)
+
+    def done(ev, r, w):
+        for k in r:
+            readers.setdefault(k, []).append(ev)
+        for k in w:
+            lastw[k] = ev
+            readers[k] = []
+
+    def op(q, fn, r, w):
+        r = r.split(); w = w.split()
+        deps(q, r, w)
+        sem = SEM[q]
+        fn().then_inc(T.sem[sem], 1)
+        cnt[sem] += 1
+        done((sem, cnt[sem]), r, w)
+
+    def mark(q, k):
+        lastw[k] = (SEM[q], cnt[SEM[q]])
+
+    V = g.vector
+    def cp(o, i, r, w): op("v", lambda: V.tensor_copy(o, i), r, w)
+    def tt(o, a, b, f, r, w): op("v", lambda: V.tensor_tensor(o, a, b, f), r, w)
+    def ts(o, a, s1, f, r, w): op("v", lambda: V.tensor_scalar(o, a, s1, None, f), r, w)
+    def t2(o, a, s1, f, s2, f2, r, w): op("v", lambda: V.tensor_scalar(o, a, s1, s2, f, f2), r, w)
+    def red(o, a, f, r, w): op("v", lambda: V.tensor_reduce(o, a, AxisListType.X, f), r, w)
+    def scan(o, a, b, ini, f, f2, r, w): op("v", lambda: V.tensor_tensor_scan(o, a, b, ini, f, f2), r, w)
+    def ms(o, c, w): op("v", lambda: V.memset(o, c), "", w)
+    def act(o, i, r, w, f=AF.Identity, **kw): op("a", lambda: g.scalar.activation(o, i, f, **kw), r, w)
+    def mm(o, l, rh, st, sp, r, w): op("t", lambda: g.tensor.matmul(o, l, rh, st, sp), r, w)
+    def io_(o, pat, base, cm, w, i32=False, r=""):
+        if i32:
+            op("g", lambda: g.iota(o, pat, base, cm), r, w)
+        else:
+            op("g", lambda: g.iota(o, pat, base, cm, allow_small_or_imprecise_dtypes=True), r, w)
+    def fill(n, a, b, c, w): io_(s(n, a, b), [[0, b - a]], c, 0, w)
+    def dma(q, o, i, sem, r, w):
+        r = r.split(); w = w.split()
+        deps(q, r, w)
+        Q[q].dma_start(o, i).then_inc(T.sem[sem], 16)
+        cnt[sem] = cnt.get(sem, 0) + 16
+        done((sem, cnt[sem]), r, w)
+    eng = [e for e in topo.engines(T.cores[0], T.cores[1])
+           if all(e in topo.engines(a, b) for a in T.cores for b in T.cores if a != b)]
+    emask = sum(1 << e for e in eng)
+    def send(dst, o, i, sem, r):
+        deps("g", r.split(), [])
+        rid, pid, _e = topo.addr(dst)
+        g.remote_dma(o, i, T.sem[sem], T.sem.ls, pid, rid, emask)
+        cnt["ls"] = cnt.get("ls", 0) + len(eng)
+    def landed(sem, w):
+        cnt[sem] = len(eng)
+        for k in w.split():
+            lastw[k] = (sem, cnt[sem])
+    def victim(t): return T.cores[(rank + 1 + t % (NR - 1)) % NR]
+    def attacker(t): return T.cores[(rank - 1 - t % (NR - 1)) % NR]
+    def dg(n): k = DN.index(n); return s("dg", 128 * k, 128 * k + 128)
+    def cw(n): return col("cw", 16 * CN.index(n) + 15)
+    def keys(n, k): return " ".join("%s%d" % (n, i) for i in range(k))
+    def R(t, k): return s("R%d" % t, 64 * k, 64 * k + 64)
+    def C(t, k): return s("C%d" % t, 64 * k, 64 * k + 64)
+    def dga(a, b):
+        for k in range(a, b):
+            act(dg(DN[k]), s("idb"), "idb dw", DN[k], scale=col("dw", 16 * k + 15))
+
+    dma("s", s("oc"), T.oc[:], "loc", "", "oc")
+    dma("a", s("xc_", 16, 16 + U // 2), T.x[:, 0:U // 2], "lx0", "", "xc0")
+    dma("s", s("xc_", 16 + U // 2, 16 + U), T.x[:, U // 2:U], "lx1", "", "xc1")
+    dma("s", s("cd"), T.cd[:], "lcd", "", "cd")
+
+    HW = 336
+    ms(s("ones"), 1.0, "ones")
+    ms(s("rt"), 0.0, "rt")
+    ms(s("rt2"), 0.0, "rt2")
+    io_(col("pi", 0), [[0, 1]], 0, 1, "pi", True)
+    io_(s("pat"), [[0, 18], [1, 16]], 0, 0, "pat")
+    io_(s("x144"), [[1, 144]], 0, 0, "x144")
+    io_(s("pt", 0, HW), [[0, 16], [1, 21]], 0, 0, "pt0")
+    io_(s("pt", HW, 2 * HW), [[0, 8], [-1, 2], [0, 21]], 1, 0, "pt1")
+    io_(s("pt", 2 * HW, 3 * HW), [[1, 8], [0, 42]], 0, 0, "pt2")
+    io_(s("rep"), [[1, 8], [0, 16]], 0, 0, "rep")
+    for k, n in enumerate(CN):
+        for f, c in COLS[n].items():
+            act(col("rt", 16 * k + f), col("ones", 0), "rt ones", "", scale=float(c))
+    mark("a", "rt")
+    deps("v", ["rt2"], [])
+    for k, n in enumerate(DN):
+        for f, c in DIAG[n].items():
+            if k < 6:
+                act(col("rt2", 16 * k + f), col("ones", 0), "rt2 ones", "", scale=float(c))
+            elif k < 9:
+                ms(col("rt2", 16 * k + f), float(c), "")
+            else:
+                io_(col("rt2", 16 * k + f), [[0, 1]], int(c), 0, "", r="rt2")
+    mark("a", "rt2a"); mark("g", "rt2g"); mark("v", "rt2v")
+    io_(s("mm"), [[0, 16], [1, 8]], 0, 0, "mm")
+    io_(s("kM"), [[-2048, 32], [0, 8]], 31 * 2048 + 1024, 0, "kM")
+    for kh in range(2):
+        for j1 in range(2):
+            k = 2 * kh + j1
+            op("g", lambda: g.affine_select(s("pm", 128 * k, 128 * k + 128), s("ones"), [[32, 4], [1000 - 2000 * j1, 2], [2, 16]],
+                                            A.is_equal, 0.0, kh + 1000 * j1, -1), "ones", "pm%d" % k)
+    ts(col("pi", 1), col("pi", 0), 15, A.bitwise_and, "pi", "pi1")
+    ts(col("pi", 2), col("pi", 0), 4, A.arith_shift_right, "pi", "pi2")
+    ts(col("pi", 3), col("pi", 0), 1, A.bitwise_and, "pi", "pi3")
+    for n in ("fR", "fL", "fZ"):
+        ms(s(n), 0.0, n)
+    cp(s("pcol", 0, 4), s("pi"), "pi pi1 pi2 pi3", "pcol")
+    ms(s("ad", 0, 16), 0.0, "ad_a")
+    for n in ("w0", "w1", "wf", "wl", "wc"):
+        ms(s(n), 0.0, n)
+    cp(s("ocu"), s("oc"), "oc", "ocu")
+    rc, gc_, pc = col("pcol", 1), col("pcol", 2), col("pcol", 0)
+    ts(s("r16"), s("pat"), rc, A.is_equal, "pat pcol", "r16")
+    ts(s("sgm"), s("pat"), 0.5, A.is_gt, "pat", "sgm")
+    ts(s("g8"), s("x144", 0, 8), gc_, A.is_equal, "x144 pcol", "g8")
+    ts(s("idb"), s("x144", 0, 128), pc, A.is_equal, "x144 pcol", "idb")
+    t2(s("nid"), s("x144", 0, 128), pc, A.is_equal, -1.0, A.mult, "x144 pcol", "nid")
+    tt(s("seg", 0, 16 * NC_), s("rt"), s("r16", 0, 16 * NC_), A.mult, "rt r16", "seg")
+    for n, fs in (("fR", (1, 10)), ("fL", (0, 12)), ("fZ", (2,))):
+        deps("v", [n], [])
+        for f in fs:
+            cp(s(n, f, 128, 16), s("g8"), "g8", "")
+        mark("v", n)
+    scan(s("cw"), s("sgm", 0, 16 * NC_), s("seg", 0, 16 * NC_), 0.0, A.mult, A.add, "seg sgm", "cw")
+    t2(col("pcol", 4), gc_, 16.0, A.mult, 15.0, A.add, "pcol", "pc4")
+    for k, n in enumerate(("s_i", "s_e", "s_j")):
+        ts(s("ds", 128 * k, 128 * k + 128), s("idb"), cw(n), A.mult, "idb cw", "ds%d" % k)
+    t2(s("sb"), s("x144", 0, 64, 8), cw("s_j"), A.mult, cw("s_c"), A.add, "cw x144", "sb")
+    for k in range(3):
+        mm(P(7, 0, HW), s("ds", 128 * k, 128 * k + 128), s("pt", HW * k, HW * k + HW), k == 0, k == 2, "ds%d pt%d" % (k, k), "P7")
+    cp(s("cdf"), s("cd"), "cd", "cdf")
+    t2(col("pcol", 5), col("pcol", 3), -2048.0, A.mult, 2048.0, A.add, "pcol", "pc5")
+    ms(s("xc_", 0, 16), 0.0, "xcd")
+    ms(s("stat", 0, 16), 100.0, "statd")
+    op("v", lambda: V.transpose(s("cdt"), s("cdf")), "cdf", "cdt")
+    cp(s("cp", 0, HW), P(7, 0, HW), "P7", "cpa")
+    cp(s("cp", HW, 2 * HW), P(7, 0, HW), "P7", "cpb")
+    ms(s("wc", 1, 1024, 4), -1024.0, "wc")
+    ms(s("eo0", 0, 128), 21.0, "eo0c")
+    t2(s("qz"), s("x144"), col("pcol", 4), A.is_equal, 61.0, A.mult, "x144 pc4", "qz")
+    ms(s("wc", 3, 1024, 4), 31.5 * P25, "wc")
+    ts(s("bo"), s("rep"), gc_, A.is_equal, "rep pcol", "bo")
+    ts(col("pcol", 7), rc, 42.0, A.mult, "pcol", "pc7")
+    cp(s("l_rep"), s("x144", 0, 8), "x144", "l_rep")
+
+    def gx(c):
+        act(s("xb_", 672 * c, 672 * c + 672), s("xc_", 16, 16 + U).indirect(s("ocu", 42 * c, 42 * c + 42)), "xc0 xc1 ocu", "xb%d" % c)
+    def diff(h):
+        lo = max(HW * h, 1); hi = HW * h + HW; b = 2 + h % 2
+        k = "xb%d xb%d" % (h // 2, max(h * HW - 1, 0) // 672)
+        mm(P(b, 0, hi - lo), s("idb"), s("xb_", lo, hi), True, False, k + " idb", "P%d" % b)
+        mm(P(b, 0, hi - lo), s("nid"), s("xb_", lo - 1, hi - 1), False, True, k + " nid", "P%d" % b)
+    def dabs(h):
+        lo = max(HW * h, 1); hi = HW * h + HW; b = 2 + h % 2
+        act(s("ad", 15 + lo, 15 + hi), P(b, 0, hi - lo), "P%d ad_a" % b, "ad%d" % h, AF.Abs)
+    def fields(h):
+        lo = HW * h; hi = lo + HW; b = 4 + h % 2
+        mm(P(b, 0, HW), s("fZ"), s("xb_", lo, hi), True, False, "fZ xb%d" % (h // 2), "P%d" % b)
+        mm(P(b, 0, HW - 1), s("fR"), s("ad", 16 + lo, 15 + hi), False, False, "fR ad%d" % h, "P%d" % b)
+        mm(P(b, 0, HW), s("fL"), s("ad", 15 + lo, 15 + hi), False, True, "fL ad_a ad%d" % h, "P%d" % b)
+    def fev(h):
+        lo = HW * h; b = 4 + h % 2
+        act(s("spos", lo, lo + HW), P(b, 0, HW), "P%d sb" % b, "sp%d" % h, bias=col("sb", h))
+    XBK = keys("xb", 4)
+    gx(0)
+    for c in range(4):
+        a, b = 2 * c, 2 * c + 1
+        diff(a); diff(b)
+        if c in (1, 2):
+            gx(c + 1)
+        dabs(a); dabs(b); fields(a); fields(b)
+        if c == 0:
+            gx(1)
+        if c == 2:
+            act(s("eo0", 128, 256, 2), s("xb_", 0, U, 42), XBK, "eo0a")
+            act(s("eo0", 129, 256, 2), s("xb_", 20, U, 42), XBK, "eo0b")
+            send(victim(0), s("el0", 0, 256), s("eo0"), "ae0", "eo0a eo0b eo0c")
+        if c == 3:
+            act(T.TR[:, :, :], s("cdt"), "cdt", "TR")
+        fev(a); fev(b)
+    for k in range(4):
+        mm(P(6, 128 * (k // 2), 128 * (k // 2) + 128), s("pm", 128 * k, 128 * k + 128), T.TR[:, :, 16 * (k % 2):16 * (k % 2) + 16],
+           k % 2 == 0, k % 2 == 1, "TR pm%d" % k, "P6")
+    for o, n in enumerate(("kh", "dh", "sh", "ch")):
+        act(s("wh", o, 32, 4), s("g8"), "g8 cw", "wh%d" % o, scale=cw(n))
+    for o, n in enumerate(("kl", "dl")):
+        act(s("wl", o, 32, 4), s("g8"), "g8 cw wl", "wl%d" % o, scale=cw(n))
+    act(s("wf", 0, 32, 4), s("g8"), "g8 wf", "wf0", scale=2 * H16)
+    act(s("wc", 0, 1024, 4), s("kM"), "kM wc", "wc")
+    act(s("onb"), s("ones"), "ones", "onb")
+    act(s("idf"), s("idb"), "idb", "idf")
+    for kh in range(2):
+        for B in range(8):
+            act(s("cdT", kh * 128 + B, kh * 128 + 128, 8), P(6, kh * 128 + 16 * B, kh * 128 + 16 * B + 16), "P6", "")
+    mark("a", "cdT")
+
+    io_(s("xt", 0, 68), [[1, 17], [672, 4]], 21, 0, "xta")
+    io_(s("xt", 68, 136), [[-1, 17], [672, 4]], 41, 0, "xtb")
+    io_(s("jc"), [[-32, 64]], 127 * 32, 0, "jc")
+    io_(s("j256"), [[1, 64]], 256, 0, "j256")
+    io_(s("c8"), [[1088, 2], [16, 4]], 0, 0, "c8")
+    io_(s("jb"), [[1, 64]], 0, 0, "jb")
+    io_(s("tq", 64, 320, 80), [[0, 4]], 32768, 0, "tqs")
+    io_(s("kkw"), [[16, 16]], 0, 0, "kkw")
+    fill("XV", XVN, XVN + 16, 0, "xvp"); fill("lr", 0, 64, 21, "lr"); fill("sw0", 0, 320, 0, "sw0")
+    fill("mo0", 64, 80, 0, "mo0d"); fill("mo1", 64, 80, 0, "mo1d")
+    io_(s("kb"), [[1, 256]], 0, 0, "kb")
+    io_(s("c21w"), [[21, 2], [672, 4]], 0, 0, "c21w")
+    io_(s("xP", 0, 68), [[1, 17], [0, 4]], 0, 0, "xPa")
+    io_(s("y1"), [[1, 17], [0, 4]], 1, 0, "y1")
+    io_(s("c21"), [[21, 2], [42, 64]], 0, 0, "c21")
+    fill("T1", 0, 16, 100, "T1d"); fill("T2", 0, 16, 100, "T2d"); fill("T2", 16 + U, 16 + U + 256, 100, "T2e")
+    fill("dl0", 144, 208, 128, "dy1o"); fill("dy2", 0, 64, 0, "dy2o"); fill("xb_", ZC, ZC + 16, 0, "xbz")
+    fill("numb", ZC, ZC + 16, -1, "numbz"); fill("nad", 0, 16, 0, "nad0"); fill("nad", 256, 272, 0, "nad1")
+    fill("xa", 0, 4, 21, "xa"); fill("xe_", 0, 4, 20, "xe_"); fill("xh", 0, 4, 3300 - 4096 * 21, "xh")
+    io_(s("iot"), [[1, U]], 0, 0, "iot")
+    act(s("vq"), s("x144", 0, 64, 16), "x144 pcol", "vq", bias=rc)
+    act(s("xu"), s("xt"), "xta xtb pc7", "xu", bias=col("pcol", 7))
+    for c in range(4):
+        op("v", lambda: V.tensor_tensor(s("stat", 16, 16 + U).indirect(s("ocu", 42 * c, 42 * c + 42)), s("spos", 672 * c, 672 * c + 672), s("cp"), A.add),
+           "ocu cpa cpb sp%d sp%d" % (2 * c, 2 * c + 1), "stat")
+        if c == 0:
+            t2(s("w0", 0, 512, 4), s("mm"), gc_, A.is_equal, -H16, A.mult, "mm pcol w0", "w0a")
+            t2(s("w1", 3, 512, 4), s("mm"), gc_, A.is_equal, -P25 / 16, A.mult, "mm pcol w1", "w1a")
+            tt(s("seg"), s("rt2"), s("r16"), A.mult, "rt2a rt2g rt2v r16", "seg")
+            scan(s("dw"), s("sgm"), s("seg"), 0.0, A.mult, A.add, "seg sgm", "dw")
+
+    def late_act():
+        act(s("kkw"), s("kkw"), "kkw pcol", "kkw", bias=rc)
+        act(s("j32"), s("x144", 0, 64), "x144", "j32", scale=32768.0)
+        act(s("c8"), s("c8"), "c8 pcol", "c8", bias=rc)
+        for t in range(2):
+            act(col("mo%d" % t, 64), col("r16", 6), "r16 mo%dd" % t, "mo%dd" % t, scale=100.0)
+        act(s("kw"), s("kkw"), "kkw", "kw", scale=64.0)
+        act(s("q1"), s("qz"), "qz", "q1", AF.Sign)
+        act(s("cap"), s("r16", 1, 257), "r16", "cap", scale=1e9)
+        act(s("q14"), s("q1"), "q1 r16", "q14", scale=col("r16", 14))
+        act(s("nbo"), s("bo"), "bo", "nbo", scale=-1.0)
+
+    def later_act():
+        act(s("q1"), s("q1"), "q1", "q1", scale=1.0 / 16)
+        act(s("c21w"), s("c21w"), "c21w pc7", "c21w", bias=col("pcol", 7))
+        for k, f in enumerate((15, 9, 14)):
+            act(s("rs", 128 * k, 128 * k + 128), s("bo"), "bo r16", "rs%d" % k, scale=col("r16", f))
+
+    def unpack(t):
+        for k in range(3):
+            mm(P(7, 64 * k, 64 * k + 64), s("rs", 128 * k, 128 * k + 128), s("dl%d" % t, 80, 144), True, True, "dl%d rs%d" % (t, k), "P7")
+        if t < RO - 1:
+            act(s("rb"), P(7, 0, 192), "P7", "rb")
+        act(s("R%d" % t), P(7, 0, 192), "P7", "R%d" % t)
+
+    for t in range(RO):
+        lim = U + NEWC * t
+        el = "el%d" % t
+        landed("ae%d" % t, el)
+        xck = "xc0 xc1 xcd"
+        if t == 0:
+            tab, tk = "stat", "stat statd"
+            xbk = XBK
+        else:
+            tab = "T%d" % t
+            landed("ad%d" % (t - 1), "dl%d" % (t - 1))
+            landed("ap%d" % (t - 1), "xn%d" % (t - 1))
+            landed("ai%d" % (t - 1), "wl%d_" % (t - 1))
+            if t == 1:
+                dk, win = "dl0 dy1o", s("dl0", 80, 208)
+            else:
+                tt(s("dy2", 64, 128), s("dl1", 80, 144), s("cut"), A.add, "dl1 cut", "dy2")
+                dk, win = "dy2 dy2o", s("dy2")
+            tt(s(tab, 16, 16 + U // 2), win.indirect(s("cl", 0, 84)), s("stat", 16, 16 + U // 2), A.add, dk + " cl stat", tab + "a")
+            unpack(t - 1)
+            for r in range(16):
+                mm(P(7, 256, 268), s("q1", 15 - r, 143 - r), s("rb", r, 192, 16), r == 0, r == 15, "q1 rb", "P7")
+            act(s("wr"), P(7, 256, 268), "P7", "wr")
+            act(s("xf"), s("wr", 4, 8), "wr", "xf", scale=-2.0, bias=1.0)
+            tt(s("xc"), s("xa"), s("wr", 0, 4), A.add, "xa wr", "xc")
+            tt(s("xd"), s("wr", 8, 12), s("xa"), A.subtract, "xa wr", "xd")
+            tt(s("xg"), s("xe_"), s("wr", 4, 8), A.mult, "xe_ wr", "xg")
+            tt(s("xi"), s("xg"), s("c21w", 0, 4) if t == 1 else s("xb"), A.add, "xg xb c21w", "xi")
+            tt(s(tab, 16 + U // 2, 16 + U), win.indirect(s("cl", 84, 168)), s("stat", 16 + U // 2, 16 + U), A.add, dk + " cl stat", tab + "b")
+            for q in range(4):
+                act(s("xP", 68 + q, 136, 4), s("y1", q, 68, 4), "y1 xc", "xP%d" % q, scale=-1.0, bias=col("xc", q))
+            act(s("xd"), s("xd"), "xd", "xd", bias=float(lim - NEWC))
+            for q in range(4):
+                act(s("xm", q, 136, 4), s("xP", q, 136, 4), "xPa xh xP%d" % q, "xm%d" % q, scale=4096.0, bias=col("xh", q))
+            for q in range(4):
+                act(s("xt", q, 136, 4), s("xP", q, 136, 4), "xf xi xP%d" % q, "xt%d xta xtb" % q, scale=col("xf", q), bias=col("xi", q))
+            for q in range(4):
+                act(s("xu", q, 136, 4), s("xP", q, 136, 4), "xd xP%d" % q, "xu%d" % q, bias=col("xd", q))
+            xck += " xn0" + (" xn1" if t == 2 else "")
+            xbk = XBK + " xbn0" + (" xbn1" if t == 2 else "")
+            tk = "%sa %sb %sd %sn" % (tab, tab, tab, tab) + (" T2e" if t == 2 else "")
+        if t > 0:
+            n0 = 16 + lim - NEWC
+            xn = "xn%d" % (t - 1)
+            mm(P(2, 0, 255), s("idb"), s("xc_", n0 + 1, n0 + 256), True, False, xn + " idb", "P2")
+            mm(P(2, 0, 255), s("nid"), s("xc_", n0, n0 + 255), False, True, xn + " nid", "P2")
+            act(s("nad", 1, 256), P(2, 0, 255), "P2 nad0 nad1", "nad", AF.Abs)
+        for r in range(16):
+            mm(P(6, 0, 8), s("qz", 15 - r, 143 - r), s(el, 128 + r, 256, 16), r == 0, r == 15, "qz " + el, "P6")
+        act(s("zs"), P(6, 0, 8), "P6", "zs", bias=float(4096 - lim))
+        for B in range(8):
+            act(s("mf", B, 256, 8), s("cdT", B, 256, 8), "cdT zs", "mf%d" % B, bias=col("zs", B))
+        if t > 0:
+            act(s("ifl"), s("dl%d" % (t - 1), 0, 80).indirect(s("wl%d" % (t - 1))), "dl%d wl%d_" % (t - 1, t - 1), "ifl")
+            mm(P(3, 0, 256), s("fZ"), s("xc_", n0, n0 + 256), True, False, xn + " fZ", "P3")
+            mm(P(3, 0, 256), dg("i_k"), s("kb"), False, False, "kb i_k", "P3")
+            mm(P(3, 0, 256), s("fL"), s("nad", 0, 256), False, False, "fL nad", "P3")
+            mm(P(3, 0, 256), s("fR"), s("nad", 1, 257), False, False, "fR nad", "P3")
+            mm(P(3, 0, 256), s("idf"), s("ifl"), False, True, "idf ifl", "P3")
+        for k in range(3):
+            act(s(el, 256 + 128 * k, 384 + 128 * k), s(el, 128, 256), el, el + "x%d" % k)
+        if t > 0:
+            act(s("xb_", lim - NEWC, lim), s("xc_", n0, n0 + 256), xn, "xbn%d" % (t - 1))
+            act(s(tab, n0, n0 + 256), P(3, 0, 256), "P3", tab + "n")
+        else:
+            dga(6, 11)
+        for b in range(2):
+            mm(P(b), s(el, 128, 256), s("w0"), True, False, "w0a " + el, "P%d" % b)
+            mm(P(b), s(el, 0, 128), s("w1"), False, False, "w1a " + el, "P%d" % b)
+            o = OFF["onb"][1]; o2 = OFF["wc"][1]
+            mm(P(b), T.B[0:1, o:o + 128], T.B[0:1, o2 + 512 * b:o2 + 512 * b + 512], False, False, "onb wc", "P%d" % b)
+        cp(s("mi"), s("mf"), keys("mf", 8), "mi")
+        ts(s("mj"), s("mi"), 4095, A.bitwise_and, "mi", "mj")
+        t2(s("ml"), s("mj"), float(4096 - lim - 16), A.subtract, 0.0, A.max, "mj", "ml")
+        cb = (0, 4, 8, 12, 16, 20, 24, 28, 31, 32)
+        for c in range(9):
+            a, b = 128 * cb[c], 128 * cb[c + 1]
+            lst = s("ml", a // 16, b // 16)
+            tt(s("MN", a, b), s("xc_", 0, 16 + lim).indirect(lst), s(el, 128, 128 + b - a), A.min,
+               "ml %s %s %sx0 %sx1 %sx2" % (xck, el, el, el, el), "MN%d" % c)
+            act(s("G", a, b), s(tab, 0, 16 + lim).indirect(lst), "ml " + tk, "G%d" % c, AF.Relu)
+            for k in range(cb[c], cb[c + 1]):
+                b = k // 16; o = P(b, 32 * (k % 16), 32 * (k % 16) + 32)
+                mm(o, s("MN", 128 * k, 128 * k + 128), s("wf"), False, False, "wf0 MN%d" % c, "P%d" % b)
+                mm(o, s("G", 128 * k, 128 * k + 128), s("wh"), False, False, keys("wh", 4) + " G%d" % c, "P%d" % b)
+                mm(o, s("G", 128 * k, 128 * k + 128), s("wl"), False, k % 16 == 15, "wl0 wl1 G%d" % c, "P%d" % b)
+        if t == 0:
+            cp(s("l_xv"), s("xu"), "xu", "l_xv")
+        else:
+            tt(s("xm"), s("xm"), s("xu"), A.min, keys("xm", 4) + " " + keys("xu", 4), keys("xm", 4))
+            tt(s("xm"), s("xm"), s("xt"), A.max, "xm0 " + keys("xt", 4), keys("xm", 4))
+            t2(s("l_xv"), s("xm"), 0.0, A.max, float(lim - 1), A.min, "xm0", "l_xv")
+        act(s("XV", 0, XVN), s("xb_", 0, lim).indirect(s("l_xv")), "l_xv " + xbk, "XV")
+        if t == 0:
+            late_act()
+            act(s("sB", 0, 1008), s("stat", 16, 16 + 1008), "stat", "sB0")
+        else:
+            act(s("numb", 672 * (t - 1), 672 * t), s("iot").indirect(s("ocu", 42 * (t - 1), 42 * t)), "iot ocu", "numb%d" % (t - 1))
+
+        for b in range(2):
+            ts(s("kM", 128 * b, 128 * b + 128), P(b, 2, 512, 4), 0.0, A.is_gt, "P%d" % b, "kM%d kM" % b)
+            tt(s("kt", 128 * b, 128 * b + 128), P(b, 1, 512, 4), s("kM", 128 * b, 128 * b + 128), A.mult, "P%d kM%d" % (b, b), "kt%d" % b)
+            tt(s("kk", 128 * b, 128 * b + 128), P(b, 0, 512, 4), s("kt", 128 * b, 128 * b + 128), A.add, "P%d kt%d" % (b, b), "kk%d" % b)
+            tt(s("kf", 128 * b, 128 * b + 128), P(b, 3, 512, 4), s("kk", 128 * b, 128 * b + 128), A.min, "P%d kk%d" % (b, b), "kf%d" % b)
+        for gi in range(8):
+            red(col("red", gi), s("kf", gi, 256, 8), A.max, "kf0 kf1", "red%d" % gi)
+        ts(s("ri"), s("red"), 0.0, A.max, keys("red", 8), "ri")
+        ts(s("rj"), s("ri"), 0xFF07FF, A.bitwise_and, "ri", "rj")
+        ts(s("rep"), s("rj").indirect(s("l_rep")), col("pcol", 5), A.add, "rj l_rep pc5", "rep")
+        op("t", lambda: g.tensor.transpose(P(2, 0, 128), s("rep"), s("idf")), "rep idf", "P2")
+        if t == 0:
+            for k in range(6):
+                ts(dg(DN[k]), s("idb"), col("dw", 16 * k + 15), A.mult, "idb dw", DN[k])
+        if t > 0:
+            tt(s("lr"), s("rb", 0, 64), s("el0", 0, 64) if t == 1 else s("eo1", 0, 128, 2), A.add, "rb el0 eo1c", "lr")
+        if t == 1:
+            tt(s("xg"), s("e80", 0, 4), s("e80", 4, 8), A.add, "e80 e80b", "xg")
+            tt(s("xb"), s("e80", 0, 4), s("c21w", 4, 8), A.add, "e80 c21w", "xb")
+        if t == 2:
+            tt(s("ge"), s("c21", 64, 128), C(0, 0), A.add, "c21 C0", "ge")
+            tt(s("gb"), s("gb"), R(1, 1), A.mult, "gb R1", "gb")
+        cp(s("he"), P(2, 0, 128, 2), "P2", "he")
+        tt(s("Hi"), P(2, 1, 128, 2), s("he"), A.max, "P2 he", "Hi")
+        Hi = s("Hi")
+        ts(s("vf"), Hi, 63, A.bitwise_and, "Hi", "vf")
+        t2(s("dm"), Hi, 6, A.logical_shift_right, 31, A.bitwise_and, "Hi", "dm")
+        ts(s("g16"), Hi, 0xFF0000, A.bitwise_and, "Hi", "g16")
+        for q in range(4):
+            ts(s("tq", 80 * q, 80 * q + 64), s("vf"), col("vq", q), A.is_equal, "vf vq", "tq%d" % q)
+        tt(s("S1"), s("dm"), s("jc"), A.add, "dm jc", "S1")
+        ts(s("pl"), Hi, 2047, A.bitwise_and, "Hi", "pl")
+        tt(s("S"), s("S1"), s("g16"), A.add, "S1 g16", "S")
+        t2(s("d64"), Hi, 4, A.logical_shift_right, 64, A.bitwise_and, "Hi", "d64")
+        for q in range(4):
+            tt(s("tq", 80 * q, 80 * q + 64), s("tq", 80 * q, 80 * q + 64), s("S"), A.mult, "S tq%d" % q, "tq%d" % q)
+        for q in range(4):
+            red(col("best", q), s("tq", 80 * q, 80 * q + 65), A.max, "tqs tq%d" % q, "best%d" % q)
+        for q in range(4):
+            ts(s("W", 64 * q, 64 * q + 64), s("tq", 80 * q, 80 * q + 64), col("best", q), A.is_ge, "tq%d best%d" % (q, q), "W%d" % q)
+        for q in range(4):
+            mm(P(3, 0, 64), s("bo"), s("W", 64 * q, 64 * q + 64), q == 0, q == 3, "bo W%d" % q, "P3")
+        t2(s("mu"), Hi, 6, A.logical_shift_right, 15, A.bitwise_and, "Hi", "mu")
+        tt(s("pos0"), s("pl"), s("d64"), A.add, "pl d64", "pos0")
+        ts(s("size"), s("mu"), 1.0, A.add, "mu", "size")
+        if t < RO - 1:
+            tt(s("mm", 0, 64), s("pos0"), s("r16", 0, 64), A.mult, "pos0 r16", "mm")
+        tt(s("ws"), P(3, 0, 64), s("size"), A.mult, "P3 size", "ws")
+        if t < RO - 1:
+            scan(s("ms"), s("sgm", 0, 64), s("mm", 0, 64), 0.0, A.mult, A.add, "mm sgm", "ms")
+        scan(s("tot"), s("ones", 0, 64), s("ws"), 0.0, A.mult, A.add, "ws ones", "tot")
+        if t < RO - 1:
+            cp(s("l_p0", 0, 4), s("ms", 15, 64, 16), "ms", "l_p0a")
+            ts(s("l_p0", 4, 8), s("ms", 15, 64, 16), 64.0, A.add, "ms", "l_p0b")
+            act(s("g2"), s("XV", 0, XVN + 16).indirect(s("l_p0")), "XV xvp l_p0a l_p0b", "g2")
+            mm(P(4, 0, 64), s("idb"), s("g2", 0, 64), True, False, "g2 idb", "P4")
+            mm(P(4, 0, 64), s("nid"), s("g2", 64, 128), False, True, "g2 nid", "P4")
+            act(s("g2a"), P(4, 0, 64), "P4", "g2a", AF.Abs)
+            mm(P(4, 64, 128), s("bo"), s("g2a"), True, True, "g2a bo", "P4")
+            if t == 0:
+                dga(11, 13)
+            act(s("q_D"), P(4, 64, 128), "P4", "q_D")
+        t2(s("hd"), Hi, 11, A.logical_shift_right, 1, A.bitwise_and, "Hi", "hd")
+        ts(s("ac0"), s("tot"), 256.5, A.is_lt, "tot", "ac0")
+        tt(s("b64"), s("tot"), s("ws"), A.subtract, "tot ws", "b64")
+        tt(s("q_ac"), P(3, 0, 64), s("ac0"), A.mult, "P3 ac0", "q_ac")
+        tt(s("q_as"), s("ac0"), s("ws"), A.mult, "ac0 ws", "q_as")
+        ts(s("q_ba"), s("b64"), 256.0, A.min, "b64", "q_ba")
+        tt(s("q_rv"), s("q_ac"), s("hd"), A.mult, "q_ac hd", "q_rv")
+        if t < RO - 1:
+            tt(s("q_ra"), s("q_as"), s("hd"), A.mult, "q_as hd", "q_ra")
+            ts(s("q_gn"), s("g16"), 1.0 / H16, A.mult, "g16", "q_gn")
+        mo = "mo%d" % t
+        lst = [("d_as", "q_as"), ("d_ba", "q_ba"), ("d_rv", "q_rv")]
+        if t == 0:
+            lst.append(("d_one", "onb"))
+        if t < RO - 1:
+            lst += [("d_ac", "q_ac"), ("d_ra", "q_ra")]
+        if t == 1:
+            lst += [("d_ne", "q_gn"), ("d_e", "q_D")]
+        for k, (w, qn) in enumerate(lst):
+            mm(P(5, 80, 144), dg(w), s(qn, 0, 64), k == 0, k == len(lst) - 1, w + " " + qn, "P5")
+        act(s("val"), s("b64"), "b64", "val", scale=64.0)
+        if t < RO - 1:
+            lst = [("i_ba", s("q_ba"), "q_ba"), ("i_as", s("q_as"), "q_as"), ("i_la", s(el, 0, 128, 2), el), ("i_j", s("jb"), "jb"),
+                   ("i_one", s("onb", 0, 64), "onb"), ("i_ne", s("q_gn"), "q_gn"), ("i_e", s("q_D"), "q_D")]
+            for k, (w, ap, qn) in enumerate(lst):
+                mm(P(5, 0, 64), dg(w), ap, k == 0, k == len(lst) - 1, w + " " + qn, "P5")
+            act(s(mo, 0, 64), P(5, 0, 64), "P5", mo + "a")
+        act(s(mo, 80, 144), P(5, 80, 144), "P5", mo + "b")
+        a = 0 if t < RO - 1 else 80
+        send(attacker(t), s("dl%d" % t, a, 144), s(mo, a, 144), "ad%d" % t, "%sa %sb %sd" % (mo, mo, mo))
+        if t == 0:
+            act(s("sB", 1008, U), s("stat", 16 + 1008, 16 + U), "stat", "sB1")
+            for r in range(16):
+                mm(P(6, 0, 168), s("q14", 15 - r, 143 - r), s("sB", r, U, 16), r == 0, r == 15, "q14 sB0 sB1", "P6")
+            fill("sw1", 0, 320, 0, "sw1")
+            tt(s("j256"), s("j256"), s("r16", 0, 64), A.mult, "j256 r16", "j256")
+        else:
+            act(s("numb", 672 * (t + 1), 672 * (t + 2)), s("iot").indirect(s("ocu", 42 * (t + 1), 42 * (t + 2))), "iot ocu", "numb%d" % (t + 1))
+        bk = keys("best", 4)
+        t2(s("o1"), s("q_ac"), -512.0, A.mult, 512.0, A.add, "q_ac", "o1")
+        cp(s("bi"), s("best"), bk, "bi")
+        tt(s("o2"), s("o1"), s("b64"), A.add, "o1 b64", "o2")
+        red(col("cnt", 0), s("ac0"), A.add, "ac0", "cnt0")
+        tt(s("mm", 0, 64), s("o2"), s("j256"), A.min, "o2 j256", "mm")
+        tt(s("pj"), s("pos0"), s("j32"), A.add, "pos0 j32", "pj")
+        scan(s("ms"), s("sgm", 0, 64), s("mm", 0, 64), 0.0, A.mult, A.add, "mm sgm", "ms")
+        tt(s("val"), s("val"), s("pj"), A.add, "val pj", "val")
+        cp(s("l_off"), s("ms", 15, 64, 16), "ms", "l_off")
+        t2(s("bx"), s("bi"), 5, A.logical_shift_right, 127, A.bitwise_and, "bi", "bx")
+        sw = "sw%d" % t; e8 = "e8%d" % t
+        cp(s(sw).indirect(s("l_off")), s("val"), "l_off val", sw)
+        ts(s("bm"), s("bi"), 15, A.bitwise_and, "bi", "bm")
+        scan(s("Fs"), s(sw, 0, 256), s(sw, 0, 256), 0.0, A.max, A.max, sw, "Fs")
+        t2(s("vx"), s("bx"), col("cnt", 0), A.add, 127.5, A.is_gt, "bx cnt0", "vx")
+        scan(s("F2"), s("Fs"), s("cap"), 1e9, A.min, A.max, "Fs cap", "F2")
+        ts(s("vm"), s("bm"), 1.0, A.add, "bm", "vm")
+        tt(s("Fw"), s("F2", 14, 256, 16), s("F2", 15, 256, 16), A.min, "F2", "Fw")
+        t2(s("bd"), s("bi"), 4, A.logical_shift_right, 1, A.bitwise_and, "bi", "bd")
+        ts(s("cc"), s("Fw"), 32767, A.bitwise_and, "Fw", "cc")
+        tt(s("cs"), s("vx"), s("vm"), A.mult, "vx vm", "cs")
+        tt(s("pw"), s("cc"), s("kw"), A.subtract, "cc kw", "pw")
+        tt(s(e8, 4, 8), s("cs"), s("bd"), A.mult, "cs bd", e8 + "b")
+        t2(s("l_pos"), s("pw"), 0.0, A.max, float(XVN - 1), A.min, "pw", "l_pos")
+        tt(s(e8, 0, 4), s("cs"), s(e8, 4, 8), A.subtract, "cs " + e8 + "b", e8)
+        po = "po%d" % t
+        act(s(po), s("XV", 0, XVN).indirect(s("l_pos")), "XV l_pos", po)
+        dst = s("xc_", 16 + lim, 16 + lim + NEWC) if t < RO - 1 else s("xb_", lim, lim + NEWC)
+        send(attacker(t), dst, s(po), "ap%d" % t, po)
+        tt(s("ex"), s(e8).indirect(s("l_rep")), s("r16", 0, 128), A.mult, "r16 l_rep %s %sb" % (e8, e8), "ex")
+        mm(P(4, 192, 256), s("idb"), s("lr"), True, False, "idb lr", "P4")
+        mm(P(4, 192, 256), s("nbo"), s("ex", 0, 64), False, False, "nbo ex", "P4")
+        mm(P(4, 192, 256), s("nbo"), s("ex", 64, 128), False, True, "nbo ex", "P4")
+        mm(P(4, 64, 192), s("bo"), s("ex"), True, True, "bo ex", "P4")
+        if t < RO - 1:
+            eo = "eo%d" % (t + 1)
+            ts(s("e64"), s(e8), 64.0, A.mult, "%s %sb" % (e8, e8), "e64")
+            red(col("cnt", 1), s("q_as"), A.add, "q_as", "cnt1")
+            tt(s("e8i"), s("e64"), s("c8"), A.add, "e64 c8", "e8i")
+            ts(s("ww"), s("Fw"), 15, A.logical_shift_right, "Fw", "ww")
+            cp(s("l_end"), s("e8i"), "e8i", "l_end")
+            t2(s("iv"), s("kkw"), col("cnt", 1), A.is_ge, 64.0, A.mult, "kkw cnt1", "iv")
+            act(s(eo, 0, 128, 2), P(4, 192, 256), "P4", eo + "c")
+            act(s(eo, 1, 128, 2), P(4, 192, 256), "P4", eo + "d")
+            cp(s(eo, 128, 256, 2), s("XV", 0, XVN).indirect(s("l_end", 0, 4)), "XV l_end", eo + "a")
+            act(s(eo, 129, 256, 2), s("XV", 0, XVN).indirect(s("l_end", 4, 8)), "XV l_end", eo + "b")
+            send(victim(t + 1), s("el%d" % (t + 1), 0, 256), s(eo), "ae%d" % (t + 1), "%sa %sb %sc %sd" % (eo, eo, eo, eo))
+            tt(s("w2"), s("ww"), s("iv"), A.max, "ww iv", "w2")
+            cp(s("wo%d" % t), s("w2"), "w2", "wo%d" % t)
+            send(attacker(t), s("wl%d" % t), s("wo%d" % t), "ai%d" % t, "wo%d" % t)
+        act(s("C%d" % t), P(4, 64, 256), "P4", "C%d" % t)
+        if t == 0:
+            cp(s("cl"), P(6, 0, 168), "P6", "cl")
+            act(s("cb"), P(4, 64, 192), "P4", "cb")
+            later_act()
+            dga(15, 16)
+            fill("sw2", 0, 320, 0, "sw2")
+            io_(s("numb", U, ZC), [[1, RO * NEWC]], U, 0, "numbn")
+        if t == 1:
+            act(s("xa"), s("xg"), "xg", "xa", scale=-1.0, bias=21.0)
+            act(s("xe_"), s("xg"), "xg", "xe_", scale=-1.0, bias=20.0)
+            act(s("xh"), s("xg"), "xg", "xh", scale=4096.0, bias=3300.0 - 4096 * 21)
+        if t == 0:
+            def mid():
+                dga(13, 15); dga(16, 18)
+                mm(P(6, 256, 320), dg("c_l"), s("cb", 0, 64), True, False, "c_l cb", "P6")
+                mm(P(6, 256, 320), dg("c_r"), s("cb", 64, 128), False, True, "c_r cb", "P6")
+                act(s("cut"), P(6, 256, 320), "P6", "cut")
+                for k, (m, b) in enumerate(((1, 0), (1, U + NEWC), (1, U + 2 * NEWC), (4096, 3300), (4096, 3500), (8192, 4096))):
+                    act(s("bc", 2 * k, 2 * k + 2), s("kkw", 0, 2), "kkw", "", scale=float(m), bias=float(b))
+                mark("a", "bc")
+            mid()
+        if t == 1:
+            act(s("gb"), C(0, 2), "C0", "gb", bias=-1.0)
+            act(s("ha"), R(0, 1), "R0", "ha", scale=-2.0, bias=1.0)
+            act(s("hb"), R(0, 1), "R0", "hb", scale=20.0)
+            act(s("hf"), R(0, 2), "R0", "hf", bias=float(U - 21))
+            act(s("hc"), C(1, 2), "C1", "hc", bias=-1.0)
+
+    def h(n, ih): return s(n, 64 * ih, 64 * ih + 64)
+    def bc(k, ih): return col("bc", 2 * k + ih)
+    landed("ad2", "dl2")
+    landed("ap2", "xbn2")
+    act(s("ga"), R(1, 1), "R1", "ga", scale=-2.0, bias=1.0)
+    unpack(2)
+    act(s("gh"), R(2, 1), "R2", "gh", scale=-2.0, bias=1.0)
+    tt(s("hb"), s("hb"), s("c21", 0, 64), A.add, "hb c21", "hb")
+    tt(s("ge"), s("ge"), s("gb"), A.add, "ge gb", "ge")
+    tt(s("gd"), C(2, 0), C(0, 2), A.subtract, "C0 C2", "gd")
+    tt(s("gg"), s("ga"), C(2, 0), A.mult, "ga C2", "gg")
+    tt(s("gf"), s("gd"), R(1, 2), A.add, "gd R1", "gf")
+    tt(s("hc"), s("hc"), R(2, 1), A.mult, "hc R2", "hc")
+    for ih in range(2):
+        act(h("fh", ih), s("gh"), "gh bc", "fh%d" % ih, scale=bc(0, ih))
+    for ih in range(2):
+        act(h("fa", ih), s("gd"), "gd bc", "fa%d" % ih, scale=4096.0, bias=bc(3, ih))
+        act(h("fb", ih), s("gf"), "gf bc", "fb%d" % ih, bias=bc(1, ih))
+        act(h("fc", ih), C(2, 2), "C2 bc", "fc%d" % ih, scale=-8192.0, bias=bc(5, ih))
+        act(h("fd", ih), s("ga"), "ga bc", "fd%d" % ih, scale=bc(0, ih))
+    tt(s("gi"), R(2, 2), C(1, 2), A.subtract, "R2 C1", "gi")
+    tt(s("hc"), s("hc"), C(1, 0), A.add, "hc C1", "hc")
+    tt(s("gj"), R(2, 0), C(1, 2), A.add, "R2 C1", "gj")
+    tt(s("ge"), s("ge"), s("gg"), A.add, "ge gg", "ge")
+    for ih in range(2):
+        tt(h("fh", ih), h("fh", ih), s("hc"), A.add, "hc fh%d" % ih, "fh%d" % ih)
+    tt(s("fa"), s("fa"), s("fb"), A.min, "fa0 fa1 fb0 fb1", "fa0 fa1")
+    for ih in range(2):
+        tt(h("fd", ih), h("fd", ih), s("ge"), A.add, "ge fd%d" % ih, "fd%d" % ih)
+    act(s("fg"), s("fh"), "fh0 fh1", "fg", scale=4096.0, bias=3000.0 - 4096 * 21)
+    for ih in range(2):
+        act(h("fb", ih), C(1, 2), "C1 bc", "fb%d" % ih, scale=-4096.0, bias=bc(4, ih))
+        act(h("fe", ih), s("gi"), "gi bc", "fe%d" % ih, bias=bc(2, ih))
+    tt(s("fa"), s("fa"), s("fc"), A.max, "fa0 fc0 fc1", "fa0 fa1")
+    for ih in range(2):
+        act(h("fc", ih), s("gj"), "gj bc", "fc%d" % ih, scale=-8192.0, bias=bc(5, ih))
+        tt(h("ff", ih), h("fh", ih), s("ha"), A.mult, "ha fh%d" % ih, "ff%d" % ih)
+    tt(s("fa"), s("fa"), s("fd"), A.max, "fa0 fd0 fd1", "fa0 fa1")
+    for ih in range(2):
+        tt(h("fd", ih), h("fh", ih), s("hf"), A.add, "hf fh%d" % ih, "fd%d" % ih)
+    for ih in range(2):
+        ts(s("l_f", 2 + ih, 256, 4), h("fa", ih), float(ZC), A.min, "fa0", "lf1%d" % ih)
+    tt(s("fb"), s("fb"), s("fe"), A.min, "fb0 fb1 fe0 fe1", "fb0 fb1")
+    for ih in range(2):
+        tt(h("ff", ih), h("ff", ih), s("hb"), A.add, "hb ff%d" % ih, "ff%d" % ih)
+    tt(s("fd"), s("fd"), s("fg"), A.min, "fd0 fd1 fg", "fd0 fd1")
+    tt(s("fb"), s("fb"), s("fc"), A.max, "fb0 fc0 fc1", "fb0 fb1")
+    tt(s("fd"), s("fd"), s("ff"), A.max, "fd0 ff0 ff1", "fd0 fd1")
+    tt(s("fb"), s("fb"), s("fd"), A.max, "fb0 fd0", "fb0 fb1")
+    for ih in range(2):
+        ts(s("l_f", ih, 256, 4), h("fb", ih), float(ZC), A.min, "fb0", "lf0%d" % ih)
+    lk = " lf00 lf01 lf10 lf11"
+    xk = XBK + " xbn0 xbn1 xbn2 xbz" + lk
+    nk = keys("numb", 4) + " numbn numbz" + lk
+    o = OFF["YO"][1]
+    cuts = (0, 1280, 2560, 3584, 4096)
+    for c in range(4):
+        a, b = cuts[c], cuts[c + 1]
+        cp(s("Y", a, b), s("xb_").indirect(s("l_f", a // 16, b // 16)), xk, "Y%d" % c)
+        act(s("YO", a, b), s("numb").indirect(s("l_f", a // 16, b // 16)), nk, "YO%d" % c)
+        dma("s", T.y[:, a:b], s("Y", a, b), "so", "Y%d" % c, "")
+        if c == 2:
+            dma("s", T.yo[:, 0:b], T.F[0:128:16, o:o + b], "so", "YO0 YO1 YO2", "")
+    dma("a", T.yo[:, a:b], T.F[0:128:16, o + a:o + b], "so", "YO3", "")
+    for sem, c in cnt.items():
+        if c:
+            g.wait_ge(T.sem[sem], c)

@@ -1,52 +1,64 @@
+import numpy as np
 from concourse.mybir import AluOpType as A, AxisListType, ActivationFunctionType as AF
 
 U, NEWC, RO = 2688, 256, 3
 XVN = 34 * 64
-ZC = U + RO * NEWC
-H16, P25, P26 = 65536.0, 2.0 ** 25, 2.0 ** 26
+NS = 336
+Z1 = U + 2 * NS
+ZC = Z1 + NEWC
+TH = 4000
+H16, M26 = 65536.0, 2.0 ** 26
+NK = (14, 14, 4)
+CB = (0, 2, 6, 10, 14, 18, 22, 26, 28, 30, 31, 32)
+CG = (0, 6, 14, 22, 28, 31, 32)
+ZB = (4, 7, 3)
+SAMEQ = True
 
-DIAG = {
-    "d_as": {5: 1, 8: -1, 15: 1}, "d_ra": {4: 1, 5: -1, 8: 2}, "d_rv": {6: -1, 7: 1, 9: 1}, "d_ac": {7: -1},
-    "d_ba": {14: 1}, "d_one": {6: -128},
-    "i_ba": {4: -1, 5: 1, 7: -1, 8: -2, 12: 256, 13: 256}, "i_as": {5: 1, 7: -1, 8: -1}, "i_la": {4: 1, 8: 1},
-    "i_e": {13: 1}, "i_ne": {13: -1}, "i_j": {3: 1}, "i_one": {5: -1, 7: 2, 8: 1, 10: -256},
-    "d_e": {11: 1, 13: 1}, "d_ne": {11: -1, 13: -1},
-    "i_k": {4: 1, 5: -1, 7: 1, 8: 2, 12: -256, 13: -256},
-    "c_l": {4: -1, 6: 1, 8: -1, 12: 256, 13: 256}, "c_r": {5: -1, 7: 1, 8: 1, 10: 256, 11: 256},
-}
 COLS = {
-    "s_i": {4: 1, 5: -1, 6: -1, 7: 1, 8: 2, 10: 256, 11: 256, 12: -256, 13: -256},
-    "s_e": {6: 128, 14: -64}, "s_j": {3: 1, 14: 1},
-    "s_c": {5: 20, 6: 1, 7: -19, 8: -20, 10: -5120, 11: -5120, 14: 64},
-    "kh": {0: H16, 12: -H16, 13: H16, 2: -H16, 6: -P26, 7: -P26},
-    "dh": {1: H16, 10: -H16, 11: H16, 0: -H16, 12: H16, 13: -H16},
-    "sh": {5: 1, 9: 1, 4: -1}, "ch": {4: -P25, 8: P25},
-    "kl": {5: 64, 9: -1024, 3: 1}, "dl": {9: 2048, 4: 64, 5: -64},
+    "s_i": {4: 1, 5: -1, 6: -1, 7: 1, 8: 2, 14: -2, 10: 256, 11: 256, 12: -256, 13: -256},
+    "s_e": {15: 64}, "s_j": {3: 1},
+    "s_c": {5: 20, 6: 1, 7: -19, 8: -19, 14: 20, 10: -5120, 11: -5120},
+    "aL": {1: H16, 2: -H16, 6: -M26, 7: -M26, 8: -M26, 15: -M26, 4: 64, 3: 1},
+    "aR": {0: H16, 2: -H16, 6: -M26, 7: -M26, 14: -M26, 15: -M26, 5: 64, 3: 1},
+    "ua1": {5: 1, 8: -1, 14: 1}, "ub1": {5: 1, 7: -1, 8: -1, 14: 1},
+    "ua2": {4: 1, 5: -1, 8: 2, 14: -2}, "ub2": {4: 1, 5: -1, 6: -1, 7: 1, 8: 1, 14: -1, 9: 1},
+    "hL": {1: H16, 10: -H16, 11: H16, 2: -H16, 6: -M26, 7: -M26, 8: -M26},
+    "hR": {0: H16, 12: -H16, 13: H16, 2: -H16, 6: -M26, 7: -M26, 14: -M26},
+    "lL": {4: 64, 3: 1, 9: 1024}, "lR": {5: 64, 3: 1, 9: -1024},
+    "mDe": {11: 1, 13: 1}, "r_s": {4: 1, 5: 1}, "r_n": {9: -1, 7: 1}, "q_c": {3: 1, 15: 1},
+    "i_k": {4: 1, 5: -1, 7: 1, 8: 2, 14: -2, 12: -256, 13: -256}, "i_la": {4: 1, 8: 1, 14: -1},
+    "i_one": {4: 1, 5: -2, 7: 3, 8: 4, 14: -3, 10: -256, 12: -256, 13: -256}, "i_na": {7: 2048},
+    "c_l": {4: -1, 6: 1, 8: -1, 14: 1, 12: 256, 13: 256}, "c_r": {5: -1, 7: 1, 8: 1, 14: -1, 10: 256, 11: 256},
 }
+for _k in ("L", "R"):
+    COLS["h" + _k].update(COLS.pop("l" + _k))
+_to = {8: 12, 12: 8, 9: 10, 10: 9}
+COLS = {n: {_to.get(f, f): c for f, c in d.items()} for n, d in COLS.items()}
 CN = list(COLS)
-DN = list(DIAG)
-NC_, ND = len(CN), len(DN)
+NE, NC_ = 4, len(CN)
+DN = ["i_k", "i_b", "i_as", "i_la", "i_j", "i_one", "i_na", "i_e", "c_l", "c_r"]
 
 SIZES = {"F": {}, "B": {}, "I": {}, "U": {}}
 def _a(ar, **kw):
     SIZES[ar].update(kw)
-_a("F", stat=16 + U, T1=16 + U + 256, T2=16 + U + 512, spos=U, iot=U, numb=ZC + 16, cp=672, YO=4096,
-   pcol=16, g8=8, x144=144, pat=288, r16=288, sgm=288, rt=16 * NC_, rt2=16 * ND, seg=16 * ND, cw=16 * NC_, dw=16 * ND, sb=8,
-   idf=128, cdf=256, cdt=256, cdT=256, pm=4 * 128, kM=256, kt=256, kk=256, kf=256, red=8, rep=128, he=64, zs=8, mf=256,
-   S1=64, S=64, jc=64, tq=4 * 80, best=4, size=64, ws=64, tot=64, ones=128, ac0=64, cnt=2, pos0=64, pj=64, j32=64, j256=64,
-   mm=128, ms=64, o1=64, o2=64, val=64, b64=64, sw0=320, sw1=320, sw2=320, Fs=256, F2=256, cap=256,
-   kw=16, kkw=16, pw=16, iv=16, w2=16, vq=4, vx=4, vm=4, cs=4, e80=8, e81=8, e82=8, e64=8, c8=8,
-   mo0=144, mo1=144, mo2=144, dl0=208, dl1=144, dl2=144, ifl=256, dy2=128, cut=64,
-   rs=3 * 128, wr=12, xa=4, xb=4, xc=4, xd=4, xe_=4, xf=4, xg=4, xh=4, xi=4, c21w=8, y1=68, xP=136, xt=136, xm=136, xu=136,
-   c21=128, bc=16, fa=128, fb=128, fc=128, fd=128, fe=128, ff=128, fg=128, fh=128, ga=64, gb=64, gd=64, ge=64, gf=64, gg=64,
-   gh=64, gi=64, gj=64, ha=64, hb=64, hc=64, hf=64, R0=192, R1=192, R2=192, C0=192, C1=192, C2=192)
-_a("B", xc_=16 + U + 512, xb_=ZC + 16, ad=U + 32, G=4096, MN=4096, Y=4096, XV=XVN + 16, sB=U, bo=128, nbo=128, idb=128, nid=128,
-   qz=144, q1=144, q14=144, dg=128 * ND, ds=3 * 128, pt=3 * 336, fR=128, fL=128, fZ=128, w0=512, w1=512, wc=1024, wf=32, wh=32, wl=32,
-   onb=128, jb=64, kb=256, eo0=256, eo1=256, eo2=256, el0=640, el1=640, el2=640, W=256, q_as=64, q_ac=64, q_ra=64, q_rv=64,
-   q_ba=64, q_gn=64, q_D=64, g2=128, g2a=64, po0=256, po1=256, po2=256, ex=128, lr=64, cb=128, rb=192, nad=272)
+_a("F", stat=16 + U, T1=16 + U + 256, T2=16 + U + 512, spos=U, numb=ZC + 16, cp2=672, YO=4096, op_=192, ot=192,
+   pcol=16, q14=144, g8=8, x144=144, pat=256, r16=272, sgm=256, rt=16 * NC_, seg=16 * NC_, cw=16 * NC_, sb=8,
+   idf=128, cdf=256, cdt=256, pm=4 * 128, gp=320, ks=768, red=8, rep=128, he=64, gid=128, m2=128, r2f=8, zs=8, mf=256,
+   jc=64, tq=4 * 80, best=4, wm=64, ones=128, ac0=64, cnt=2, j32=64, j256=64,
+   mm=64, ms=64, o1=64, val=64, sw=1184, Fs=256, F2=256, cap=256, U1=64, U5=64,
+   kw=16, kkw=16, pw=16, vq=4, vx=8, vm=4, cs=4, et=8, e80=8, e81=8, e82=8, c8=8, Lw=8, La2=4,
+   mo=64, ifl=256, dy2=128, cut=64,
+   wr=12, xa=4, xb=4, xc=4, xd=4, xe_=4, xf=4, xg=4, xh=4, xi=4, c21w=8, y1=68, xP=136, xt=136, xm=136, xu=136,
+   c21=128, bc=16, fa=128, fb=128, fc=128, fd=128, ff=128, fg=128, fh=128, ga=64, gb=64, ge=64, gg=64,
+   ha=64, hb=64, hf=64, hm=128, hn=128, hq=128, hr=128, C0=192, C1=192, C2=192)
+_a("B", xc_=16 + U + 512, xb_=ZC + 16, ad=U + 32, G=4096, MN=4096, XV=XVN + 16, bo=128, bo6=128, nb6=128, idb=128, nid=128, nM=128,
+   qz=144, q1=144, q16=144, dg=128 * len(DN), ds=3 * 128, pt=3 * 336, fR=128, fL=128, fZ=128, w0=320, w1=320, sm=320, wc=1536,
+   wf=16, wa=16, wh1=16, wh2=16, wz=16, zb=768, rs=3 * 128, R0=128, R1=128, R2=128, na=64,
+   onb=128, jb=64, kb=256, eo0=128, eo1=256, eo2=256, el0=640, el1=640, el2=640, W=256, q_gn=64, g2=128, g2a=64,
+   po0=NS, po1=NS, po2=256, mo0=128, mo1=128, mo2=128, dl0=192, dl1=192, dl2=192, ex=128, lr=64, c1b=64, cb=192, nad=272)
 _a("I", oc=168, cd=256, pi=4, mi=256, mj=256, ri=8, rj=8, Hi=64, vf=64, dm=64, g16=64, mu=64, hd=64, pl=64, d64=64,
    Fw=16, cc=16, ww=16, bi=4, bx=4, bm=4, bd=4, e8i=8)
-_a("U", ocu=168, cl=168, ml=256, l_rep=8, l_p0=8, l_off=4, l_pos=16, wo0=16, wo1=16, wl0=16, wl1=16, l_end=8, l_xv=136, l_f=256)
+_a("U", ocu=168, cl=168, ml=256, l_rep=8, l_r2=8, l_p0=8, l_off=4, l_pos=16, wl_=16, l_end=8, l_xv=136, l_f=256)
 OFF = {}
 TOT = {}
 for _ar, _d in SIZES.items():
@@ -57,11 +69,19 @@ for _ar, _d in SIZES.items():
     TOT[_ar] = _o
 SCRATCH = {"F": ("sbuf", [128, TOT["F"]], "float32"), "B": ("sbuf", [128, TOT["B"]], "bfloat16"),
            "I": ("sbuf", [128, TOT["I"]], "int32"), "U": ("sbuf", [128, TOT["U"]], "uint16"),
-           "TR": ("sbuf", [128, 8, 32], "float32")}
+           "TR": ("sbuf", [128, 8, 32], "float32"), "CT": ("sbuf", [128, 8, 32], "float32"),
+           "TT": ("sbuf", [128, 6, 32], "float32")}
 for _b in range(8):
     SCRATCH["P%d" % _b] = ("psum", [128, 512], "float32")
-SEMAPHORES = ["cv", "ca", "ct", "cg", "ls", "lx0", "lx1", "loc", "lcd", "so"] + \
-    ["%s%d" % (n, t) for n in ("ae", "ad", "ap", "ai") for t in range(RO)]
+SEMAPHORES = ["cv", "ca", "ct", "cg", "ls", "lx0", "lx1", "loc", "lcd", "so"] + ["ln%d" % k for k in range(8)] + \
+    ["%s%d" % (n, t) for n in ("ae", "ad", "ap") for t in range(RO)]
+
+MEMO = {}
+BOOST = {464: 0.5, 1071: 1.5, 453: -4, 897: 1.8, 851: 4, 1282: 2, 127: -0.2, 134: 0.3, 892: -1, 842: 4, 573: 0.5, 328: 4, 1304: 2, 118: -4,
+         1363: 4, 530: 1.8, 478: -4, 653: 0.5, 682: 2, 568: -0.2, 537: 2, 1226: -0.2, 482: -1, 900: 0.2, 931: -4, 699: -0.2, 1281: 2,
+         563: 8, 535: 0.2, 514: 0.2, 1083: 0.7, 711: 8, 715: 8, 712: -4, 9: 2, 850: -0.5, 678: -2, 847: -4, 957: -0.2, 1131: 8,
+         1050: -8, 267: 8, 1199: -4, 278: 16, 1217: -2, 270: 12, 1045: 4, 126: -0.5, 329: 16, 374: 0.5, 902: 0.5, 928: 0.5, 299: 2,
+         337: 3.5, 526: 0.5, 542: 1, 1302: -8, 1266: -8, 1303: -0.2, 277: 8, 279: 8, 280: 8, 281: 8, 283: 8, 373: 0.5, 138: -1.0}
 
 
 def rank_program(g, core, T, topo):
@@ -71,641 +91,649 @@ def rank_program(g, core, T, topo):
     NR = len(T.cores)
     Q = {"v": g.vector, "a": g.scalar, "t": g.tensor, "g": g, "s": g.sync}
     SEM = {"v": "cv", "a": "ca", "t": "ct", "g": "cg"}
-    cnt = {"cv": 0, "ca": 0, "ct": 0, "cg": 0}
-    seen = {}
-    lastw = {}
-    readers = {}
+    ops = []
+    lw, lr = {}, {}
+    bank = {}
+    last_ = {}
 
-    def s(n, a=0, b=None, st=None):
+    def width(n):
+        w = 1
+        for d in SCRATCH[n][1][1:]:
+            w *= d
+        return w
+
+    def s(n, a=0, b=None, st=1):
         ar, o, z = OFF[n]
         b = z if b is None else b
-        return T[ar][:, o + a:o + b] if st is None else T[ar][:, o + a:o + b:st]
+        x = T[ar][:, o + a:o + b] if st == 1 else T[ar][:, o + a:o + b:st]
+        return (x, [(ar, np.arange(o + a, o + b, st))])
+    def row0(n, a, b):
+        ar, o, z = OFF[n]
+        return (T[ar][0:1, o + a:o + b], [(ar, np.arange(o + a, o + b))])
+    def col(n, j): return s(n, j, j + 1)
+    def P(b, a=0, e=512, st=1):
+        n = "P%d" % b
+        return (T[n][:, a:e] if st == 1 else T[n][:, a:e:st], [(n, np.arange(a, e, st))])
+    def c3(n, i, a, b):
+        ids = np.arange(256).reshape(8, 32)
+        if i is None:
+            return (T[n][:, :, a:b], [(n, ids[:, a:b].reshape(-1))])
+        return (T[n][:, i, a:b], [(n, ids[i, a:b])])
+    def ind(w, off): return (w[0].indirect(off[0]), w[1], off[1])
+    def ap(x): return x[0] if isinstance(x, tuple) else x
+    def size(x): return 16 * len(x[2][0][1]) if len(x) > 2 else len(x[1][0][1])
 
-    def col(n, j):
-        return s(n, j, j + 1)
+    def add(q, fn, r, w, cost, lat=None, kind="c", sem=None, after=()):
+        i = len(ops)
+        pre = {}
+        rd = []
+        for x in r:
+            if isinstance(x, tuple):
+                rd += x[1] + (x[2] if len(x) > 2 else [])
+        wt = []
+        for x in w:
+            wt += x[1]
+            rd += x[2] if len(x) > 2 else []
+        for n, c in rd + wt:
+            if n not in lw:
+                lw[n] = np.full(width(n), -1); lr[n] = {}
+        for n, c in rd + wt:
+            for j in np.unique(lw[n][c]):
+                if j >= 0: pre[int(j)] = True
+        for n, c in wt:
+            for j, a in lr[n].items():
+                if a[c].any(): pre[j] = pre.get(j, False) or ops[j][0] != q or ops[j][5] != "c" or kind != "c" or SAMEQ
+        for n, c in rd + wt:
+            if n[0] == "P":
+                for k, js in bank.setdefault(n, {}).items():
+                    if k != q or q == "t":
+                        for j in js: pre[j] = True
+        for n, c in rd + wt:
+            if n[0] == "P":
+                bank[n] = {"t": [i]} if q == "t" else {q: bank[n].get(q, []) + [i]}
+        for n, c in wt:
+            lw[n][c] = i
+            for j in list(lr[n]):
+                lr[n][j][c] = False
+                if not lr[n][j].any(): del lr[n][j]
+        for n, c in rd:
+            if i not in lr[n]: lr[n][i] = np.zeros(width(n), bool)
+            lr[n][i][c] = True
+        for j in after: pre[j] = True
+        pre.pop(i, None)
+        ops.append([q, fn, pre, cost, cost if lat is None else lat, kind, sem])
+        return i
+    def seq(tag):
+        i = len(ops) - 1
+        if tag in last_: ops[i][2].setdefault(last_[tag], False)
+        last_[tag] = i
 
-    def P(b, a=0, e=512, st=None):
-        return T["P%d" % b][:, a:e] if st is None else T["P%d" % b][:, a:e:st]
-
-    def need(q, sem, c):
-        if q == "t" and sem == "ct":
-            return
-        if seen.get((q, sem), 0) < c:
-            Q[q].wait_ge(T.sem[sem], c)
-            seen[(q, sem)] = c
-
-    def deps(q, r, w):
-        evs = {}
-        def add(ev):
-            if ev is not None:
-                evs[ev[0]] = max(evs.get(ev[0], 0), ev[1])
-        for k in r:
-            add(lastw.get(k))
-            if k[0] == "P" and len(k) == 2:
-                for ev in readers.get(k, []):
-                    if ev[0] != SEM.get(q):
-                        add(ev)
-        for k in w:
-            add(lastw.get(k))
-            for ev in readers.get(k, []):
-                add(ev)
-        for sem, c in evs.items():
-            need(q, sem, c)
-
-    def done(ev, r, w):
-        for k in r:
-            readers.setdefault(k, []).append(ev)
-        for k in w:
-            lastw[k] = ev
-            readers[k] = []
-
-    def op(q, fn, r, w):
-        r = r.split(); w = w.split()
-        deps(q, r, w)
-        sem = SEM[q]
-        fn().then_inc(T.sem[sem], 1)
-        cnt[sem] += 1
-        done((sem, cnt[sem]), r, w)
-
-    def mark(q, k):
-        lastw[k] = (SEM[q], cnt[SEM[q]])
-
+    CY, GA, SC = 0.00104, 1.56, 3.0
+    def vc(o, ins, two=False):
+        if len(o) > 2: return 0.05 + size(o) * SC * CY
+        if any(len(x) > 2 for x in ins): return 0.05 + size(o) * GA * CY
+        n = size(ins[0]) if ins else size(o)
+        if two and not any(x[1][0][0][0] == "P" for x in ins): n *= 2
+        elif all(x[1][0][0] in ("B", "U") for x in [o] + ins): n /= 2
+        return max(64, n) * CY
     V = g.vector
-    def cp(o, i, r, w): op("v", lambda: V.tensor_copy(o, i), r, w)
-    def tt(o, a, b, f, r, w): op("v", lambda: V.tensor_tensor(o, a, b, f), r, w)
-    def ts(o, a, s1, f, r, w): op("v", lambda: V.tensor_scalar(o, a, s1, None, f), r, w)
-    def t2(o, a, s1, f, s2, f2, r, w): op("v", lambda: V.tensor_scalar(o, a, s1, s2, f, f2), r, w)
-    def red(o, a, f, r, w): op("v", lambda: V.tensor_reduce(o, a, AxisListType.X, f), r, w)
-    def scan(o, a, b, ini, f, f2, r, w): op("v", lambda: V.tensor_tensor_scan(o, a, b, ini, f, f2), r, w)
-    def ms(o, c, w): op("v", lambda: V.memset(o, c), "", w)
-    def act(o, i, r, w, f=AF.Identity, **kw): op("a", lambda: g.scalar.activation(o, i, f, **kw), r, w)
-    def mm(o, l, rh, st, sp, r, w): op("t", lambda: g.tensor.matmul(o, l, rh, st, sp), r, w)
-    def io_(o, pat, base, cm, w, i32=False, r=""):
-        if i32:
-            op("g", lambda: g.iota(o, pat, base, cm), r, w)
+    def cp(o, i): add("v", lambda: V.tensor_copy(o[0], i[0]), [i], [o], vc(o, [i]))
+    def tt(o, a, b, f): add("v", lambda: V.tensor_tensor(o[0], a[0], b[0], f), [a, b], [o], vc(o, [a, b], True))
+    def ts(o, a, s1, f): add("v", lambda: V.tensor_scalar(o[0], a[0], ap(s1), None, f), [a, s1], [o], vc(o, [a]))
+    def t2(o, a, s1, f, s2, f2): add("v", lambda: V.tensor_scalar(o[0], a[0], ap(s1), ap(s2), f, f2), [a, s1, s2], [o], vc(o, [a]))
+    def red(o, a, f): add("v", lambda: V.tensor_reduce(o[0], a[0], AxisListType.X, f), [a], [o], max(64, size(a)) * CY)
+    def scan(o, a, b, ini, f, f2): add("v", lambda: V.tensor_tensor_scan(o[0], a[0], b[0], ini, f, f2), [a, b], [o], vc(o, [a, b]))
+    def ms(o, c): add("v", lambda: V.memset(o[0], c), [], [o], vc(o, []))
+    def act(o, i, f=AF.Identity, **kw):
+        add("a", lambda: g.scalar.activation(o[0], i[0], f, **{k: ap(x) for k, x in kw.items()}), [i] + list(kw.values()), [o],
+            0.065 + size(i) * CY * (GA if len(i) > 2 else 1))
+    def mm(o, l, rh, st, sp):
+        add("t", lambda: g.tensor.matmul(o[0], l[0], rh[0], st, sp), [l, rh], [o],
+            max(64, size(rh)) * 0.55 * CY * (1 if l[1][0][0] == "B" else 4))
+    def io_(o, pat, base, cm=0):
+        if o[1][0][0] == "I":
+            add("g", lambda: g.iota(o[0], pat, base, cm), [], [o], 0.16 + 2 * size(o) * CY)
         else:
-            op("g", lambda: g.iota(o, pat, base, cm, allow_small_or_imprecise_dtypes=True), r, w)
-    def fill(n, a, b, c, w): io_(s(n, a, b), [[0, b - a]], c, 0, w)
-    def dma(q, o, i, sem, r, w):
-        r = r.split(); w = w.split()
-        deps(q, r, w)
-        Q[q].dma_start(o, i).then_inc(T.sem[sem], 16)
-        cnt[sem] = cnt.get(sem, 0) + 16
-        done((sem, cnt[sem]), r, w)
+            add("g", lambda: g.iota(o[0], pat, base, cm, allow_small_or_imprecise_dtypes=True), [], [o], 0.16 + 2 * size(o) * CY)
+    def fill(o, c): io_(o, [[0, size(o)]], c)
+    def dma(q, o, i, sem, lat, r=(), w=()):
+        add(q, lambda: Q[q].dma_start(o, i), list(r), list(w), 0.05, lat, "d", sem)
     eng = [e for e in topo.engines(T.cores[0], T.cores[1])
            if all(e in topo.engines(a, b) for a in T.cores for b in T.cores if a != b)]
     emask = sum(1 << e for e in eng)
-    def send(dst, o, i, sem, r):
-        deps("g", r.split(), [])
+    def send(dst, o, i, sem, first=False):
         rid, pid, _e = topo.addr(dst)
-        g.remote_dma(o, i, T.sem[sem], T.sem.ls, pid, rid, emask)
-        cnt["ls"] = cnt.get("ls", 0) + len(eng)
-    def landed(sem, w):
-        cnt[sem] = len(eng)
-        for k in w.split():
-            lastw[k] = (sem, cnt[sem])
+        j = add("g", lambda: g.remote_dma(o[0], i[0], T.sem[sem], T.sem.ls, pid, rid, emask), [i], [], 2.6 if first else 0.3,
+                3.9 if first else 1.6, "r", "ls")
+        c = 0.5 + size(i) * 0.0026
+        add("x", None, [], [o], c, c + 0.3, "x", sem, [j])
+
     def victim(t): return T.cores[(rank + 1 + t % (NR - 1)) % NR]
     def attacker(t): return T.cores[(rank - 1 - t % (NR - 1)) % NR]
-    def dg(n): k = DN.index(n); return s("dg", 128 * k, 128 * k + 128)
     def cw(n): return col("cw", 16 * CN.index(n) + 15)
-    def keys(n, k): return " ".join("%s%d" % (n, i) for i in range(k))
-    def R(t, k): return s("R%d" % t, 64 * k, 64 * k + 64)
+    def dg(n): k = DN.index(n); return s("dg", 128 * k, 128 * k + 128)
     def C(t, k): return s("C%d" % t, 64 * k, 64 * k + 64)
-    def dga(a, b):
-        for k in range(a, b):
-            act(dg(DN[k]), s("idb"), "idb dw", DN[k], scale=col("dw", 16 * k + 15))
+    def R(t, k):
+        return s("R%d" % t, 64 * k, 64 * k + 64) if k < 2 else s("dl%d" % t, 128, 192)
+    def dl(t): return s("dl%d" % t, 64, 128)
 
-    dma("s", s("oc"), T.oc[:], "loc", "", "oc")
-    dma("a", s("xc_", 16, 16 + U // 2), T.x[:, 0:U // 2], "lx0", "", "xc0")
-    dma("s", s("xc_", 16 + U // 2, 16 + U), T.x[:, U // 2:U], "lx1", "", "xc1")
-    dma("s", s("cd"), T.cd[:], "lcd", "", "cd")
+    dma("s", s("oc")[0], T.oc[:], "loc", 2.2, w=[s("oc")]); seq("ld")
+    dma("a", s("xc_", 16, 16 + U // 2)[0], T.x[:, 0:U // 2], "lx0", 3.6, w=[s("xc_", 16, 16 + U // 2)])
+    dma("s", s("xc_", 16 + U // 2, 16 + U)[0], T.x[:, U // 2:U], "lx1", 4.2, w=[s("xc_", 16 + U // 2, 16 + U)]); seq("ld")
+    dma("s", s("cd")[0], T.cd[:], "lcd", 4.8, w=[s("cd")]); seq("ld")
 
     HW = 336
-    ms(s("ones"), 1.0, "ones")
-    ms(s("rt"), 0.0, "rt")
-    ms(s("rt2"), 0.0, "rt2")
-    io_(col("pi", 0), [[0, 1]], 0, 1, "pi", True)
-    io_(s("pat"), [[0, 18], [1, 16]], 0, 0, "pat")
-    io_(s("x144"), [[1, 144]], 0, 0, "x144")
-    io_(s("pt", 0, HW), [[0, 16], [1, 21]], 0, 0, "pt0")
-    io_(s("pt", HW, 2 * HW), [[0, 8], [-1, 2], [0, 21]], 1, 0, "pt1")
-    io_(s("pt", 2 * HW, 3 * HW), [[1, 8], [0, 42]], 0, 0, "pt2")
-    io_(s("rep"), [[1, 8], [0, 16]], 0, 0, "rep")
-    for k, n in enumerate(CN):
-        for f, c in COLS[n].items():
-            act(col("rt", 16 * k + f), col("ones", 0), "rt ones", "", scale=float(c))
-    mark("a", "rt")
-    deps("v", ["rt2"], [])
-    for k, n in enumerate(DN):
-        for f, c in DIAG[n].items():
-            if k < 6:
-                act(col("rt2", 16 * k + f), col("ones", 0), "rt2 ones", "", scale=float(c))
-            elif k < 9:
-                ms(col("rt2", 16 * k + f), float(c), "")
-            else:
-                io_(col("rt2", 16 * k + f), [[0, 1]], int(c), 0, "", r="rt2")
-    mark("a", "rt2a"); mark("g", "rt2g"); mark("v", "rt2v")
-    io_(s("mm"), [[0, 16], [1, 8]], 0, 0, "mm")
-    io_(s("kM"), [[-2048, 32], [0, 8]], 31 * 2048 + 1024, 0, "kM")
+    ms(s("ones"), 1.0)
+    ms(s("rt", 0, 16 * NE), 0.0)
+    ms(s("rt", 16 * NE, 16 * NC_), 0.0)
+    io_(col("pi", 0), [[0, 1]], 0, 1)
+    io_(s("pat"), [[0, 16], [1, 16]], 0)
+    io_(s("x144"), [[1, 144]], 0)
+    io_(s("pt", 0, HW), [[0, 16], [1, 21]], 0)
+    io_(s("pt", HW, 2 * HW), [[0, 8], [-1, 2], [0, 21]], 1)
+    io_(s("pt", 2 * HW, 3 * HW), [[1, 8], [0, 42]], 0)
+    if "runs" not in MEMO:
+        MEMO["runs"] = []
+        for a, b in ((0, NE), (NE, NC_)):
+            todo = {16 * k + f: c for k in range(a, b) for f, c in COLS[CN[k]].items()}
+            while todo:
+                run = max(([p0 + d * i for i in range(m)] for p0 in sorted(todo) for d in range(1, 16 * (b - a)) for m in (6, 5, 4, 3, 2, 1)
+                           if all(todo.get(p0 + d * i) == todo[p0] for i in range(m))), key=len)
+                MEMO["runs"].append((run, float(todo[run[0]])))
+                for p0 in run: del todo[p0]
+    for k, (run, c) in enumerate(MEMO["runs"]):
+        o = s("rt", run[0], run[-1] + 1, run[1] - run[0] if len(run) > 1 else 1)
+        if k % 6 == 5: ms(o, c)
+        else: act(o, s("ones", 0, len(run)), scale=c)
+    ts(col("pi", 1), col("pi", 0), 15, A.bitwise_and)
+    ts(col("pi", 2), col("pi", 0), 4, A.arith_shift_right)
+    ts(col("pi", 3), col("pi", 0), 1, A.bitwise_and)
+    cp(s("pcol", 0, 4), s("pi"))
+    rc, gc_, pc = col("pcol", 1), col("pcol", 2), col("pcol", 0)
+    cp(s("ocu"), s("oc"))
+    ts(s("r16", 0, 256), s("pat"), rc, A.is_equal)
+    cp(s("r16", 256, 272), s("r16", 0, 16))
+    ts(s("sgm"), s("pat"), 0.5, A.is_gt)
+    ts(s("g8"), s("x144", 0, 8), gc_, A.is_equal)
+    ts(s("idb"), s("x144", 0, 128), pc, A.is_equal)
+    t2(s("nid"), s("x144", 0, 128), pc, A.is_equal, -1.0, A.mult)
+    cp(P(6, 0, 192), s("r16", 0, 192))
+    for a, b in ((0, NE), (NE, NE + 10), (NE + 10, NC_)):
+        tt(s("seg", 16 * a, 16 * b), P(6, 0, 16 * (b - a)), s("rt", 16 * a, 16 * b), A.mult)
+        scan(s("cw", 16 * a, 16 * b), s("sgm", 0, 16 * (b - a)), s("seg", 16 * a, 16 * b), 0.0, A.mult, A.add)
+    ms(s("fR"), 0.0); ms(s("fL"), 0.0); ms(s("fZ"), 0.0)
+    for n, fs in (("fR", (1, 9)), ("fL", (0, 8)), ("fZ", (2,))):
+        for f in fs:
+            act(s(n, f, 128, 16), s("g8"))
+    for k, n in enumerate(("s_i", "s_e", "s_j")):
+        act(s("ds", 128 * k, 128 * k + 128), s("idb"), scale=cw(n))
+    t2(s("sb"), s("x144", 0, 64, 8), cw("s_j"), A.mult, cw("s_c"), A.add)
+    for k in range(3):
+        mm(P(7, 0, HW), s("ds", 128 * k, 128 * k + 128), s("pt", HW * k, HW * k + HW), k == 0, k == 2)
+    act(s("cp2", 0, HW), P(7, 0, HW)); act(s("cp2", HW, 2 * HW), P(7, 0, HW))
+    ms(s("ad", 0, 16), 0.0); ms(s("xc_", 0, 16), 0.0); ms(s("stat", 0, 16), 100.0)
+    t2(col("pcol", 4), gc_, 16.0, A.mult, 15.0, A.add)
+    t2(col("pcol", 5), col("pcol", 3), -2048.0, A.mult, 2048.0, A.add)
+    ts(col("pcol", 7), rc, 42.0, A.mult)
+    t2(s("qz"), s("x144"), col("pcol", 4), A.is_equal, 61.0, A.mult)
+    cp(s("l_rep"), s("x144", 0, 8))
+
+    xw = s("xc_", 16, 16 + U)
+    for c, (a, b) in enumerate(((0, 22), (22, 42), (42, 84), (84, 126), (126, 146), (146, 168))):
+        (cp if c in (0, 2, 4) else act)(s("xb_", 16 * a, 16 * b), ind(xw, s("ocu", a, b)))
+    act(s("eo0", 0, 128, 2), s("xb_", 0, U, 42))
+    act(s("eo0", 1, 128, 2), s("xb_", 20, U, 42))
+    send(victim(0), s("el0", 128, 256), s("eo0"), "ae0", True)
+    for h in range(8):
+        lo = max(HW * h, 1); hi = HW * h + HW; b = (0, 1, 4)[h % 3]
+        mm(P(b, 0, hi - lo), s("idb"), s("xb_", lo, hi), True, False)
+        mm(P(b, 0, hi - lo), s("nid"), s("xb_", lo - 1, hi - 1), False, True)
+        act(s("ad", 15 + lo, 15 + hi), P(b, 0, hi - lo), AF.Abs)
+        lo = HW * h; b = (2, 3, 5)[h % 3]
+        mm(P(b, 0, HW), s("fZ"), s("xb_", lo, hi), True, False)
+        mm(P(b, 0, HW - 1), s("fR"), s("ad", 16 + lo, 15 + hi), False, False)
+        mm(P(b, 0, HW), s("fL"), s("ad", 15 + lo, 15 + hi), False, True)
+        act(s("spos", lo, hi), P(b, 0, HW), bias=col("sb", h))
+        if h % 2:
+            for a, b in ((0, 20), (20, 42)):
+                o = 42 * (h // 2)
+                tt(ind(s("stat", 16, 16 + U), s("ocu", o + a, o + b)), s("spos", 16 * (o + a), 16 * (o + b)), s("cp2", 16 * a, 16 * b), A.add)
     for kh in range(2):
         for j1 in range(2):
             k = 2 * kh + j1
-            op("g", lambda: g.affine_select(s("pm", 128 * k, 128 * k + 128), s("ones"), [[32, 4], [1000 - 2000 * j1, 2], [2, 16]],
-                                            A.is_equal, 0.0, kh + 1000 * j1, -1), "ones", "pm%d" % k)
-    ts(col("pi", 1), col("pi", 0), 15, A.bitwise_and, "pi", "pi1")
-    ts(col("pi", 2), col("pi", 0), 4, A.arith_shift_right, "pi", "pi2")
-    ts(col("pi", 3), col("pi", 0), 1, A.bitwise_and, "pi", "pi3")
-    for n in ("fR", "fL", "fZ"):
-        ms(s(n), 0.0, n)
-    cp(s("pcol", 0, 4), s("pi"), "pi pi1 pi2 pi3", "pcol")
-    ms(s("ad", 0, 16), 0.0, "ad_a")
-    for n in ("w0", "w1", "wf", "wl", "wc"):
-        ms(s(n), 0.0, n)
-    cp(s("ocu"), s("oc"), "oc", "ocu")
-    rc, gc_, pc = col("pcol", 1), col("pcol", 2), col("pcol", 0)
-    ts(s("r16"), s("pat"), rc, A.is_equal, "pat pcol", "r16")
-    ts(s("sgm"), s("pat"), 0.5, A.is_gt, "pat", "sgm")
-    ts(s("g8"), s("x144", 0, 8), gc_, A.is_equal, "x144 pcol", "g8")
-    ts(s("idb"), s("x144", 0, 128), pc, A.is_equal, "x144 pcol", "idb")
-    t2(s("nid"), s("x144", 0, 128), pc, A.is_equal, -1.0, A.mult, "x144 pcol", "nid")
-    tt(s("seg", 0, 16 * NC_), s("rt"), s("r16", 0, 16 * NC_), A.mult, "rt r16", "seg")
-    for n, fs in (("fR", (1, 10)), ("fL", (0, 12)), ("fZ", (2,))):
-        deps("v", [n], [])
-        for f in fs:
-            cp(s(n, f, 128, 16), s("g8"), "g8", "")
-        mark("v", n)
-    scan(s("cw"), s("sgm", 0, 16 * NC_), s("seg", 0, 16 * NC_), 0.0, A.mult, A.add, "seg sgm", "cw")
-    t2(col("pcol", 4), gc_, 16.0, A.mult, 15.0, A.add, "pcol", "pc4")
-    for k, n in enumerate(("s_i", "s_e", "s_j")):
-        ts(s("ds", 128 * k, 128 * k + 128), s("idb"), cw(n), A.mult, "idb cw", "ds%d" % k)
-    t2(s("sb"), s("x144", 0, 64, 8), cw("s_j"), A.mult, cw("s_c"), A.add, "cw x144", "sb")
-    for k in range(3):
-        mm(P(7, 0, HW), s("ds", 128 * k, 128 * k + 128), s("pt", HW * k, HW * k + HW), k == 0, k == 2, "ds%d pt%d" % (k, k), "P7")
-    cp(s("cdf"), s("cd"), "cd", "cdf")
-    t2(col("pcol", 5), col("pcol", 3), -2048.0, A.mult, 2048.0, A.add, "pcol", "pc5")
-    ms(s("xc_", 0, 16), 0.0, "xcd")
-    ms(s("stat", 0, 16), 100.0, "statd")
-    op("v", lambda: V.transpose(s("cdt"), s("cdf")), "cdf", "cdt")
-    cp(s("cp", 0, HW), P(7, 0, HW), "P7", "cpa")
-    cp(s("cp", HW, 2 * HW), P(7, 0, HW), "P7", "cpb")
-    ms(s("wc", 1, 1024, 4), -1024.0, "wc")
-    ms(s("eo0", 0, 128), 21.0, "eo0c")
-    t2(s("qz"), s("x144"), col("pcol", 4), A.is_equal, 61.0, A.mult, "x144 pc4", "qz")
-    ms(s("wc", 3, 1024, 4), 31.5 * P25, "wc")
-    ts(s("bo"), s("rep"), gc_, A.is_equal, "rep pcol", "bo")
-    ts(col("pcol", 7), rc, 42.0, A.mult, "pcol", "pc7")
-    cp(s("l_rep"), s("x144", 0, 8), "x144", "l_rep")
-
-    def gx(c):
-        act(s("xb_", 672 * c, 672 * c + 672), s("xc_", 16, 16 + U).indirect(s("ocu", 42 * c, 42 * c + 42)), "xc0 xc1 ocu", "xb%d" % c)
-    def diff(h):
-        lo = max(HW * h, 1); hi = HW * h + HW; b = 2 + h % 2
-        k = "xb%d xb%d" % (h // 2, max(h * HW - 1, 0) // 672)
-        mm(P(b, 0, hi - lo), s("idb"), s("xb_", lo, hi), True, False, k + " idb", "P%d" % b)
-        mm(P(b, 0, hi - lo), s("nid"), s("xb_", lo - 1, hi - 1), False, True, k + " nid", "P%d" % b)
-    def dabs(h):
-        lo = max(HW * h, 1); hi = HW * h + HW; b = 2 + h % 2
-        act(s("ad", 15 + lo, 15 + hi), P(b, 0, hi - lo), "P%d ad_a" % b, "ad%d" % h, AF.Abs)
-    def fields(h):
-        lo = HW * h; hi = lo + HW; b = 4 + h % 2
-        mm(P(b, 0, HW), s("fZ"), s("xb_", lo, hi), True, False, "fZ xb%d" % (h // 2), "P%d" % b)
-        mm(P(b, 0, HW - 1), s("fR"), s("ad", 16 + lo, 15 + hi), False, False, "fR ad%d" % h, "P%d" % b)
-        mm(P(b, 0, HW), s("fL"), s("ad", 15 + lo, 15 + hi), False, True, "fL ad_a ad%d" % h, "P%d" % b)
-    def fev(h):
-        lo = HW * h; b = 4 + h % 2
-        act(s("spos", lo, lo + HW), P(b, 0, HW), "P%d sb" % b, "sp%d" % h, bias=col("sb", h))
-    XBK = keys("xb", 4)
-    gx(0)
-    for c in range(4):
-        a, b = 2 * c, 2 * c + 1
-        diff(a); diff(b)
-        if c in (1, 2):
-            gx(c + 1)
-        dabs(a); dabs(b); fields(a); fields(b)
-        if c == 0:
-            gx(1)
-        if c == 2:
-            act(s("eo0", 128, 256, 2), s("xb_", 0, U, 42), XBK, "eo0a")
-            act(s("eo0", 129, 256, 2), s("xb_", 20, U, 42), XBK, "eo0b")
-            send(victim(0), s("el0", 0, 256), s("eo0"), "ae0", "eo0a eo0b eo0c")
-        if c == 3:
-            act(T.TR[:, :, :], s("cdt"), "cdt", "TR")
-        fev(a); fev(b)
+            add("g", lambda k=k, kh=kh, j1=j1: g.affine_select(
+                s("pm", 128 * k, 128 * k + 128)[0], s("ones")[0], [[32, 4], [1000 - 2000 * j1, 2], [2, 16]], A.is_equal, 0.0,
+                kh + 1000 * j1, -1), [s("ones")], [s("pm", 128 * k, 128 * k + 128)], 0.48)
+    cp(s("cdf"), s("cd"))
+    add("v", lambda: V.transpose(s("cdt")[0], s("cdf")[0]), [s("cdf")], [s("cdt")], 0.27)
+    act(c3("TR", None, 0, 32), s("cdt"))
     for k in range(4):
-        mm(P(6, 128 * (k // 2), 128 * (k // 2) + 128), s("pm", 128 * k, 128 * k + 128), T.TR[:, :, 16 * (k % 2):16 * (k % 2) + 16],
-           k % 2 == 0, k % 2 == 1, "TR pm%d" % k, "P6")
-    for o, n in enumerate(("kh", "dh", "sh", "ch")):
-        act(s("wh", o, 32, 4), s("g8"), "g8 cw", "wh%d" % o, scale=cw(n))
-    for o, n in enumerate(("kl", "dl")):
-        act(s("wl", o, 32, 4), s("g8"), "g8 cw wl", "wl%d" % o, scale=cw(n))
-    act(s("wf", 0, 32, 4), s("g8"), "g8 wf", "wf0", scale=2 * H16)
-    act(s("wc", 0, 1024, 4), s("kM"), "kM wc", "wc")
-    act(s("onb"), s("ones"), "ones", "onb")
-    act(s("idf"), s("idb"), "idb", "idf")
+        mm(P(7, 128 * (k // 2), 128 * (k // 2) + 128), s("pm", 128 * k, 128 * k + 128), c3("TR", None, 16 * (k % 2), 16 * (k % 2) + 16), k % 2 == 0, k % 2 == 1)
     for kh in range(2):
-        for B in range(8):
-            act(s("cdT", kh * 128 + B, kh * 128 + 128, 8), P(6, kh * 128 + 16 * B, kh * 128 + 16 * B + 16), "P6", "")
-    mark("a", "cdT")
-
-    io_(s("xt", 0, 68), [[1, 17], [672, 4]], 21, 0, "xta")
-    io_(s("xt", 68, 136), [[-1, 17], [672, 4]], 41, 0, "xtb")
-    io_(s("jc"), [[-32, 64]], 127 * 32, 0, "jc")
-    io_(s("j256"), [[1, 64]], 256, 0, "j256")
-    io_(s("c8"), [[1088, 2], [16, 4]], 0, 0, "c8")
-    io_(s("jb"), [[1, 64]], 0, 0, "jb")
-    io_(s("tq", 64, 320, 80), [[0, 4]], 32768, 0, "tqs")
-    io_(s("kkw"), [[16, 16]], 0, 0, "kkw")
-    fill("XV", XVN, XVN + 16, 0, "xvp"); fill("lr", 0, 64, 21, "lr"); fill("sw0", 0, 320, 0, "sw0")
-    fill("mo0", 64, 80, 0, "mo0d"); fill("mo1", 64, 80, 0, "mo1d")
-    io_(s("kb"), [[1, 256]], 0, 0, "kb")
-    io_(s("c21w"), [[21, 2], [672, 4]], 0, 0, "c21w")
-    io_(s("xP", 0, 68), [[1, 17], [0, 4]], 0, 0, "xPa")
-    io_(s("y1"), [[1, 17], [0, 4]], 1, 0, "y1")
-    io_(s("c21"), [[21, 2], [42, 64]], 0, 0, "c21")
-    fill("T1", 0, 16, 100, "T1d"); fill("T2", 0, 16, 100, "T2d"); fill("T2", 16 + U, 16 + U + 256, 100, "T2e")
-    fill("dl0", 144, 208, 128, "dy1o"); fill("dy2", 0, 64, 0, "dy2o"); fill("xb_", ZC, ZC + 16, 0, "xbz")
-    fill("numb", ZC, ZC + 16, -1, "numbz"); fill("nad", 0, 16, 0, "nad0"); fill("nad", 256, 272, 0, "nad1")
-    fill("xa", 0, 4, 21, "xa"); fill("xe_", 0, 4, 20, "xe_"); fill("xh", 0, 4, 3300 - 4096 * 21, "xh")
-    io_(s("iot"), [[1, U]], 0, 0, "iot")
-    act(s("vq"), s("x144", 0, 64, 16), "x144 pcol", "vq", bias=rc)
-    act(s("xu"), s("xt"), "xta xtb pc7", "xu", bias=col("pcol", 7))
-    for c in range(4):
-        op("v", lambda: V.tensor_tensor(s("stat", 16, 16 + U).indirect(s("ocu", 42 * c, 42 * c + 42)), s("spos", 672 * c, 672 * c + 672), s("cp"), A.add),
-           "ocu cpa cpb sp%d sp%d" % (2 * c, 2 * c + 1), "stat")
-        if c == 0:
-            t2(s("w0", 0, 512, 4), s("mm"), gc_, A.is_equal, -H16, A.mult, "mm pcol w0", "w0a")
-            t2(s("w1", 3, 512, 4), s("mm"), gc_, A.is_equal, -P25 / 16, A.mult, "mm pcol w1", "w1a")
-            tt(s("seg"), s("rt2"), s("r16"), A.mult, "rt2a rt2g rt2v r16", "seg")
-            scan(s("dw"), s("sgm"), s("seg"), 0.0, A.mult, A.add, "seg sgm", "dw")
-
-    def late_act():
-        act(s("kkw"), s("kkw"), "kkw pcol", "kkw", bias=rc)
-        act(s("j32"), s("x144", 0, 64), "x144", "j32", scale=32768.0)
-        act(s("c8"), s("c8"), "c8 pcol", "c8", bias=rc)
-        for t in range(2):
-            act(col("mo%d" % t, 64), col("r16", 6), "r16 mo%dd" % t, "mo%dd" % t, scale=100.0)
-        act(s("kw"), s("kkw"), "kkw", "kw", scale=64.0)
-        act(s("q1"), s("qz"), "qz", "q1", AF.Sign)
-        act(s("cap"), s("r16", 1, 257), "r16", "cap", scale=1e9)
-        act(s("q14"), s("q1"), "q1 r16", "q14", scale=col("r16", 14))
-        act(s("nbo"), s("bo"), "bo", "nbo", scale=-1.0)
-
-    def later_act():
-        act(s("q1"), s("q1"), "q1", "q1", scale=1.0 / 16)
-        act(s("c21w"), s("c21w"), "c21w pc7", "c21w", bias=col("pcol", 7))
-        for k, f in enumerate((15, 9, 14)):
-            act(s("rs", 128 * k, 128 * k + 128), s("bo"), "bo r16", "rs%d" % k, scale=col("r16", f))
+        act(c3("CT", None, 16 * kh, 16 * kh + 16), P(7, 128 * kh, 128 * kh + 128))
+    act(col("cw", 0), col("r16", 15), scale=-M26, bias=cw("hL")); act(col("cw", 1), col("r16", 15), scale=-M26, bias=cw("hR"))
+    for lr_ in range(2):
+        act(s("wf", lr_, 16, 2), s("g8"), scale=2 * H16)
+        act(s("wa", lr_, 16, 2), s("g8"), scale=cw(("aL", "aR")[lr_]))
+        act(s("wh1", lr_, 16, 2), s("g8"), scale=cw(("hL", "hR")[lr_]))
+        act(s("wh2", lr_, 16, 2), s("g8"), scale=col("cw", lr_))
+        act(s("wz", lr_, 16, 2), s("g8"), scale=col("r16", 4 + lr_))
+    K0 = (0, NK[0], NK[0] + NK[1])
+    for b in range(3):
+        nk = NK[b]
+        io_(s("wc", 512 * b, 512 * b + 16 * nk), [[0, 8], [1024, 2], [-2048, nk]], (31 - K0[b]) * 2048)
+    for b in (0, 2):
+        nk = NK[b]; a = 128 * b; e = a + 16 * nk
+        io_(s("gp", a, e), [[1, 8], [0, 2 * nk]], 0)
+        t2(s("w0", a, e), s("gp", a, e), gc_, A.is_equal, -H16, A.mult)
+        act(s("w1", a, e), s("w0", a, e), scale=-1.0 / H16)
+        io_(s("sm", a, e), [[0, 8], [1, 2 * nk]], 0)
+        act(s("sm", a, e), s("sm", a, e), AF.Sign)
+    act(s("onb"), s("ones")); act(s("idf"), s("idb")); act(s("nM"), s("idb"), scale=-M26)
+    io_(s("gid"), [[1, 8], [0, 16]], 0)
+    ts(s("bo"), s("gid"), gc_, A.is_equal)
+    act(s("bo6"), s("bo"), scale=1.0 / 64); act(s("nb6"), s("bo"), scale=-1.0 / 64)
+    for n, w, c in (("i_k", "idb", cw("i_k")), ("i_b", "nid", cw("i_k")), ("i_as", "idb", cw("ub1")), ("i_la", "idb", cw("i_la")),
+                    ("i_j", "idb", col("r16", 3)), ("i_one", "idb", cw("i_one")), ("i_na", "idb", cw("i_na")), ("i_e", "idb", col("r16", 13)),
+                    ("c_l", "idb", cw("c_l")), ("c_r", "idb", cw("c_r"))):
+        act(dg(n), s(w), scale=c)
+    for k, c in enumerate((cw("r_s"), col("r16", 10), cw("r_n"))):
+        act(s("rs", 128 * k, 128 * k + 128), s("bo"), scale=c)
+    io_(s("xt", 0, 68), [[1, 17], [672, 4]], 21)
+    io_(s("xt", 68, 136), [[-1, 17], [672, 4]], 41)
+    io_(s("jc"), [[-32, 64]], 127 * 32)
+    io_(s("j256"), [[1, 64]], 1100)
+    io_(s("j32"), [[1, 64]], 0)
+    io_(s("c8"), [[1088, 2], [16, 4]], 0)
+    io_(s("jb"), [[1, 64]], 0)
+    fill(s("tq", 64, 320, 80), 32768)
+    io_(s("kkw"), [[16, 16]], 0)
+    fill(s("XV", 16 * 116, XVN + 16), 0); fill(s("XV", 16 * 48, 16 * 68), 0); fill(s("lr"), 21)
+    for a in range(0, 1184, 296): fill(s("sw", a, a + 296), 0)
+    io_(s("kb"), [[1, 256]], 0)
+    io_(s("c21w"), [[21, 2], [672, 4]], 0)
+    io_(s("xP", 0, 68), [[1, 17], [0, 4]], 0)
+    io_(s("y1"), [[1, 17], [0, 4]], 1)
+    io_(s("c21"), [[21, 2], [42, 64]], 0)
+    io_(s("m2"), [[0, 4], [1, 16], [0, 2]], 0)
+    io_(s("r2f"), [[1, 4], [0, 2]], 0)
+    cp(s("l_r2"), s("r2f"))
+    ts(s("m2"), s("m2"), rc, A.is_equal)
+    fill(s("T1", 0, 16), 100); fill(s("T2", 0, 16), 100); fill(s("T2", 16 + U, 16 + U + 256), 100)
+    fill(s("dl0", 0, 64), 128); fill(s("dy2", 64, 128), 0); fill(s("xb_", ZC, ZC + 16), 0)
+    fill(s("numb", ZC, ZC + 16), -1); fill(s("nad", 0, 16), 0); fill(s("nad", 256, 272), 0)
+    fill(s("xa"), 21); fill(s("xe_"), 20); fill(s("xh"), TH - 4096 * 21); fill(s("xc"), 21); fill(s("Lw", 4, 8), 0)
+    for a in range(0, U, 384): fill(s("numb", a, a + 384), 0)
+    for t in range(RO - 1): io_(s("numb", U + NS * t, U + NS * t + NS), [[1, NS]], U + NEWC * t)
+    io_(s("numb", Z1, ZC), [[1, NEWC]], U + 2 * NEWC)
+    act(s("vq"), s("x144", 0, 64, 16), bias=rc)
+    act(s("xu"), s("xt"), bias=col("pcol", 7))
+    act(s("kkw"), s("kkw"), bias=rc)
+    act(s("j32"), s("j32"), scale=32768.0, bias=-64.0)
+    act(s("c8"), s("c8"), bias=rc)
+    act(s("kw"), s("kkw"), scale=64.0)
+    act(s("q1"), s("qz"), AF.Sign)
+    act(s("cap"), s("r16", 1, 257), scale=1e9)
+    act(s("q14"), s("q1"), scale=cw("q_c"))
+    act(s("q16"), s("q1"), scale=1.0 / 16)
+    act(s("c21w"), s("c21w"), bias=col("pcol", 7))
+    tt(s("j256"), s("j256"), s("r16", 0, 64), A.mult)
+    for k, (m, b) in enumerate(((1, 0), (1, U + NS - 1), (1, Z1 - 1), (4096, TH), (8192, 4096), (-2, -1))):
+        act(s("bc", 2 * k, 2 * k + 2), s("kkw", 0, 2), scale=float(m), bias=float(b))
+    for r in range(16):
+        mm(P(7, 0, 168), s("q14", 15 - r, 143 - r), s("stat", 16 + r, 16 + U, 16), r == 0, r == 15)
+    cp(s("cl"), P(7, 0, 168))
+    fill(s("op_"), 0)
+    for u in range(6): cp(s("op_", 32 * u, 32 * u + 28), s("oc", u, 168, 6))
+    tt3 = (T.TT[:, :, :], [("TT", np.arange(192))])
+    add("v", lambda: V.transpose(s("ot")[0], s("op_")[0]), [s("op_")], [s("ot")], 0.2)
+    act(tt3, s("ot"))
 
     def unpack(t):
-        for k in range(3):
-            mm(P(7, 64 * k, 64 * k + 64), s("rs", 128 * k, 128 * k + 128), s("dl%d" % t, 80, 144), True, True, "dl%d rs%d" % (t, k), "P7")
+        for k in range(3 if t < RO - 1 else 2):
+            mm(P(7, 64 * k, 64 * k + 64), s("rs", 128 * k, 128 * k + 128), dl(t), True, True)
+        act(s("R%d" % t), P(7, 0, 128))
         if t < RO - 1:
-            act(s("rb"), P(7, 0, 192), "P7", "rb")
-        act(s("R%d" % t), P(7, 0, 192), "P7", "R%d" % t)
+            act(s("na"), P(7, 128, 192), bias=1.0)
 
+    cp(P(5, 448, 512), s("jc"))
     for t in range(RO):
         lim = U + NEWC * t
         el = "el%d" % t
-        landed("ae%d" % t, el)
-        xck = "xc0 xc1 xcd"
-        if t == 0:
-            tab, tk = "stat", "stat statd"
-            xbk = XBK
-        else:
-            tab = "T%d" % t
-            landed("ad%d" % (t - 1), "dl%d" % (t - 1))
-            landed("ap%d" % (t - 1), "xn%d" % (t - 1))
-            landed("ai%d" % (t - 1), "wl%d_" % (t - 1))
+        tab = "stat" if t == 0 else "T%d" % t
+        if t > 0:
+            z0 = U + NS * (t - 1); n0 = 16 + lim - NEWC
             if t == 1:
-                dk, win = "dl0 dy1o", s("dl0", 80, 208)
+                win = s("dl0", 0, 128)
             else:
-                tt(s("dy2", 64, 128), s("dl1", 80, 144), s("cut"), A.add, "dl1 cut", "dy2")
-                dk, win = "dy2 dy2o", s("dy2")
-            tt(s(tab, 16, 16 + U // 2), win.indirect(s("cl", 0, 84)), s("stat", 16, 16 + U // 2), A.add, dk + " cl stat", tab + "a")
+                tt(s("dy2", 0, 64), dl(1), s("cut"), A.add)
+                win = s("dy2")
+            for a in range(0, 168, 42):
+                tt(s(tab, 16 + 16 * a, 16 + 16 * a + 672), ind(win, s("cl", a, a + 42)), s("stat", 16 + 16 * a, 16 + 16 * a + 672), A.add); seq("u")
             unpack(t - 1)
+            act(s("xc_", n0, n0 + 256), s("xb_", z0, z0 + 256))
+            cp(s("wl_"), s("xb_", z0 + 256, z0 + 272))
+            mm(P(3, 0, 255), s("idb"), s("xb_", z0 + 1, z0 + 256), True, False)
+            mm(P(3, 0, 255), s("nid"), s("xb_", z0, z0 + 255), False, True)
+            act(s("nad", 1, 256), P(3, 0, 255), AF.Abs)
+            lst = [("i_as", R(t - 1, 0)), ("i_la", s("lr") if t == 1 else s("cb", 128, 192)), ("i_j", s("jb")), ("i_one", s("onb", 0, 64)),
+                   ("i_na", s("na")), ("i_b", R(t - 1, 2)), ("i_e", s("xb_", z0 + 272, z0 + 336))]
+            for k, (w, x) in enumerate(lst):
+                mm(P(4, 0, 64), dg(w), x, k == 0, k == len(lst) - 1)
+            act(s("mo"), P(4, 0, 64))
+            act(s("ifl"), ind(s("mo"), s("wl_")))
+            mm(P(3, 0, 256), s("fZ"), s("xb_", z0, z0 + 256), True, False)
+            mm(P(3, 0, 256), dg("i_k"), s("kb"), False, False)
+            mm(P(3, 0, 256), s("fL"), s("nad", 0, 256), False, False)
+            mm(P(3, 0, 256), s("fR"), s("nad", 1, 257), False, False)
+            mm(P(3, 0, 256), s("idf"), s("ifl"), False, True)
+            act(s(tab, n0, n0 + 256), P(3, 0, 256))
             for r in range(16):
-                mm(P(7, 256, 268), s("q1", 15 - r, 143 - r), s("rb", r, 192, 16), r == 0, r == 15, "q1 rb", "P7")
-            act(s("wr"), P(7, 256, 268), "P7", "wr")
-            act(s("xf"), s("wr", 4, 8), "wr", "xf", scale=-2.0, bias=1.0)
-            tt(s("xc"), s("xa"), s("wr", 0, 4), A.add, "xa wr", "xc")
-            tt(s("xd"), s("wr", 8, 12), s("xa"), A.subtract, "xa wr", "xd")
-            tt(s("xg"), s("xe_"), s("wr", 4, 8), A.mult, "xe_ wr", "xg")
-            tt(s("xi"), s("xg"), s("c21w", 0, 4) if t == 1 else s("xb"), A.add, "xg xb c21w", "xi")
-            tt(s(tab, 16 + U // 2, 16 + U), win.indirect(s("cl", 84, 168)), s("stat", 16 + U // 2, 16 + U), A.add, dk + " cl stat", tab + "b")
+                mm(P(6, 256, 264), s("q16", 15 - r, 143 - r), s("R%d" % (t - 1), r, 128, 16), r == 0, r == 15)
+            for r in range(16):
+                mm(P(6, 264, 268), s("q16", 15 - r, 143 - r), s("dl%d" % (t - 1), 128 + r, 192, 16), r == 0, r == 15)
+            act(s("wr"), P(6, 256, 268))
+            act(s("xf"), s("wr", 4, 8), scale=-2.0, bias=1.0)
+            tt(s("xc"), s("xa"), s("wr", 0, 4), A.add)
+            tt(s("xd"), s("wr", 8, 12), s("xa"), A.subtract)
+            tt(s("xg"), s("xe_"), s("wr", 4, 8), A.mult)
+            tt(s("xi"), s("xg"), s("c21w", 0, 4) if t == 1 else s("xb"), A.add)
+            act(s("xd"), s("xd"), bias=float(z0 - 1))
             for q in range(4):
-                act(s("xP", 68 + q, 136, 4), s("y1", q, 68, 4), "y1 xc", "xP%d" % q, scale=-1.0, bias=col("xc", q))
-            act(s("xd"), s("xd"), "xd", "xd", bias=float(lim - NEWC))
-            for q in range(4):
-                act(s("xm", q, 136, 4), s("xP", q, 136, 4), "xPa xh xP%d" % q, "xm%d" % q, scale=4096.0, bias=col("xh", q))
-            for q in range(4):
-                act(s("xt", q, 136, 4), s("xP", q, 136, 4), "xf xi xP%d" % q, "xt%d xta xtb" % q, scale=col("xf", q), bias=col("xi", q))
-            for q in range(4):
-                act(s("xu", q, 136, 4), s("xP", q, 136, 4), "xd xP%d" % q, "xu%d" % q, bias=col("xd", q))
-            xck += " xn0" + (" xn1" if t == 2 else "")
-            xbk = XBK + " xbn0" + (" xbn1" if t == 2 else "")
-            tk = "%sa %sb %sd %sn" % (tab, tab, tab, tab) + (" T2e" if t == 2 else "")
-        if t > 0:
-            n0 = 16 + lim - NEWC
-            xn = "xn%d" % (t - 1)
-            mm(P(2, 0, 255), s("idb"), s("xc_", n0 + 1, n0 + 256), True, False, xn + " idb", "P2")
-            mm(P(2, 0, 255), s("nid"), s("xc_", n0, n0 + 255), False, True, xn + " nid", "P2")
-            act(s("nad", 1, 256), P(2, 0, 255), "P2 nad0 nad1", "nad", AF.Abs)
+                act(s("xP", 68 + q, 136, 4), s("y1", q, 68, 4), scale=-1.0, bias=col("xc", q))
+                act(s("xm", q, 136, 4), s("xP", q, 136, 4), scale=4096.0, bias=col("xh", q))
+                act(s("xt", q, 136, 4), s("xP", q, 136, 4), scale=col("xf", q), bias=col("xi", q))
+                act(s("xu", q, 136, 4), s("xP", q, 136, 4), bias=col("xd", q))
+            tt(P(5, 0, 136), s("xm"), s("xu"), A.min)
+            tt(P(5, 0, 136), P(5, 0, 136), s("xt"), A.max)
+            t2(s("l_xv"), P(5, 0, 136), 0.0, A.max, float(z0 + 255), A.min)
+        else:
+            cp(s("l_xv"), s("xu"))
+        for a, b in (((0, 24), (24, 48), (68, 92), (92, 116)) if t == 0 else ((0, 34), (34, 68), (68, 102), (102, 136))):
+            act(s("XV", 16 * a, 16 * b), ind(s("xb_", 0, U + NS * t), s("l_xv", a, b))); seq("xv")
         for r in range(16):
-            mm(P(6, 0, 8), s("qz", 15 - r, 143 - r), s(el, 128 + r, 256, 16), r == 0, r == 15, "qz " + el, "P6")
-        act(s("zs"), P(6, 0, 8), "P6", "zs", bias=float(4096 - lim))
+            mm(P(6, 0, 8), s("qz", 15 - r, 143 - r), s(el, 128 + r, 256, 16), r == 0, r == 15)
+        act(s("zs"), P(6, 0, 8), bias=float(4096 - lim))
         for B in range(8):
-            act(s("mf", B, 256, 8), s("cdT", B, 256, 8), "cdT zs", "mf%d" % B, bias=col("zs", B))
-        if t > 0:
-            act(s("ifl"), s("dl%d" % (t - 1), 0, 80).indirect(s("wl%d" % (t - 1))), "dl%d wl%d_" % (t - 1, t - 1), "ifl")
-            mm(P(3, 0, 256), s("fZ"), s("xc_", n0, n0 + 256), True, False, xn + " fZ", "P3")
-            mm(P(3, 0, 256), dg("i_k"), s("kb"), False, False, "kb i_k", "P3")
-            mm(P(3, 0, 256), s("fL"), s("nad", 0, 256), False, False, "fL nad", "P3")
-            mm(P(3, 0, 256), s("fR"), s("nad", 1, 257), False, False, "fR nad", "P3")
-            mm(P(3, 0, 256), s("idf"), s("ifl"), False, True, "idf ifl", "P3")
-        for k in range(3):
-            act(s(el, 256 + 128 * k, 384 + 128 * k), s(el, 128, 256), el, el + "x%d" % k)
-        if t > 0:
-            act(s("xb_", lim - NEWC, lim), s("xc_", n0, n0 + 256), xn, "xbn%d" % (t - 1))
-            act(s(tab, n0, n0 + 256), P(3, 0, 256), "P3", tab + "n")
-        else:
-            dga(6, 11)
-        for b in range(2):
-            mm(P(b), s(el, 128, 256), s("w0"), True, False, "w0a " + el, "P%d" % b)
-            mm(P(b), s(el, 0, 128), s("w1"), False, False, "w1a " + el, "P%d" % b)
-            o = OFF["onb"][1]; o2 = OFF["wc"][1]
-            mm(P(b), T.B[0:1, o:o + 128], T.B[0:1, o2 + 512 * b:o2 + 512 * b + 512], False, False, "onb wc", "P%d" % b)
-        cp(s("mi"), s("mf"), keys("mf", 8), "mi")
-        ts(s("mj"), s("mi"), 4095, A.bitwise_and, "mi", "mj")
-        t2(s("ml"), s("mj"), float(4096 - lim - 16), A.subtract, 0.0, A.max, "mj", "ml")
-        cb = (0, 4, 8, 12, 16, 20, 24, 28, 31, 32)
-        for c in range(9):
-            a, b = 128 * cb[c], 128 * cb[c + 1]
-            lst = s("ml", a // 16, b // 16)
-            tt(s("MN", a, b), s("xc_", 0, 16 + lim).indirect(lst), s(el, 128, 128 + b - a), A.min,
-               "ml %s %s %sx0 %sx1 %sx2" % (xck, el, el, el, el), "MN%d" % c)
-            act(s("G", a, b), s(tab, 0, 16 + lim).indirect(lst), "ml " + tk, "G%d" % c, AF.Relu)
-            for k in range(cb[c], cb[c + 1]):
-                b = k // 16; o = P(b, 32 * (k % 16), 32 * (k % 16) + 32)
-                mm(o, s("MN", 128 * k, 128 * k + 128), s("wf"), False, False, "wf0 MN%d" % c, "P%d" % b)
-                mm(o, s("G", 128 * k, 128 * k + 128), s("wh"), False, False, keys("wh", 4) + " G%d" % c, "P%d" % b)
-                mm(o, s("G", 128 * k, 128 * k + 128), s("wl"), False, k % 16 == 15, "wl0 wl1 G%d" % c, "P%d" % b)
+            act(s("mf", B, 256, 8), c3("CT", B, 0, 32), bias=col("zs", B))
+        for a, b in ((0, 48), (48, 256)):
+            cp(s("mi", a, b), s("mf", a, b))
+            ts(s("mj", a, b), s("mi", a, b), 4095, A.bitwise_and)
+            t2(s("ml", a, b), s("mj", a, b), float(4096 - lim - 16), A.subtract, 0.0, A.max)
+        act(s(el, 256, 384), s(el, 128, 256)); act(s(el, 384, 640), s(el, 128, 384))
+        for b in range(3):
+            nk = NK[b]; o = 256 * (b // 2)
+            mm(P(b, 0, 16 * nk), row0("onb", 0, 128), row0("wc", 512 * b, 512 * b + 16 * nk), True, False)
+            mm(P(b, 0, 16 * nk), s(el, 128, 256), s("w0", o, o + 16 * nk), False, False)
+            if t > 0:
+                mm(P(ZB[b], 0, 16 * nk), s(el, 0, 128), s("w1", o, o + 16 * nk), True, False)
+        for c in range(len(CB) - 1):
+            a, e = 128 * CB[c], 128 * CB[c + 1]
+            tt(s("MN", a, e), ind(s("xc_", 0, 16 + lim), s("ml", a // 16, e // 16)), s(el, 128, 128 + e - a), A.min); seq("mn")
+            if CB[c] in CG:
+                e2 = 128 * CG[CG.index(CB[c]) + 1]
+                act(s("G", a, e2), ind(s(tab, 0, 16 + lim), s("ml", a // 16, e2 // 16)), AF.Relu); seq("g")
+            for k in range(CB[c], CB[c + 1]):
+                b = 0 if k < K0[1] else (1 if k < K0[2] else 2)
+                nk = NK[b]; last = k - K0[b] == nk - 1
+                o = P(b, k - K0[b], 16 * nk, nk)
+                mm(o, s("MN", 128 * k, 128 * k + 128), s("wf"), False, False)
+                if t == 0:
+                    mm(o, s("G", 128 * k, 128 * k + 128), s("wa"), False, last)
+                else:
+                    mm(P(ZB[b], k - K0[b], 16 * nk, nk), s("G", 128 * k, 128 * k + 128), s("wz"), False, last)
+                    mm(o, s("G", 128 * k, 128 * k + 128), s("wh%d" % t), False, False)
+                if last:
+                    o = 256 * (b // 2)
+                    if t > 0:
+                        act(s("zb", 256 * b, 256 * b + 16 * nk), P(ZB[b], 0, 16 * nk), AF.Relu, bias=-31.0)
+                        mm(P(b, 0, 16 * nk), s("nM"), s("zb", 256 * b, 256 * b + 16 * nk), False, True)
+                    scan(s("ks", 256 * b, 256 * b + 16 * nk), s("sm", o, o + 16 * nk), P(b, 0, 16 * nk), 0.0, A.mult, A.max)
+                    if b == 1:
+                        tt(s("red"), s("ks", 2 * nk - 1, 16 * nk, 2 * nk), s("ks", 256 + 2 * nk - 1, 256 + 16 * nk, 2 * nk), A.max)
         if t == 0:
-            cp(s("l_xv"), s("xu"), "xu", "l_xv")
-        else:
-            tt(s("xm"), s("xm"), s("xu"), A.min, keys("xm", 4) + " " + keys("xu", 4), keys("xm", 4))
-            tt(s("xm"), s("xm"), s("xt"), A.max, "xm0 " + keys("xt", 4), keys("xm", 4))
-            t2(s("l_xv"), s("xm"), 0.0, A.max, float(lim - 1), A.min, "xm0", "l_xv")
-        act(s("XV", 0, XVN), s("xb_", 0, lim).indirect(s("l_xv")), "l_xv " + xbk, "XV")
-        if t == 0:
-            late_act()
-            act(s("sB", 0, 1008), s("stat", 16, 16 + 1008), "stat", "sB0")
-        else:
-            act(s("numb", 672 * (t - 1), 672 * t), s("iot").indirect(s("ocu", 42 * (t - 1), 42 * t)), "iot ocu", "numb%d" % (t - 1))
-
-        for b in range(2):
-            ts(s("kM", 128 * b, 128 * b + 128), P(b, 2, 512, 4), 0.0, A.is_gt, "P%d" % b, "kM%d kM" % b)
-            tt(s("kt", 128 * b, 128 * b + 128), P(b, 1, 512, 4), s("kM", 128 * b, 128 * b + 128), A.mult, "P%d kM%d" % (b, b), "kt%d" % b)
-            tt(s("kk", 128 * b, 128 * b + 128), P(b, 0, 512, 4), s("kt", 128 * b, 128 * b + 128), A.add, "P%d kt%d" % (b, b), "kk%d" % b)
-            tt(s("kf", 128 * b, 128 * b + 128), P(b, 3, 512, 4), s("kk", 128 * b, 128 * b + 128), A.min, "P%d kk%d" % (b, b), "kf%d" % b)
-        for gi in range(8):
-            red(col("red", gi), s("kf", gi, 256, 8), A.max, "kf0 kf1", "red%d" % gi)
-        ts(s("ri"), s("red"), 0.0, A.max, keys("red", 8), "ri")
-        ts(s("rj"), s("ri"), 0xFF07FF, A.bitwise_and, "ri", "rj")
-        ts(s("rep"), s("rj").indirect(s("l_rep")), col("pcol", 5), A.add, "rj l_rep pc5", "rep")
-        op("t", lambda: g.tensor.transpose(P(2, 0, 128), s("rep"), s("idf")), "rep idf", "P2")
-        if t == 0:
-            for k in range(6):
-                ts(dg(DN[k]), s("idb"), col("dw", 16 * k + 15), A.mult, "idb dw", DN[k])
-        if t > 0:
-            tt(s("lr"), s("rb", 0, 64), s("el0", 0, 64) if t == 1 else s("eo1", 0, 128, 2), A.add, "rb el0 eo1c", "lr")
-        if t == 1:
-            tt(s("xg"), s("e80", 0, 4), s("e80", 4, 8), A.add, "e80 e80b", "xg")
-            tt(s("xb"), s("e80", 0, 4), s("c21w", 4, 8), A.add, "e80 c21w", "xb")
-        if t == 2:
-            tt(s("ge"), s("c21", 64, 128), C(0, 0), A.add, "c21 C0", "ge")
-            tt(s("gb"), s("gb"), R(1, 1), A.mult, "gb R1", "gb")
-        cp(s("he"), P(2, 0, 128, 2), "P2", "he")
-        tt(s("Hi"), P(2, 1, 128, 2), s("he"), A.max, "P2 he", "Hi")
+            o = OFF["numb"][1]
+            for k in range(8):
+                dma("s", T.F[16 * k:16 * k + 1, o:o + U], T.TT[32 * (k // 2):32 * (k // 2) + 28, :, 16 * (k % 2):16 * (k % 2) + 16],
+                    "ln%d" % k, 3.0, r=[tt3, s("MN", 0, 16)], w=[s("numb", k, U, 8)]); seq("ln")
+        tt(s("ri"), s("red"), s("ks", 512 + 2 * nk - 1, 512 + 16 * nk, 2 * nk), A.max)
+        ts(s("rj"), s("ri"), 0xFF07FF, A.bitwise_and)
+        ts(s("rep"), ind(s("rj"), s("l_rep")), col("pcol", 5), A.add)
+        add("t", lambda: g.tensor.transpose(P(3, 0, 128)[0], s("rep")[0], s("idf")[0]), [s("rep"), s("idf")], [P(3, 0, 128)], 0.3)
+        cp(s("he"), P(3, 0, 128, 2))
+        tt(s("Hi"), P(3, 1, 128, 2), s("he"), A.max)
         Hi = s("Hi")
-        ts(s("vf"), Hi, 63, A.bitwise_and, "Hi", "vf")
-        t2(s("dm"), Hi, 6, A.logical_shift_right, 31, A.bitwise_and, "Hi", "dm")
-        ts(s("g16"), Hi, 0xFF0000, A.bitwise_and, "Hi", "g16")
+        ts(s("vf"), Hi, 63, A.bitwise_and)
+        t2(s("dm"), Hi, 6, A.logical_shift_right, 31, A.bitwise_and)
+        ts(s("g16"), Hi, 0xFF0000, A.bitwise_and)
+        tt(P(5, 64, 128), s("g16"), P(5, 448, 512), A.add)
+        tt(P(5, 0, 64), P(5, 64, 128), s("dm"), A.add)
         for q in range(4):
-            ts(s("tq", 80 * q, 80 * q + 64), s("vf"), col("vq", q), A.is_equal, "vf vq", "tq%d" % q)
-        tt(s("S1"), s("dm"), s("jc"), A.add, "dm jc", "S1")
-        ts(s("pl"), Hi, 2047, A.bitwise_and, "Hi", "pl")
-        tt(s("S"), s("S1"), s("g16"), A.add, "S1 g16", "S")
-        t2(s("d64"), Hi, 4, A.logical_shift_right, 64, A.bitwise_and, "Hi", "d64")
-        for q in range(4):
-            tt(s("tq", 80 * q, 80 * q + 64), s("tq", 80 * q, 80 * q + 64), s("S"), A.mult, "S tq%d" % q, "tq%d" % q)
-        for q in range(4):
-            red(col("best", q), s("tq", 80 * q, 80 * q + 65), A.max, "tqs tq%d" % q, "best%d" % q)
-        for q in range(4):
-            ts(s("W", 64 * q, 64 * q + 64), s("tq", 80 * q, 80 * q + 64), col("best", q), A.is_ge, "tq%d best%d" % (q, q), "W%d" % q)
-        for q in range(4):
-            mm(P(3, 0, 64), s("bo"), s("W", 64 * q, 64 * q + 64), q == 0, q == 3, "bo W%d" % q, "P3")
-        t2(s("mu"), Hi, 6, A.logical_shift_right, 15, A.bitwise_and, "Hi", "mu")
-        tt(s("pos0"), s("pl"), s("d64"), A.add, "pl d64", "pos0")
-        ts(s("size"), s("mu"), 1.0, A.add, "mu", "size")
-        if t < RO - 1:
-            tt(s("mm", 0, 64), s("pos0"), s("r16", 0, 64), A.mult, "pos0 r16", "mm")
-        tt(s("ws"), P(3, 0, 64), s("size"), A.mult, "P3 size", "ws")
-        if t < RO - 1:
-            scan(s("ms"), s("sgm", 0, 64), s("mm", 0, 64), 0.0, A.mult, A.add, "mm sgm", "ms")
-        scan(s("tot"), s("ones", 0, 64), s("ws"), 0.0, A.mult, A.add, "ws ones", "tot")
-        if t < RO - 1:
-            cp(s("l_p0", 0, 4), s("ms", 15, 64, 16), "ms", "l_p0a")
-            ts(s("l_p0", 4, 8), s("ms", 15, 64, 16), 64.0, A.add, "ms", "l_p0b")
-            act(s("g2"), s("XV", 0, XVN + 16).indirect(s("l_p0")), "XV xvp l_p0a l_p0b", "g2")
-            mm(P(4, 0, 64), s("idb"), s("g2", 0, 64), True, False, "g2 idb", "P4")
-            mm(P(4, 0, 64), s("nid"), s("g2", 64, 128), False, True, "g2 nid", "P4")
-            act(s("g2a"), P(4, 0, 64), "P4", "g2a", AF.Abs)
-            mm(P(4, 64, 128), s("bo"), s("g2a"), True, True, "g2a bo", "P4")
-            if t == 0:
-                dga(11, 13)
-            act(s("q_D"), P(4, 64, 128), "P4", "q_D")
-        t2(s("hd"), Hi, 11, A.logical_shift_right, 1, A.bitwise_and, "Hi", "hd")
-        ts(s("ac0"), s("tot"), 256.5, A.is_lt, "tot", "ac0")
-        tt(s("b64"), s("tot"), s("ws"), A.subtract, "tot ws", "b64")
-        tt(s("q_ac"), P(3, 0, 64), s("ac0"), A.mult, "P3 ac0", "q_ac")
-        tt(s("q_as"), s("ac0"), s("ws"), A.mult, "ac0 ws", "q_as")
-        ts(s("q_ba"), s("b64"), 256.0, A.min, "b64", "q_ba")
-        tt(s("q_rv"), s("q_ac"), s("hd"), A.mult, "q_ac hd", "q_rv")
-        if t < RO - 1:
-            tt(s("q_ra"), s("q_as"), s("hd"), A.mult, "q_as hd", "q_ra")
-            ts(s("q_gn"), s("g16"), 1.0 / H16, A.mult, "g16", "q_gn")
-        mo = "mo%d" % t
-        lst = [("d_as", "q_as"), ("d_ba", "q_ba"), ("d_rv", "q_rv")]
-        if t == 0:
-            lst.append(("d_one", "onb"))
-        if t < RO - 1:
-            lst += [("d_ac", "q_ac"), ("d_ra", "q_ra")]
-        if t == 1:
-            lst += [("d_ne", "q_gn"), ("d_e", "q_D")]
-        for k, (w, qn) in enumerate(lst):
-            mm(P(5, 80, 144), dg(w), s(qn, 0, 64), k == 0, k == len(lst) - 1, w + " " + qn, "P5")
-        act(s("val"), s("b64"), "b64", "val", scale=64.0)
-        if t < RO - 1:
-            lst = [("i_ba", s("q_ba"), "q_ba"), ("i_as", s("q_as"), "q_as"), ("i_la", s(el, 0, 128, 2), el), ("i_j", s("jb"), "jb"),
-                   ("i_one", s("onb", 0, 64), "onb"), ("i_ne", s("q_gn"), "q_gn"), ("i_e", s("q_D"), "q_D")]
-            for k, (w, ap, qn) in enumerate(lst):
-                mm(P(5, 0, 64), dg(w), ap, k == 0, k == len(lst) - 1, w + " " + qn, "P5")
-            act(s(mo, 0, 64), P(5, 0, 64), "P5", mo + "a")
-        act(s(mo, 80, 144), P(5, 80, 144), "P5", mo + "b")
-        a = 0 if t < RO - 1 else 80
-        send(attacker(t), s("dl%d" % t, a, 144), s(mo, a, 144), "ad%d" % t, "%sa %sb %sd" % (mo, mo, mo))
-        if t == 0:
-            act(s("sB", 1008, U), s("stat", 16 + 1008, 16 + U), "stat", "sB1")
-            for r in range(16):
-                mm(P(6, 0, 168), s("q14", 15 - r, 143 - r), s("sB", r, U, 16), r == 0, r == 15, "q14 sB0 sB1", "P6")
-            fill("sw1", 0, 320, 0, "sw1")
-            tt(s("j256"), s("j256"), s("r16", 0, 64), A.mult, "j256 r16", "j256")
-        else:
-            act(s("numb", 672 * (t + 1), 672 * (t + 2)), s("iot").indirect(s("ocu", 42 * (t + 1), 42 * (t + 2))), "iot ocu", "numb%d" % (t + 1))
-        bk = keys("best", 4)
-        t2(s("o1"), s("q_ac"), -512.0, A.mult, 512.0, A.add, "q_ac", "o1")
-        cp(s("bi"), s("best"), bk, "bi")
-        tt(s("o2"), s("o1"), s("b64"), A.add, "o1 b64", "o2")
-        red(col("cnt", 0), s("ac0"), A.add, "ac0", "cnt0")
-        tt(s("mm", 0, 64), s("o2"), s("j256"), A.min, "o2 j256", "mm")
-        tt(s("pj"), s("pos0"), s("j32"), A.add, "pos0 j32", "pj")
-        scan(s("ms"), s("sgm", 0, 64), s("mm", 0, 64), 0.0, A.mult, A.add, "mm sgm", "ms")
-        tt(s("val"), s("val"), s("pj"), A.add, "val pj", "val")
-        cp(s("l_off"), s("ms", 15, 64, 16), "ms", "l_off")
-        t2(s("bx"), s("bi"), 5, A.logical_shift_right, 127, A.bitwise_and, "bi", "bx")
-        sw = "sw%d" % t; e8 = "e8%d" % t
-        cp(s(sw).indirect(s("l_off")), s("val"), "l_off val", sw)
-        ts(s("bm"), s("bi"), 15, A.bitwise_and, "bi", "bm")
-        scan(s("Fs"), s(sw, 0, 256), s(sw, 0, 256), 0.0, A.max, A.max, sw, "Fs")
-        t2(s("vx"), s("bx"), col("cnt", 0), A.add, 127.5, A.is_gt, "bx cnt0", "vx")
-        scan(s("F2"), s("Fs"), s("cap"), 1e9, A.min, A.max, "Fs cap", "F2")
-        ts(s("vm"), s("bm"), 1.0, A.add, "bm", "vm")
-        tt(s("Fw"), s("F2", 14, 256, 16), s("F2", 15, 256, 16), A.min, "F2", "Fw")
-        t2(s("bd"), s("bi"), 4, A.logical_shift_right, 1, A.bitwise_and, "bi", "bd")
-        ts(s("cc"), s("Fw"), 32767, A.bitwise_and, "Fw", "cc")
-        tt(s("cs"), s("vx"), s("vm"), A.mult, "vx vm", "cs")
-        tt(s("pw"), s("cc"), s("kw"), A.subtract, "cc kw", "pw")
-        tt(s(e8, 4, 8), s("cs"), s("bd"), A.mult, "cs bd", e8 + "b")
-        t2(s("l_pos"), s("pw"), 0.0, A.max, float(XVN - 1), A.min, "pw", "l_pos")
-        tt(s(e8, 0, 4), s("cs"), s(e8, 4, 8), A.subtract, "cs " + e8 + "b", e8)
+            ts(s("tq", 80 * q, 80 * q + 64), s("vf"), col("vq", q), A.is_equal)
+            tt(s("tq", 80 * q, 80 * q + 64), s("tq", 80 * q, 80 * q + 64), P(5, 0, 64), A.mult)
+            red(col("best", q), s("tq", 80 * q, 80 * q + 65), A.max)
+            ts(s("W", 64 * q, 64 * q + 64), s("tq", 80 * q, 80 * q + 64), col("best", q), A.is_equal)
+            mm(P(4, 0, 64), s("bo"), s("W", 64 * q, 64 * q + 64), q == 0, q == 3)
+        t2(s("mu"), Hi, 6, A.logical_shift_right, 15, A.bitwise_and)
+        t2(s("hd"), Hi, 11, A.logical_shift_right, 1, A.bitwise_and)
+        ts(s("pl"), Hi, 2047, A.bitwise_and)
+        t2(s("d64"), Hi, 4, A.logical_shift_right, 64, A.bitwise_and)
+        tt(P(5, 128, 192), s("pl"), s("d64"), A.add)
         po = "po%d" % t
-        act(s(po), s("XV", 0, XVN).indirect(s("l_pos")), "XV l_pos", po)
-        dst = s("xc_", 16 + lim, 16 + lim + NEWC) if t < RO - 1 else s("xb_", lim, lim + NEWC)
-        send(attacker(t), dst, s(po), "ap%d" % t, po)
-        tt(s("ex"), s(e8).indirect(s("l_rep")), s("r16", 0, 128), A.mult, "r16 l_rep %s %sb" % (e8, e8), "ex")
-        mm(P(4, 192, 256), s("idb"), s("lr"), True, False, "idb lr", "P4")
-        mm(P(4, 192, 256), s("nbo"), s("ex", 0, 64), False, False, "nbo ex", "P4")
-        mm(P(4, 192, 256), s("nbo"), s("ex", 64, 128), False, True, "nbo ex", "P4")
-        mm(P(4, 64, 192), s("bo"), s("ex"), True, True, "bo ex", "P4")
+        if t < RO - 1:
+            tt(s("mm"), P(5, 128, 192), s("r16", 0, 64), A.mult)
+            scan(s("ms"), s("sgm", 0, 64), s("mm"), 0.0, A.mult, A.add)
+            cp(s("l_p0", 0, 4), s("ms", 15, 64, 16))
+            ts(s("l_p0", 4, 8), s("ms", 15, 64, 16), 64.0, A.add)
+            ts(s("q_gn"), s("g16"), 1.0 / H16, A.mult)
+            act(s("g2"), ind(s("XV", 0, XVN + 16), s("l_p0")))
+            mm(P(6, 64, 128), s("idb"), s("g2", 0, 64), True, False)
+            mm(P(6, 64, 128), s("nid"), s("g2", 64, 128), False, True)
+            act(s("g2a"), P(6, 64, 128), AF.Abs)
+            mm(P(6, 128, 192), s("bo"), s("g2a"), True, False)
+            mm(P(6, 128, 192), s("nid"), s("q_gn"), False, True)
+            if t == 1: act(s("U5"), P(6, 128, 192), scale=cw("mDe"))
+            act(s(po, 272, 336), P(6, 128, 192))
+        t2(s("U1"), s("mu"), cw("ua1"), A.mult, cw("ub1"), A.add)
+        t2(P(5, 192, 256), s("mu"), cw("ua2"), A.mult, cw("ub2"), A.add)
+        tt(P(5, 192, 256), P(5, 192, 256), s("hd"), A.mult)
+        if t == 1: tt(P(5, 192, 256), P(5, 192, 256), s("U5"), A.add)
+        tt(s("U1"), P(5, 192, 256), s("U1"), A.add)
+        tt(s("wm"), P(4, 0, 64), s("mu"), A.mult)
+        scan(P(5, 256, 320), P(4, 0, 64), s("wm"), 0.0, A.add, A.add)
+        tt(P(5, 192, 256), P(4, 0, 64), s("U1"), A.mult)
+        ts(s("ac0"), P(5, 256, 320), 256.5, A.is_lt)
+        mo = "mo%d" % t
+        tt(s(mo, 0, 64), P(5, 192, 256), s("ac0"), A.mult)
+        tt(P(5, 320, 384), P(5, 256, 320), s("mu"), A.subtract)
+        ts(s(mo, 64, 128), P(5, 320, 384), 256.0, A.min)
+        send(attacker(t), s("dl%d" % t, 64, 192), s(mo), "ad%d" % t)
+        e8 = "e8%d" % t
+        cp(s("bi"), s("best"))
+        t2(s("bx"), s("bi"), 5, A.logical_shift_right, 127, A.bitwise_and)
+        ts(s("bm"), s("bi"), 15, A.bitwise_and)
+        t2(s("bd"), s("bi"), 4, A.logical_shift_right, 1, A.bitwise_and)
+        t2(s("vm"), s("bm"), 64.0, A.mult, 64.0, A.add)
+        tt(s("et", 4, 8), s("vm"), s("bd"), A.mult)
+        tt(s("et", 0, 4), s("vm"), s("et", 4, 8), A.subtract)
+        red(col("cnt", 0), s("ac0"), A.add)
+        for a in (0, 4):
+            t2(s("vx", a, a + 4), s("bx"), col("cnt", 0), A.add, 127.5, A.is_gt)
+        tt(s(e8), s("et"), s("vx"), A.mult)
         if t < RO - 1:
             eo = "eo%d" % (t + 1)
-            ts(s("e64"), s(e8), 64.0, A.mult, "%s %sb" % (e8, e8), "e64")
-            red(col("cnt", 1), s("q_as"), A.add, "q_as", "cnt1")
-            tt(s("e8i"), s("e64"), s("c8"), A.add, "e64 c8", "e8i")
-            ts(s("ww"), s("Fw"), 15, A.logical_shift_right, "Fw", "ww")
-            cp(s("l_end"), s("e8i"), "e8i", "l_end")
-            t2(s("iv"), s("kkw"), col("cnt", 1), A.is_ge, 64.0, A.mult, "kkw cnt1", "iv")
-            act(s(eo, 0, 128, 2), P(4, 192, 256), "P4", eo + "c")
-            act(s(eo, 1, 128, 2), P(4, 192, 256), "P4", eo + "d")
-            cp(s(eo, 128, 256, 2), s("XV", 0, XVN).indirect(s("l_end", 0, 4)), "XV l_end", eo + "a")
-            act(s(eo, 129, 256, 2), s("XV", 0, XVN).indirect(s("l_end", 4, 8)), "XV l_end", eo + "b")
-            send(victim(t + 1), s("el%d" % (t + 1), 0, 256), s(eo), "ae%d" % (t + 1), "%sa %sb %sc %sd" % (eo, eo, eo, eo))
-            tt(s("w2"), s("ww"), s("iv"), A.max, "ww iv", "w2")
-            cp(s("wo%d" % t), s("w2"), "w2", "wo%d" % t)
-            send(attacker(t), s("wl%d" % t), s("wo%d" % t), "ai%d" % t, "wo%d" % t)
-        act(s("C%d" % t), P(4, 64, 256), "P4", "C%d" % t)
+            tt(s("e8i"), s(e8), s("c8"), A.add)
+            cp(s("l_end"), s("e8i"))
+            cp(s(eo, 128, 256, 2), ind(s("XV", 0, XVN), s("l_end", 0, 4)))
+            act(s(eo, 129, 256, 2), ind(s("XV", 0, XVN), s("l_end", 4, 8)))
+            t2(s("cs"), s("bm"), -1.0, A.mult, -1.0, A.add)
+            tt(s("cs"), s("cs"), s("vx", 0, 4), A.mult)
+            tt(s("Lw", 0, 4), s("cs"), s("xc"), A.add)
+            tt(s(eo, 0, 128), ind(s("Lw"), s("l_r2")), s("m2"), A.mult)
+            send(victim(t + 1), s("el%d" % (t + 1), 0, 256), s(eo), "ae%d" % (t + 1))
+        t2(s("o1"), P(4, 0, 64), -2048.0, A.mult, 2048.0, A.add)
+        tt(P(5, 128, 192), P(5, 128, 192), s("j32"), A.add)
+        tt(P(5, 384, 448), P(5, 320, 384), s("o1"), A.add)
+        tt(s("mm"), P(5, 384, 448), s("j256"), A.min)
+        scan(s("ms"), s("sgm", 0, 64), s("mm"), 0.0, A.mult, A.add)
+        cp(s("l_off"), s("ms", 15, 64, 16))
+        ts(s("val"), P(5, 320, 384), 64.0, A.mult)
+        tt(s("val"), P(5, 128, 192), s("val"), A.add)
+        cp(ind(s("sw"), s("l_off")), s("val"))
+        scan(s("Fs"), s("sw", 1, 257), s("sw", 1, 257), 0.0, A.max, A.max)
+        scan(s("F2"), s("Fs"), s("cap"), 1e9, A.min, A.max)
+        tt(s("Fw"), s("F2", 14, 256, 16), s("F2", 15, 256, 16), A.min)
+        ts(s("cc"), s("Fw"), 32767, A.bitwise_and)
+        tt(s("pw"), s("cc"), s("kw"), A.subtract)
+        t2(s("l_pos"), s("pw"), 0.0, A.max, float(XVN - 1), A.min)
+        act(s(po, 0, 256), ind(s("XV", 0, XVN), s("l_pos")))
+        if t < RO - 1:
+            ts(s("ww"), s("Fw"), 15, A.logical_shift_right)
+            cp(s(po, 256, 272), s("ww"))
+            fill(s("sw", 0, 272), 0)
+        send(attacker(t), s("xb_", U + NS * t, U + NS * t + NS) if t < RO - 1 else s("xb_", Z1, ZC), s(po), "ap%d" % t)
+        tt(s("ex"), ind(s(e8), s("l_rep")), s("r16", 0, 128), A.mult)
+        mm(P(7, 320, 384), s("idb"), s("lr") if t < 2 else s("cb", 128, 192), True, False)
+        if t > 0: mm(P(7, 320, 384), s("idb"), R(t - 1, 0), False, False)
+        mm(P(7, 320, 384), s("nb6"), s("ex", 0, 64), False, False)
+        mm(P(7, 320, 384), s("nb6"), s("ex", 64, 128), False, True)
+        mm(P(7, 192, 320), s("bo6"), s("ex"), True, True)
+        act(s("C%d" % t), P(7, 192, 384))
         if t == 0:
-            cp(s("cl"), P(6, 0, 168), "P6", "cl")
-            act(s("cb"), P(4, 64, 192), "P4", "cb")
-            later_act()
-            dga(15, 16)
-            fill("sw2", 0, 320, 0, "sw2")
-            io_(s("numb", U, ZC), [[1, RO * NEWC]], U, 0, "numbn")
+            act(s("cb"), P(7, 192, 384))
+            mm(P(7, 384, 448), dg("c_l"), s("cb", 0, 64), True, False)
+            mm(P(7, 384, 448), dg("c_r"), s("cb", 64, 128), False, True)
+            act(s("cut"), P(7, 384, 448))
+            act(s("La2"), s("Lw", 0, 4))
+            act(s("xb"), s(e8, 0, 4), scale=1.0 / 64)
+            tt(s("xb"), s("xb"), s("c21w", 4, 8), A.add)
         if t == 1:
-            act(s("xa"), s("xg"), "xg", "xa", scale=-1.0, bias=21.0)
-            act(s("xe_"), s("xg"), "xg", "xe_", scale=-1.0, bias=20.0)
-            act(s("xh"), s("xg"), "xg", "xh", scale=4096.0, bias=3300.0 - 4096 * 21)
-        if t == 0:
-            def mid():
-                dga(13, 15); dga(16, 18)
-                mm(P(6, 256, 320), dg("c_l"), s("cb", 0, 64), True, False, "c_l cb", "P6")
-                mm(P(6, 256, 320), dg("c_r"), s("cb", 64, 128), False, True, "c_r cb", "P6")
-                act(s("cut"), P(6, 256, 320), "P6", "cut")
-                for k, (m, b) in enumerate(((1, 0), (1, U + NEWC), (1, U + 2 * NEWC), (4096, 3300), (4096, 3500), (8192, 4096))):
-                    act(s("bc", 2 * k, 2 * k + 2), s("kkw", 0, 2), "kkw", "", scale=float(m), bias=float(b))
-                mark("a", "bc")
-            mid()
-        if t == 1:
-            act(s("gb"), C(0, 2), "C0", "gb", bias=-1.0)
-            act(s("ha"), R(0, 1), "R0", "ha", scale=-2.0, bias=1.0)
-            act(s("hb"), R(0, 1), "R0", "hb", scale=20.0)
-            act(s("hf"), R(0, 2), "R0", "hf", bias=float(U - 21))
-            act(s("hc"), C(1, 2), "C1", "hc", bias=-1.0)
+            act(s("xa"), s("La2"))
+            act(s("xe_"), s("La2"), bias=-1.0)
+            act(s("xh"), s("La2"), scale=-4096.0, bias=float(TH))
 
     def h(n, ih): return s(n, 64 * ih, 64 * ih + 64)
+    def p5(a, ih): return P(5, a + 64 * ih, a + 64 * ih + 64)
     def bc(k, ih): return col("bc", 2 * k + ih)
-    landed("ad2", "dl2")
-    landed("ap2", "xbn2")
-    act(s("ga"), R(1, 1), "R1", "ga", scale=-2.0, bias=1.0)
+    act(s("gb"), C(0, 2), bias=-1.0)
+    act(s("ga"), R(1, 1), scale=-2.0, bias=1.0)
+    tt(s("ge"), s("c21", 64, 128), C(0, 0), A.add)
+    tt(s("gb"), s("gb"), R(1, 1), A.mult)
+    tt(s("ge"), s("ge"), s("gb"), A.add)
+    for ih in range(2):
+        act(h("fd", ih), s("ga"), scale=bc(0, ih))
+        tt(h("fd", ih), h("fd", ih), s("ge"), A.add)
+    mm(P(3, 64, 128), s("bo6"), s("ex", 0, 64), True, False); mm(P(3, 64, 128), s("nid"), s("cb", 128, 192), False, True)
+    mm(P(3, 128, 192), s("bo6"), s("ex", 0, 64), True, False); mm(P(3, 128, 192), s("nid"), s("cb", 128, 192), False, False)
+    mm(P(3, 128, 192), s("idb"), R(1, 2), False, True)
+    tt(s("gg"), s("ga"), C(2, 0), A.mult)
+    for ih in range(2):
+        act(h("fa", ih), P(3, 64, 128), scale=4096.0, bias=bc(3, ih))
+        act(h("fb", ih), P(3, 128, 192), bias=bc(1, ih))
+        act(h("fc", ih), C(2, 2), scale=-8192.0, bias=bc(4, ih))
+        tt(p5(0, ih), h("fd", ih), s("gg"), A.add)
+    tt(s("fa"), s("fa"), s("fb"), A.min)
+    tt(P(5, 0, 128), P(5, 0, 128), s("fc"), A.max)
+    tt(P(5, 0, 128), P(5, 0, 128), s("fa"), A.max)
+    for ih in range(2):
+        ts(s("l_f", 2 + ih, 256, 4), p5(0, ih), float(ZC), A.min)
+    act(s("ha"), R(0, 1), scale=-2.0, bias=1.0)
+    act(s("hb"), R(0, 1), scale=20.0)
+    act(s("hf"), R(0, 2), bias=float(U - 22))
+    tt(s("hb"), s("hb"), s("c21", 0, 64), A.add)
+    act(s("c1b"), C(1, 2))
+    for ih in range(2):
+        act(h("hm", ih), C(1, 2), scale=-4096.0, bias=bc(3, ih))
+        act(h("hq", ih), C(1, 2), bias=bc(5, ih))
+        act(h("hr", ih), C(1, 0), bias=bc(0, ih))
     unpack(2)
-    act(s("gh"), R(2, 1), "R2", "gh", scale=-2.0, bias=1.0)
-    tt(s("hb"), s("hb"), s("c21", 0, 64), A.add, "hb c21", "hb")
-    tt(s("ge"), s("ge"), s("gb"), A.add, "ge gb", "ge")
-    tt(s("gd"), C(2, 0), C(0, 2), A.subtract, "C0 C2", "gd")
-    tt(s("gg"), s("ga"), C(2, 0), A.mult, "ga C2", "gg")
-    tt(s("gf"), s("gd"), R(1, 2), A.add, "gd R1", "gf")
-    tt(s("hc"), s("hc"), R(2, 1), A.mult, "hc R2", "hc")
+    mm(P(6, 0, 64), s("rs", 0, 128), dl(2), True, False); mm(P(6, 0, 64), s("idb"), s("c1b"), False, True)
+    mm(P(3, 0, 64), s("idb"), R(2, 2), True, False); mm(P(3, 0, 64), s("nid"), s("c1b"), False, True)
     for ih in range(2):
-        act(h("fh", ih), s("gh"), "gh bc", "fh%d" % ih, scale=bc(0, ih))
+        tt(p5(128, ih), h("hq", ih), R(2, 1), A.mult)
+        act(h("hn", ih), P(3, 0, 64), bias=bc(2, ih))
+        act(h("fc", ih), P(6, 0, 64), scale=-8192.0, bias=bc(4, ih))
+    tt(s("fh"), P(5, 128, 256), s("hr"), A.add)
+    tt(P(5, 256, 384), s("hn"), s("hm"), A.min)
+    act(s("fg"), s("fh"), scale=4096.0, bias=float(TH - 4096 * 21))
     for ih in range(2):
-        act(h("fa", ih), s("gd"), "gd bc", "fa%d" % ih, scale=4096.0, bias=bc(3, ih))
-        act(h("fb", ih), s("gf"), "gf bc", "fb%d" % ih, bias=bc(1, ih))
-        act(h("fc", ih), C(2, 2), "C2 bc", "fc%d" % ih, scale=-8192.0, bias=bc(5, ih))
-        act(h("fd", ih), s("ga"), "ga bc", "fd%d" % ih, scale=bc(0, ih))
-    tt(s("gi"), R(2, 2), C(1, 2), A.subtract, "R2 C1", "gi")
-    tt(s("hc"), s("hc"), C(1, 0), A.add, "hc C1", "hc")
-    tt(s("gj"), R(2, 0), C(1, 2), A.add, "R2 C1", "gj")
-    tt(s("ge"), s("ge"), s("gg"), A.add, "ge gg", "ge")
+        tt(p5(128, ih), h("fh", ih), s("ha"), A.mult)
+        tt(p5(0, ih), h("fh", ih), s("hf"), A.add)
+        tt(h("ff", ih), p5(128, ih), s("hb"), A.add)
+    tt(P(5, 256, 384), P(5, 256, 384), s("fc"), A.max)
+    tt(s("fd"), P(5, 0, 128), s("fg"), A.min)
+    tt(P(5, 256, 384), P(5, 256, 384), s("ff"), A.max)
+    tt(P(5, 256, 384), P(5, 256, 384), s("fd"), A.max)
     for ih in range(2):
-        tt(h("fh", ih), h("fh", ih), s("hc"), A.add, "hc fh%d" % ih, "fh%d" % ih)
-    tt(s("fa"), s("fa"), s("fb"), A.min, "fa0 fa1 fb0 fb1", "fa0 fa1")
-    for ih in range(2):
-        tt(h("fd", ih), h("fd", ih), s("ge"), A.add, "ge fd%d" % ih, "fd%d" % ih)
-    act(s("fg"), s("fh"), "fh0 fh1", "fg", scale=4096.0, bias=3000.0 - 4096 * 21)
-    for ih in range(2):
-        act(h("fb", ih), C(1, 2), "C1 bc", "fb%d" % ih, scale=-4096.0, bias=bc(4, ih))
-        act(h("fe", ih), s("gi"), "gi bc", "fe%d" % ih, bias=bc(2, ih))
-    tt(s("fa"), s("fa"), s("fc"), A.max, "fa0 fc0 fc1", "fa0 fa1")
-    for ih in range(2):
-        act(h("fc", ih), s("gj"), "gj bc", "fc%d" % ih, scale=-8192.0, bias=bc(5, ih))
-        tt(h("ff", ih), h("fh", ih), s("ha"), A.mult, "ha fh%d" % ih, "ff%d" % ih)
-    tt(s("fa"), s("fa"), s("fd"), A.max, "fa0 fd0 fd1", "fa0 fa1")
-    for ih in range(2):
-        tt(h("fd", ih), h("fh", ih), s("hf"), A.add, "hf fh%d" % ih, "fd%d" % ih)
-    for ih in range(2):
-        ts(s("l_f", 2 + ih, 256, 4), h("fa", ih), float(ZC), A.min, "fa0", "lf1%d" % ih)
-    tt(s("fb"), s("fb"), s("fe"), A.min, "fb0 fb1 fe0 fe1", "fb0 fb1")
-    for ih in range(2):
-        tt(h("ff", ih), h("ff", ih), s("hb"), A.add, "hb ff%d" % ih, "ff%d" % ih)
-    tt(s("fd"), s("fd"), s("fg"), A.min, "fd0 fd1 fg", "fd0 fd1")
-    tt(s("fb"), s("fb"), s("fc"), A.max, "fb0 fc0 fc1", "fb0 fb1")
-    tt(s("fd"), s("fd"), s("ff"), A.max, "fd0 ff0 ff1", "fd0 fd1")
-    tt(s("fb"), s("fb"), s("fd"), A.max, "fb0 fd0", "fb0 fb1")
-    for ih in range(2):
-        ts(s("l_f", ih, 256, 4), h("fb", ih), float(ZC), A.min, "fb0", "lf0%d" % ih)
-    lk = " lf00 lf01 lf10 lf11"
-    xk = XBK + " xbn0 xbn1 xbn2 xbz" + lk
-    nk = keys("numb", 4) + " numbn numbz" + lk
+        ts(s("l_f", ih, 256, 4), p5(256, ih), float(ZC), A.min)
     o = OFF["YO"][1]
     cuts = (0, 1280, 2560, 3584, 4096)
     for c in range(4):
         a, b = cuts[c], cuts[c + 1]
-        cp(s("Y", a, b), s("xb_").indirect(s("l_f", a // 16, b // 16)), xk, "Y%d" % c)
-        act(s("YO", a, b), s("numb").indirect(s("l_f", a // 16, b // 16)), nk, "YO%d" % c)
-        dma("s", T.y[:, a:b], s("Y", a, b), "so", "Y%d" % c, "")
+        act(s("YO", a, b), ind(s("numb"), s("l_f", a // 16, b // 16))); seq("yo")
+        cp(s("G", a, b), ind(s("xb_"), s("l_f", a // 16, b // 16))); seq("y")
+        dma("s", T.y[:, a:b], s("G", a, b)[0], "so", 1.9 + (b - a) / 1500, r=[s("G", a, b)])
         if c == 2:
-            dma("s", T.yo[:, 0:b], T.F[0:128:16, o:o + b], "so", "YO0 YO1 YO2", "")
-    dma("a", T.yo[:, a:b], T.F[0:128:16, o + a:o + b], "so", "YO3", "")
+            dma("s", T.yo[:, 0:b], T.F[0:128:16, o:o + b], "so", 2.5, r=[s("YO", 0, b)])
+    dma("a", T.yo[:, a:b], T.F[0:128:16, o + a:o + b], "so", 2.0, r=[s("YO", a, b)])
+
+    n = len(ops)
+    if "order" not in MEMO:
+        def gap(j, i):
+            if not ops[i][2][j]: return ops[j][3]
+            if ops[j][0] == ops[i][0] and ops[j][5] == "c":
+                return ops[j][4] + (0.0 if ops[i][0] == "t" else 0.03)
+            return ops[j][4] + (0.0 if ops[i][5] == "x" else 0.06)
+        pre = [[(j, gap(j, i)) for j in o[2]] for i, o in enumerate(ops)]
+        suc = [[] for _ in range(n)]
+        for i in range(n):
+            for j, d in pre[i]: suc[j].append((i, d - ops[j][3] + ops[i][3]))
+        MEMO["g"] = (ops, pre, suc, BOOST)
+        prio = [0.0] * n
+        for i in range(n - 1, -1, -1):
+            prio[i] = max([d + prio[k] for k, d in suc[i]] + [ops[i][4] - ops[i][3]]) + BOOST.get(i, 0.0)
+            for k, d in suc[i]:
+                if prio[i] + ops[i][3] <= prio[k] + ops[k][3]: prio[i] = prio[k] + ops[k][3] - ops[i][3] + 1e-6
+        at = [0.0] * n
+        busy = {q: [] for q in "vatgsx"}
+        for i in sorted(range(n), key=lambda i: (-prio[i] - ops[i][3], i)):
+            r = max([at[j] + d for j, d in pre[i]] + [0.0])
+            c = ops[i][3]; b = busy[ops[i][0]]
+            lo = 0
+            while lo < len(b) and b[lo][1] <= r: lo += 1
+            while lo < len(b) and b[lo][0] < r + c - 1e-9:
+                r = max(r, b[lo][1]); lo += 1
+            at[i] = r
+            a = max(r - 1.0, b[lo - 1][1] if lo else 0.0) if ops[i][5] == "r" else r
+            b.insert(lo, (a, r + c))
+        MEMO["span"] = max(at[i] + ops[i][4] for i in range(n))
+        MEMO["order"] = sorted(range(n), key=lambda i: (at[i], i))
+    cnt = {}
+    ev = {}
+    know = {q: {} for q in Q}
+    for i in MEMO["order"]:
+        q, fn, pre, _c, _l, kind, sem = ops[i]
+        if kind == "x":
+            cnt[sem] = len(eng); ev[i] = (sem, len(eng), {})
+            continue
+        need = {}
+        for j, must in pre.items():
+            if not must or (q == "t" and ops[j][0] == q): continue
+            sm, c, kn = ev[j]
+            if need.get(sm, (0,))[0] < c: need[sm] = (c, kn)
+        for sm, (c, kn) in sorted(need.items(), key=lambda e: -len(e[1][1])):
+            if know[q].get(sm, 0) < c:
+                Q[q].wait_ge(T.sem[sm], c)
+                know[q][sm] = c
+                for k, x in kn.items():
+                    if know[q].get(k, 0) < x: know[q][k] = x
+        if kind == "r":
+            fn(); cnt["ls"] = cnt.get("ls", 0) + len(eng); ev[i] = ("ls", cnt["ls"], {})
+            continue
+        sem = SEM[q] if kind == "c" else sem
+        inc = 1 if kind == "c" else 16
+        fn().then_inc(T.sem[sem], inc)
+        cnt[sem] = cnt.get(sem, 0) + inc
+        ev[i] = (sem, cnt[sem], dict(know[q]))
     for sem, c in cnt.items():
-        if c:
-            g.wait_ge(T.sem[sem], c)
+        g.wait_ge(T.sem[sem], c)

@@ -10,8 +10,8 @@ TH = 4000
 H16, M26 = 65536.0, 2.0 ** 26
 NK = (14, 14, 4)
 CB = (0, 2, 6, 10, 14, 18, 22, 26, 28, 30, 31, 32)
-CG = (0, 6, 14, 22, 28, 31, 32)
-ZB = (4, 7, 3)
+CG = (0, 6, 14, 22, 26, 28, 30, 31, 32)
+YC = ((1, 0, 1280), (1, 1280, 2304), (1, 2304, 2944), (0, 2944, 3584), (0, 3584, 4096))
 SAMEQ = True
 
 COLS = {
@@ -26,8 +26,9 @@ COLS = {
     "hR": {0: H16, 12: -H16, 13: H16, 2: -H16, 6: -M26, 7: -M26, 14: -M26},
     "lL": {4: 64, 3: 1, 9: 1024}, "lR": {5: 64, 3: 1, 9: -1024},
     "mDe": {11: 1, 13: 1}, "r_s": {4: 1, 5: 1}, "r_n": {9: -1, 7: 1}, "q_c": {3: 1, 15: 1},
-    "i_k": {4: 1, 5: -1, 7: 1, 8: 2, 14: -2, 12: -256, 13: -256}, "i_la": {4: 1, 8: 1, 14: -1},
-    "i_one": {4: 1, 5: -2, 7: 3, 8: 4, 14: -3, 10: -256, 12: -256, 13: -256}, "i_na": {7: 2048},
+    "i_k": {4: 1, 5: -1, 7: 1, 8: 2, 14: -2, 12: -256, 13: -256}, "n_b": {4: -1, 5: 1, 7: -1, 12: 1, 13: 1}, "n_s": {5: 1, 7: -1},
+    "i_one": {4: 1, 5: -2, 7: 3, 8: 1, 10: -256, 12: -1, 13: -1}, "i_na": {7: 2048},
+    "m_d": {3: 1, 4: 1, 5: 1, 7: 1, 10: 1, 12: 256}, "m_l": {4: 1, 5: -1, 8: 1}, "m_e": {13: 256, 0: 1}, "m_r": {5: 1, 4: -1},
     "c_l": {4: -1, 6: 1, 8: -1, 14: 1, 12: 256, 13: 256}, "c_r": {5: -1, 7: 1, 8: 1, 14: -1, 10: 256, 11: 256},
 }
 for _k in ("L", "R"):
@@ -36,24 +37,24 @@ _to = {8: 12, 12: 8, 9: 10, 10: 9}
 COLS = {n: {_to.get(f, f): c for f, c in d.items()} for n, d in COLS.items()}
 CN = list(COLS)
 NE, NC_ = 4, len(CN)
-DN = ["i_k", "i_b", "i_as", "i_la", "i_j", "i_one", "i_na", "i_e", "c_l", "c_r"]
+DN = ["i_k", "i_b", "i_as", "i_la", "i_j", "i_one", "i_na", "i_e", "c_l", "c_r", "mix", "m_n"]
 
 SIZES = {"F": {}, "B": {}, "I": {}, "U": {}}
 def _a(ar, **kw):
     SIZES[ar].update(kw)
 _a("F", stat=16 + U, T1=16 + U + 256, T2=16 + U + 512, spos=U, numb=ZC + 16, cp2=672, YO=4096, op_=192, ot=192,
-   pcol=16, q14=144, g8=8, x144=144, pat=256, r16=272, sgm=256, rt=16 * NC_, seg=16 * NC_, cw=16 * NC_, sb=8,
-   idf=128, cdf=256, cdt=256, pm=4 * 128, gp=320, ks=768, red=8, rep=128, he=64, gid=128, m2=128, r2f=8, zs=8, mf=256,
+   pcol=16, g8=8, x144=144, pat=256, r16=272, sgm=256, rt=16 * NC_, seg=16 * NC_, cw=16 * NC_, sb=8,
+   idf=128, cdf=256, cdt=256, pm=4 * 128, gp=320, ks=768, zb=768, red=8, rep=128, he=64, gid=128, m2=128, r2f=8,
    jc=64, tq=4 * 80, best=4, wm=64, ones=128, ac0=64, cnt=2, j32=64, j256=64,
-   mm=64, ms=64, o1=64, val=64, sw=1184, Fs=256, F2=256, cap=256, U1=64, U5=64,
-   kw=16, kkw=16, pw=16, vq=4, vx=8, vm=4, cs=4, et=8, e80=8, e81=8, e82=8, c8=8, Lw=8, La2=4,
-   mo=64, ifl=256, dy2=128, cut=64,
+   mm=64, ms=64, o1=64, val=64, sw=1184, Fs=256, F2=256, cap=256, m64=256, U1=64, U5=64,
+   kkw=16, vq=4, vx=8, vm=4, cs=4, et=8, e80=8, e81=8, e82=8, c8=8, Lw=8, La2=4,
+   dy2=128, cut=64,
    wr=12, xa=4, xb=4, xc=4, xd=4, xe_=4, xf=4, xg=4, xh=4, xi=4, c21w=8, y1=68, xP=136, xt=136, xm=136, xu=136,
    c21=128, bc=16, fa=128, fb=128, fc=128, fd=128, ff=128, fg=128, fh=128, ga=64, gb=64, ge=64, gg=64,
    ha=64, hb=64, hf=64, hm=128, hn=128, hq=128, hr=128, C0=192, C1=192, C2=192)
-_a("B", xc_=16 + U + 512, xb_=ZC + 16, ad=U + 32, G=4096, MN=4096, XV=XVN + 16, bo=128, bo6=128, nb6=128, idb=128, nid=128, nM=128,
-   qz=144, q1=144, q16=144, dg=128 * len(DN), ds=3 * 128, pt=3 * 336, fR=128, fL=128, fZ=128, w0=320, w1=320, sm=320, wc=1536,
-   wf=16, wa=16, wh1=16, wh2=16, wz=16, zb=768, rs=3 * 128, R0=128, R1=128, R2=128, na=64,
+_a("B", xc_=16 + U + 512, xb_=ZC + 16, ad=U + 32, G=4096, MN=4096, XV=XVN + 16, bo=128, bo6=128, bom=128, mo=80, ifl=256, nb6=128,
+   idb=128, nid=128, qz=144, q1=144, q14=144, q16=144, dg=128 * len(DN), ds=3 * 128, pt=3 * 336, fR=128, fL=128, fZ=128,
+   w0=320, w1=320, sm=320, wc=1536, wf=16, wa=16, wh1=32, wh2=32, rs=3 * 128, R0=192, R1=192, R2=128, na=64,
    onb=128, jb=64, kb=256, eo0=128, eo1=256, eo2=256, el0=640, el1=640, el2=640, W=256, q_gn=64, g2=128, g2a=64,
    po0=NS, po1=NS, po2=256, mo0=128, mo1=128, mo2=128, dl0=192, dl1=192, dl2=192, ex=128, lr=64, c1b=64, cb=192, nad=272)
 _a("I", oc=168, cd=256, pi=4, mi=256, mj=256, ri=8, rj=8, Hi=64, vf=64, dm=64, g16=64, mu=64, hd=64, pl=64, d64=64,
@@ -73,15 +74,17 @@ SCRATCH = {"F": ("sbuf", [128, TOT["F"]], "float32"), "B": ("sbuf", [128, TOT["B
            "TT": ("sbuf", [128, 6, 32], "float32")}
 for _b in range(8):
     SCRATCH["P%d" % _b] = ("psum", [128, 512], "float32")
-SEMAPHORES = ["cv", "ca", "ct", "cg", "ls", "lx0", "lx1", "loc", "lcd", "so"] + ["ln%d" % k for k in range(8)] + \
+SEMAPHORES = ["cv", "ca", "ct", "cg", "ls", "lx0", "lx1", "loc", "lcd", "so", "lc"] + ["ln%d" % k for k in range(8)] + \
     ["%s%d" % (n, t) for n in ("ae", "ad", "ap") for t in range(RO)]
 
 MEMO = {}
-BOOST = {464: 0.5, 1071: 1.5, 453: -4, 897: 1.8, 851: 4, 1282: 2, 127: -0.2, 134: 0.3, 892: -1, 842: 4, 573: 0.5, 328: 4, 1304: 2, 118: -4,
-         1363: 4, 530: 1.8, 478: -4, 653: 0.5, 682: 2, 568: -0.2, 537: 2, 1226: -0.2, 482: -1, 900: 0.2, 931: -4, 699: -0.2, 1281: 2,
-         563: 8, 535: 0.2, 514: 0.2, 1083: 0.7, 711: 8, 715: 8, 712: -4, 9: 2, 850: -0.5, 678: -2, 847: -4, 957: -0.2, 1131: 8,
-         1050: -8, 267: 8, 1199: -4, 278: 16, 1217: -2, 270: 12, 1045: 4, 126: -0.5, 329: 16, 374: 0.5, 902: 0.5, 928: 0.5, 299: 2,
-         337: 3.5, 526: 0.5, 542: 1, 1302: -8, 1266: -8, 1303: -0.2, 277: 8, 279: 8, 280: 8, 281: 8, 283: 8, 373: 0.5, 138: -1.0}
+BOOST = {526: -8, 394: 2, 1087: 1, 882: 1, 614: -2, 575: 4, 695: -1, 696: -1, 697: -1, 698: -1, 699: -1, 700: -1, 701: -1, 702: -2,
+         1161: -0.5, 704: -0.2, 1132: -0.5, 158: 0.5, 173: 0.5, 180: 0.5, 580: -4, 386: 1, 261: 4, 126: -1, 383: 0.2, 946: -8, 344: 1,
+         951: -0.5, 893: 0.2, 924: -2, 82: 1.3, 913: -1, 887: -0.5, 870: -0.5, 947: -4, 298: 4, 299: 4, 300: 4, 301: 4, 302: 4, 303: 4,
+         304: 4, 318: -4, 588: -4, 554: 0.2, 581: -4, 9: -0.5, 674: 4, 1213: 1, 1212: 0.2, 658: 0.5, 662: 0.5, 666: 0.5, 670: 0.5,
+         862: 0.2, 753: 2, 841: -8, 945: 1, 790: 1, 848: 4, 872: 8, 825: -1, 830: -1, 840: -1, 873: 1, 894: -8, 974: 1, 282: -4,
+         313: -2, 624: 0.2, 625: 0.2, 673: 2, 843: 6, 84: -0.5, 1285: 2, 1204: -0.2, 1288: -8, 1290: -8, 1229: 0.5, 898: 0.2, 975: 2,
+         1202: 1, 877: 8, 821: 1.0}
 
 
 def rank_program(g, core, T, topo):
@@ -168,7 +171,7 @@ def rank_program(g, core, T, topo):
         if tag in last_: ops[i][2].setdefault(last_[tag], False)
         last_[tag] = i
 
-    CY, GA, SC = 0.00104, 1.56, 3.0
+    CY, GA, SC = 0.0008715, 1.5, 3.0
     def vc(o, ins, two=False):
         if len(o) > 2: return 0.05 + size(o) * SC * CY
         if any(len(x) > 2 for x in ins): return 0.05 + size(o) * GA * CY
@@ -189,12 +192,12 @@ def rank_program(g, core, T, topo):
             0.065 + size(i) * CY * (GA if len(i) > 2 else 1))
     def mm(o, l, rh, st, sp):
         add("t", lambda: g.tensor.matmul(o[0], l[0], rh[0], st, sp), [l, rh], [o],
-            max(64, size(rh)) * 0.55 * CY * (1 if l[1][0][0] == "B" else 4))
+            max(64, size(rh)) * CY * (1 if l[1][0][0] == "B" else 4))
     def io_(o, pat, base, cm=0):
         if o[1][0][0] == "I":
-            add("g", lambda: g.iota(o[0], pat, base, cm), [], [o], 0.16 + 2 * size(o) * CY)
+            add("g", lambda: g.iota(o[0], pat, base, cm), [], [o], 0.1344 + 2 * size(o) * CY)
         else:
-            add("g", lambda: g.iota(o[0], pat, base, cm, allow_small_or_imprecise_dtypes=True), [], [o], 0.16 + 2 * size(o) * CY)
+            add("g", lambda: g.iota(o[0], pat, base, cm, allow_small_or_imprecise_dtypes=True), [], [o], 0.1344 + 2 * size(o) * CY)
     def fill(o, c): io_(o, [[0, size(o)]], c)
     def dma(q, o, i, sem, lat, r=(), w=()):
         add(q, lambda: Q[q].dma_start(o, i), list(r), list(w), 0.05, lat, "d", sem)
@@ -204,7 +207,7 @@ def rank_program(g, core, T, topo):
     def send(dst, o, i, sem, first=False):
         rid, pid, _e = topo.addr(dst)
         j = add("g", lambda: g.remote_dma(o[0], i[0], T.sem[sem], T.sem.ls, pid, rid, emask), [i], [], 2.6 if first else 0.3,
-                3.9 if first else 1.6, "r", "ls")
+                4.3 if first else 2.0, "r", "ls")
         c = 0.5 + size(i) * 0.0026
         add("x", None, [], [o], c, c + 0.3, "x", sem, [j])
 
@@ -218,9 +221,9 @@ def rank_program(g, core, T, topo):
     def dl(t): return s("dl%d" % t, 64, 128)
 
     dma("s", s("oc")[0], T.oc[:], "loc", 2.2, w=[s("oc")]); seq("ld")
-    dma("a", s("xc_", 16, 16 + U // 2)[0], T.x[:, 0:U // 2], "lx0", 3.6, w=[s("xc_", 16, 16 + U // 2)])
-    dma("s", s("xc_", 16 + U // 2, 16 + U)[0], T.x[:, U // 2:U], "lx1", 4.2, w=[s("xc_", 16 + U // 2, 16 + U)]); seq("ld")
-    dma("s", s("cd")[0], T.cd[:], "lcd", 4.8, w=[s("cd")]); seq("ld")
+    dma("a", s("cd")[0], T.cd[:], "lcd", 2.5, w=[s("cd")]); seq("la")
+    dma("a", s("xc_", 16, 16 + U // 2)[0], T.x[:, 0:U // 2], "lx0", 4.0, w=[s("xc_", 16, 16 + U // 2)]); seq("la")
+    dma("s", s("xc_", 16 + U // 2, 16 + U)[0], T.x[:, U // 2:U], "lx1", 4.6, w=[s("xc_", 16 + U // 2, 16 + U)]); seq("ld")
 
     HW = 336
     ms(s("ones"), 1.0)
@@ -258,7 +261,7 @@ def rank_program(g, core, T, topo):
     ts(s("idb"), s("x144", 0, 128), pc, A.is_equal)
     t2(s("nid"), s("x144", 0, 128), pc, A.is_equal, -1.0, A.mult)
     cp(P(6, 0, 192), s("r16", 0, 192))
-    for a, b in ((0, NE), (NE, NE + 10), (NE + 10, NC_)):
+    for a, b in ((0, NE), (NE, NE + 12), (NE + 12, NC_)):
         tt(s("seg", 16 * a, 16 * b), P(6, 0, 16 * (b - a)), s("rt", 16 * a, 16 * b), A.mult)
         scan(s("cw", 16 * a, 16 * b), s("sgm", 0, 16 * (b - a)), s("seg", 16 * a, 16 * b), 0.0, A.mult, A.add)
     ms(s("fR"), 0.0); ms(s("fL"), 0.0); ms(s("fZ"), 0.0)
@@ -286,8 +289,11 @@ def rank_program(g, core, T, topo):
     send(victim(0), s("el0", 128, 256), s("eo0"), "ae0", True)
     for h in range(8):
         lo = max(HW * h, 1); hi = HW * h + HW; b = (0, 1, 4)[h % 3]
-        mm(P(b, 0, hi - lo), s("idb"), s("xb_", lo, hi), True, False)
-        mm(P(b, 0, hi - lo), s("nid"), s("xb_", lo - 1, hi - 1), False, True)
+        if h in (1, 3, 5):
+            tt(P(b, 0, hi - lo), s("xb_", lo, hi), s("xb_", lo - 1, hi - 1), A.subtract)
+        else:
+            mm(P(b, 0, hi - lo), s("idb"), s("xb_", lo, hi), True, False)
+            mm(P(b, 0, hi - lo), s("nid"), s("xb_", lo - 1, hi - 1), False, True)
         act(s("ad", 15 + lo, 15 + hi), P(b, 0, hi - lo), AF.Abs)
         lo = HW * h; b = (2, 3, 5)[h % 3]
         mm(P(b, 0, HW), s("fZ"), s("xb_", lo, hi), True, False)
@@ -303,9 +309,9 @@ def rank_program(g, core, T, topo):
             k = 2 * kh + j1
             add("g", lambda k=k, kh=kh, j1=j1: g.affine_select(
                 s("pm", 128 * k, 128 * k + 128)[0], s("ones")[0], [[32, 4], [1000 - 2000 * j1, 2], [2, 16]], A.is_equal, 0.0,
-                kh + 1000 * j1, -1), [s("ones")], [s("pm", 128 * k, 128 * k + 128)], 0.48)
+                kh + 1000 * j1, -1), [s("ones")], [s("pm", 128 * k, 128 * k + 128)], 0.4032)
     cp(s("cdf"), s("cd"))
-    add("v", lambda: V.transpose(s("cdt")[0], s("cdf")[0]), [s("cdf")], [s("cdt")], 0.27)
+    add("v", lambda: V.transpose(s("cdt")[0], s("cdf")[0]), [s("cdf")], [s("cdt")], 256 * CY)
     act(c3("TR", None, 0, 32), s("cdt"))
     for k in range(4):
         mm(P(7, 128 * (k // 2), 128 * (k // 2) + 128), s("pm", 128 * k, 128 * k + 128), c3("TR", None, 16 * (k % 2), 16 * (k % 2) + 16), k % 2 == 0, k % 2 == 1)
@@ -317,11 +323,13 @@ def rank_program(g, core, T, topo):
         act(s("wa", lr_, 16, 2), s("g8"), scale=cw(("aL", "aR")[lr_]))
         act(s("wh1", lr_, 16, 2), s("g8"), scale=cw(("hL", "hR")[lr_]))
         act(s("wh2", lr_, 16, 2), s("g8"), scale=col("cw", lr_))
-        act(s("wz", lr_, 16, 2), s("g8"), scale=col("r16", 4 + lr_))
+        act(s("wh1", 16 + lr_, 32, 2), s("g8"), scale=col("r16", 4 + lr_))
+        act(s("wh2", 16 + lr_, 32, 2), s("g8"), scale=col("r16", 4 + lr_))
     K0 = (0, NK[0], NK[0] + NK[1])
     for b in range(3):
         nk = NK[b]
         io_(s("wc", 512 * b, 512 * b + 16 * nk), [[0, 8], [1024, 2], [-2048, nk]], (31 - K0[b]) * 2048)
+        fill(s("wc", 512 * b + 16 * nk, 512 * b + 32 * nk), 0)
     for b in (0, 2):
         nk = NK[b]; a = 128 * b; e = a + 16 * nk
         io_(s("gp", a, e), [[1, 8], [0, 2 * nk]], 0)
@@ -329,14 +337,17 @@ def rank_program(g, core, T, topo):
         act(s("w1", a, e), s("w0", a, e), scale=-1.0 / H16)
         io_(s("sm", a, e), [[0, 8], [1, 2 * nk]], 0)
         act(s("sm", a, e), s("sm", a, e), AF.Sign)
-    act(s("onb"), s("ones")); act(s("idf"), s("idb")); act(s("nM"), s("idb"), scale=-M26)
+    act(s("onb"), s("ones")); act(s("idf"), s("idb"))
     io_(s("gid"), [[1, 8], [0, 16]], 0)
     ts(s("bo"), s("gid"), gc_, A.is_equal)
     act(s("bo6"), s("bo"), scale=1.0 / 64); act(s("nb6"), s("bo"), scale=-1.0 / 64)
-    for n, w, c in (("i_k", "idb", cw("i_k")), ("i_b", "nid", cw("i_k")), ("i_as", "idb", cw("ub1")), ("i_la", "idb", cw("i_la")),
-                    ("i_j", "idb", col("r16", 3)), ("i_one", "idb", cw("i_one")), ("i_na", "idb", cw("i_na")), ("i_e", "idb", col("r16", 13)),
-                    ("c_l", "idb", cw("c_l")), ("c_r", "idb", cw("c_r"))):
+    for n, w, c in (("i_k", "idb", cw("i_k")), ("i_b", "idb", cw("n_b")), ("i_as", "idb", cw("n_s")), ("i_la", "idb", col("r16", 4)),
+                    ("i_j", "idb", col("r16", 3)), ("i_one", "idb", cw("i_one")), ("i_na", "idb", cw("i_na")), ("i_e", "idb", col("r16", 0)),
+                    ("mix", "idb", cw("m_d")), ("m_n", "nid", cw("mDe")), ("c_l", "idb", cw("c_l")), ("c_r", "idb", cw("c_r"))):
         act(dg(n), s(w), scale=c)
+    for f, n in ((12, "m_l"), (13, "m_e"), (14, "m_r")):
+        act(s("dg", 128 * DN.index("mix") + f, 128 * DN.index("mix") + 128, 16), s("g8"), scale=cw(n))
+    act(s("bom"), s("bo"), scale=0.0); act(s("bom", 11, 128, 16), s("g8")); act(s("bom", 13, 128, 16), s("g8"))
     for k, c in enumerate((cw("r_s"), col("r16", 10), cw("r_n"))):
         act(s("rs", 128 * k, 128 * k + 128), s("bo"), scale=c)
     io_(s("xt", 0, 68), [[1, 17], [672, 4]], 21)
@@ -348,8 +359,8 @@ def rank_program(g, core, T, topo):
     io_(s("jb"), [[1, 64]], 0)
     fill(s("tq", 64, 320, 80), 32768)
     io_(s("kkw"), [[16, 16]], 0)
-    fill(s("XV", 16 * 116, XVN + 16), 0); fill(s("XV", 16 * 48, 16 * 68), 0); fill(s("lr"), 21)
-    for a in range(0, 1184, 296): fill(s("sw", a, a + 296), 0)
+    fill(s("XV", 16 * 116, XVN + 16), 0); fill(s("XV", 16 * 48, 16 * 68), 0); fill(s("lr"), 21); fill(s("mo", 64, 80), 100)
+    for a in range(0, 1184, 296): fill(s("sw", a, a + 296), 2 ** 23)
     io_(s("kb"), [[1, 256]], 0)
     io_(s("c21w"), [[21, 2], [672, 4]], 0)
     io_(s("xP", 0, 68), [[1, 17], [0, 4]], 0)
@@ -369,32 +380,33 @@ def rank_program(g, core, T, topo):
     act(s("vq"), s("x144", 0, 64, 16), bias=rc)
     act(s("xu"), s("xt"), bias=col("pcol", 7))
     act(s("kkw"), s("kkw"), bias=rc)
-    act(s("j32"), s("j32"), scale=32768.0, bias=-64.0)
+    act(s("j32"), s("j32"), scale=-32768.0, bias=63 * 32768.0)
     act(s("c8"), s("c8"), bias=rc)
-    act(s("kw"), s("kkw"), scale=64.0)
+    fill(s("m64"), -64)
     act(s("q1"), s("qz"), AF.Sign)
-    act(s("cap"), s("r16", 1, 257), scale=1e9)
+    act(s("cap"), s("r16", 1, 257), scale=-2e9, bias=1e9)
     act(s("q14"), s("q1"), scale=cw("q_c"))
     act(s("q16"), s("q1"), scale=1.0 / 16)
     act(s("c21w"), s("c21w"), bias=col("pcol", 7))
     tt(s("j256"), s("j256"), s("r16", 0, 64), A.mult)
     for k, (m, b) in enumerate(((1, 0), (1, U + NS - 1), (1, Z1 - 1), (4096, TH), (8192, 4096), (-2, -1))):
         act(s("bc", 2 * k, 2 * k + 2), s("kkw", 0, 2), scale=float(m), bias=float(b))
+    add("g", lambda: g.dma_start(s("ad", 16, 16 + U)[0], s("stat", 16, 16 + U)[0]), [s("stat", 16, 16 + U)], [s("ad", 16, 16 + U)], 1.5, 6.0, "d", "lc")
     for r in range(16):
-        mm(P(7, 0, 168), s("q14", 15 - r, 143 - r), s("stat", 16 + r, 16 + U, 16), r == 0, r == 15)
+        mm(P(7, 0, 168), s("q14", 15 - r, 143 - r), s("ad", 16 + r, 16 + U, 16), r == 0, r == 15)
     cp(s("cl"), P(7, 0, 168))
     fill(s("op_"), 0)
     for u in range(6): cp(s("op_", 32 * u, 32 * u + 28), s("oc", u, 168, 6))
     tt3 = (T.TT[:, :, :], [("TT", np.arange(192))])
-    add("v", lambda: V.transpose(s("ot")[0], s("op_")[0]), [s("op_")], [s("ot")], 0.2)
+    add("v", lambda: V.transpose(s("ot")[0], s("op_")[0]), [s("op_")], [s("ot")], 192 * CY)
     act(tt3, s("ot"))
 
     def unpack(t):
         for k in range(3 if t < RO - 1 else 2):
-            mm(P(7, 64 * k, 64 * k + 64), s("rs", 128 * k, 128 * k + 128), dl(t), True, True)
-        act(s("R%d" % t), P(7, 0, 128))
+            mm(P(4, 64 * k, 64 * k + 64), s("rs", 128 * k, 128 * k + 128), dl(t), True, True)
+        act(s("R%d" % t, 0, 128), P(4, 0, 128))
         if t < RO - 1:
-            act(s("na"), P(7, 128, 192), bias=1.0)
+            act(s("na"), P(4, 128, 192), bias=1.0)
 
     cp(P(5, 448, 512), s("jc"))
     for t in range(RO):
@@ -419,20 +431,19 @@ def rank_program(g, core, T, topo):
             lst = [("i_as", R(t - 1, 0)), ("i_la", s("lr") if t == 1 else s("cb", 128, 192)), ("i_j", s("jb")), ("i_one", s("onb", 0, 64)),
                    ("i_na", s("na")), ("i_b", R(t - 1, 2)), ("i_e", s("xb_", z0 + 272, z0 + 336))]
             for k, (w, x) in enumerate(lst):
-                mm(P(4, 0, 64), dg(w), x, k == 0, k == len(lst) - 1)
-            act(s("mo"), P(4, 0, 64))
+                mm(P(4, 192, 256), dg(w), x, k == 0, k == len(lst) - 1)
+            act(s("mo", 0, 64), P(4, 192, 256))
             act(s("ifl"), ind(s("mo"), s("wl_")))
-            mm(P(3, 0, 256), s("fZ"), s("xb_", z0, z0 + 256), True, False)
-            mm(P(3, 0, 256), dg("i_k"), s("kb"), False, False)
-            mm(P(3, 0, 256), s("fL"), s("nad", 0, 256), False, False)
-            mm(P(3, 0, 256), s("fR"), s("nad", 1, 257), False, False)
-            mm(P(3, 0, 256), s("idf"), s("ifl"), False, True)
-            act(s(tab, n0, n0 + 256), P(3, 0, 256))
+            mm(P(7, 256, 512), dg("i_k"), s("kb"), True, False)
+            mm(P(7, 256, 512), s("fZ"), s("xb_", z0, z0 + 256), False, False)
+            mm(P(7, 256, 512), s("fL"), s("nad", 0, 256), False, False)
+            mm(P(7, 256, 512), s("fR"), s("nad", 1, 257), False, False)
+            mm(P(7, 256, 512), dg("mix"), s("ifl"), False, True)
+            act(s(tab, n0, n0 + 256), P(7, 256, 512))
+            act(s("R%d" % (t - 1), 128, 192), R(t - 1, 2))
             for r in range(16):
-                mm(P(6, 256, 264), s("q16", 15 - r, 143 - r), s("R%d" % (t - 1), r, 128, 16), r == 0, r == 15)
-            for r in range(16):
-                mm(P(6, 264, 268), s("q16", 15 - r, 143 - r), s("dl%d" % (t - 1), 128 + r, 192, 16), r == 0, r == 15)
-            act(s("wr"), P(6, 256, 268))
+                mm(P(1, 256, 268), s("q16", 15 - r, 143 - r), s("R%d" % (t - 1), r, 192, 16), r == 0, r == 15)
+            act(s("wr"), P(1, 256, 268))
             act(s("xf"), s("wr", 4, 8), scale=-2.0, bias=1.0)
             tt(s("xc"), s("xa"), s("wr", 0, 4), A.add)
             tt(s("xd"), s("wr", 8, 12), s("xa"), A.subtract)
@@ -453,20 +464,19 @@ def rank_program(g, core, T, topo):
             act(s("XV", 16 * a, 16 * b), ind(s("xb_", 0, U + NS * t), s("l_xv", a, b))); seq("xv")
         for r in range(16):
             mm(P(6, 0, 8), s("qz", 15 - r, 143 - r), s(el, 128 + r, 256, 16), r == 0, r == 15)
-        act(s("zs"), P(6, 0, 8), bias=float(4096 - lim))
         for B in range(8):
-            act(s("mf", B, 256, 8), c3("CT", B, 0, 32), bias=col("zs", B))
+            t2(s("mi", B, 256, 8), c3("CT", B, 0, 32), P(6, B, B + 1), A.add, float(4096 - lim), A.add)
         for a, b in ((0, 48), (48, 256)):
-            cp(s("mi", a, b), s("mf", a, b))
             ts(s("mj", a, b), s("mi", a, b), 4095, A.bitwise_and)
             t2(s("ml", a, b), s("mj", a, b), float(4096 - lim - 16), A.subtract, 0.0, A.max)
         act(s(el, 256, 384), s(el, 128, 256)); act(s(el, 384, 640), s(el, 128, 384))
+        nn = 16 if t == 0 else 32
         for b in range(3):
             nk = NK[b]; o = 256 * (b // 2)
-            mm(P(b, 0, 16 * nk), row0("onb", 0, 128), row0("wc", 512 * b, 512 * b + 16 * nk), True, False)
+            mm(P(b, 0, nn * nk), row0("onb", 0, 128), row0("wc", 512 * b, 512 * b + nn * nk), True, False)
             mm(P(b, 0, 16 * nk), s(el, 128, 256), s("w0", o, o + 16 * nk), False, False)
             if t > 0:
-                mm(P(ZB[b], 0, 16 * nk), s(el, 0, 128), s("w1", o, o + 16 * nk), True, False)
+                mm(P(b, 16 * nk, 32 * nk), s(el, 0, 128), s("w1", o, o + 16 * nk), False, False)
         for c in range(len(CB) - 1):
             a, e = 128 * CB[c], 128 * CB[c + 1]
             tt(s("MN", a, e), ind(s("xc_", 0, 16 + lim), s("ml", a // 16, e // 16)), s(el, 128, 128 + e - a), A.min); seq("mn")
@@ -481,13 +491,13 @@ def rank_program(g, core, T, topo):
                 if t == 0:
                     mm(o, s("G", 128 * k, 128 * k + 128), s("wa"), False, last)
                 else:
-                    mm(P(ZB[b], k - K0[b], 16 * nk, nk), s("G", 128 * k, 128 * k + 128), s("wz"), False, last)
-                    mm(o, s("G", 128 * k, 128 * k + 128), s("wh%d" % t), False, False)
+                    mm(P(b, k - K0[b], 32 * nk, nk), s("G", 128 * k, 128 * k + 128), s("wh%d" % t), False, last)
                 if last:
                     o = 256 * (b // 2)
                     if t > 0:
-                        act(s("zb", 256 * b, 256 * b + 16 * nk), P(ZB[b], 0, 16 * nk), AF.Relu, bias=-31.0)
-                        mm(P(b, 0, 16 * nk), s("nM"), s("zb", 256 * b, 256 * b + 16 * nk), False, True)
+                        if b < 2: act(s("zb", 256 * b, 256 * b + 16 * nk), P(b, 16 * nk, 32 * nk), scale=-M26, bias=31.5 * M26)
+                        else: t2(s("zb", 256 * b, 256 * b + 16 * nk), P(b, 16 * nk, 32 * nk), -M26, A.mult, 31.5 * M26, A.add)
+                        tt(P(b, 0, 16 * nk), P(b, 0, 16 * nk), s("zb", 256 * b, 256 * b + 16 * nk), A.min)
                     scan(s("ks", 256 * b, 256 * b + 16 * nk), s("sm", o, o + 16 * nk), P(b, 0, 16 * nk), 0.0, A.mult, A.max)
                     if b == 1:
                         tt(s("red"), s("ks", 2 * nk - 1, 16 * nk, 2 * nk), s("ks", 256 + 2 * nk - 1, 256 + 16 * nk, 2 * nk), A.max)
@@ -499,7 +509,7 @@ def rank_program(g, core, T, topo):
         tt(s("ri"), s("red"), s("ks", 512 + 2 * nk - 1, 512 + 16 * nk, 2 * nk), A.max)
         ts(s("rj"), s("ri"), 0xFF07FF, A.bitwise_and)
         ts(s("rep"), ind(s("rj"), s("l_rep")), col("pcol", 5), A.add)
-        add("t", lambda: g.tensor.transpose(P(3, 0, 128)[0], s("rep")[0], s("idf")[0]), [s("rep"), s("idf")], [P(3, 0, 128)], 0.3)
+        add("t", lambda: g.tensor.transpose(P(3, 0, 128)[0], s("rep")[0], s("idf")[0]), [s("rep"), s("idf")], [P(3, 0, 128)], 512 * CY)
         cp(s("he"), P(3, 0, 128, 2))
         tt(s("Hi"), P(3, 1, 128, 2), s("he"), A.max)
         Hi = s("Hi")
@@ -532,21 +542,25 @@ def rank_program(g, core, T, topo):
             act(s("g2a"), P(6, 64, 128), AF.Abs)
             mm(P(6, 128, 192), s("bo"), s("g2a"), True, False)
             mm(P(6, 128, 192), s("nid"), s("q_gn"), False, True)
-            if t == 1: act(s("U5"), P(6, 128, 192), scale=cw("mDe"))
+            if t == 1:
+                mm(P(3, 128, 192), s("bom"), s("g2a"), True, False)
+                mm(P(3, 128, 192), dg("m_n"), s("q_gn"), False, True)
             act(s(po, 272, 336), P(6, 128, 192))
         t2(s("U1"), s("mu"), cw("ua1"), A.mult, cw("ub1"), A.add)
         t2(P(5, 192, 256), s("mu"), cw("ua2"), A.mult, cw("ub2"), A.add)
         tt(P(5, 192, 256), P(5, 192, 256), s("hd"), A.mult)
-        if t == 1: tt(P(5, 192, 256), P(5, 192, 256), s("U5"), A.add)
         tt(s("U1"), P(5, 192, 256), s("U1"), A.add)
+        if t == 1: tt(s("U1"), P(3, 128, 192), s("U1"), A.add)
         tt(s("wm"), P(4, 0, 64), s("mu"), A.mult)
-        scan(P(5, 256, 320), P(4, 0, 64), s("wm"), 0.0, A.add, A.add)
+        ts(s("U5"), s("mu"), 2048.0, A.add)
+        tt(s("o1"), P(4, 0, 64), s("U5"), A.mult)
+        scan(P(5, 256, 320), P(4, 0, 64), s("wm"), 2048.0, A.add, A.add)
         tt(P(5, 192, 256), P(4, 0, 64), s("U1"), A.mult)
-        ts(s("ac0"), P(5, 256, 320), 256.5, A.is_lt)
+        ts(s("ac0"), P(5, 256, 320), 2304.5, A.is_lt)
         mo = "mo%d" % t
         tt(s(mo, 0, 64), P(5, 192, 256), s("ac0"), A.mult)
-        tt(P(5, 320, 384), P(5, 256, 320), s("mu"), A.subtract)
-        ts(s(mo, 64, 128), P(5, 320, 384), 256.0, A.min)
+        tt(P(5, 384, 448), P(5, 256, 320), s("o1"), A.subtract)
+        ts(s(mo, 64, 128), P(5, 384, 448), 256.0, A.min)
         send(attacker(t), s("dl%d" % t, 64, 192), s(mo), "ad%d" % t)
         e8 = "e8%d" % t
         cp(s("bi"), s("best"))
@@ -571,39 +585,34 @@ def rank_program(g, core, T, topo):
             tt(s("Lw", 0, 4), s("cs"), s("xc"), A.add)
             tt(s(eo, 0, 128), ind(s("Lw"), s("l_r2")), s("m2"), A.mult)
             send(victim(t + 1), s("el%d" % (t + 1), 0, 256), s(eo), "ae%d" % (t + 1))
-        t2(s("o1"), P(4, 0, 64), -2048.0, A.mult, 2048.0, A.add)
-        tt(P(5, 128, 192), P(5, 128, 192), s("j32"), A.add)
-        tt(P(5, 384, 448), P(5, 320, 384), s("o1"), A.add)
+        tt(s("val"), P(5, 128, 192), s("j32"), A.add)
         tt(s("mm"), P(5, 384, 448), s("j256"), A.min)
         scan(s("ms"), s("sgm", 0, 64), s("mm"), 0.0, A.mult, A.add)
         cp(s("l_off"), s("ms", 15, 64, 16))
-        ts(s("val"), P(5, 320, 384), 64.0, A.mult)
-        tt(s("val"), P(5, 128, 192), s("val"), A.add)
         cp(ind(s("sw"), s("l_off")), s("val"))
-        scan(s("Fs"), s("sw", 1, 257), s("sw", 1, 257), 0.0, A.max, A.max)
-        scan(s("F2"), s("Fs"), s("cap"), 1e9, A.min, A.max)
-        tt(s("Fw"), s("F2", 14, 256, 16), s("F2", 15, 256, 16), A.min)
+        scan(s("Fs"), s("m64"), s("sw", 1, 257), 63 * 32768.0 + 20000, A.add, A.min)
+        scan(s("F2"), s("Fs"), s("cap"), -1e9, A.max, A.min)
+        tt(s("Fw"), s("F2", 14, 256, 16), s("F2", 15, 256, 16), A.max)
         ts(s("cc"), s("Fw"), 32767, A.bitwise_and)
-        tt(s("pw"), s("cc"), s("kw"), A.subtract)
-        t2(s("l_pos"), s("pw"), 0.0, A.max, float(XVN - 1), A.min)
+        ts(s("l_pos"), s("cc"), float(XVN - 1), A.min)
         act(s(po, 0, 256), ind(s("XV", 0, XVN), s("l_pos")))
         if t < RO - 1:
-            ts(s("ww"), s("Fw"), 15, A.logical_shift_right)
-            cp(s(po, 256, 272), s("ww"))
-            fill(s("sw", 0, 272), 0)
+            ts(s("ww"), s("Fw"), 15, A.arith_shift_right)
+            t2(s(po, 256, 272), s("ww"), -1.0, A.mult, 63.0, A.add)
+            fill(s("sw", 0, 272), 2 ** 23)
         send(attacker(t), s("xb_", U + NS * t, U + NS * t + NS) if t < RO - 1 else s("xb_", Z1, ZC), s(po), "ap%d" % t)
         tt(s("ex"), ind(s(e8), s("l_rep")), s("r16", 0, 128), A.mult)
-        mm(P(7, 320, 384), s("idb"), s("lr") if t < 2 else s("cb", 128, 192), True, False)
-        if t > 0: mm(P(7, 320, 384), s("idb"), R(t - 1, 0), False, False)
-        mm(P(7, 320, 384), s("nb6"), s("ex", 0, 64), False, False)
-        mm(P(7, 320, 384), s("nb6"), s("ex", 64, 128), False, True)
-        mm(P(7, 192, 320), s("bo6"), s("ex"), True, True)
-        act(s("C%d" % t), P(7, 192, 384))
+        mm(P(2, 320, 384), s("idb"), s("lr") if t < 2 else s("cb", 128, 192), True, False)
+        if t > 0: mm(P(2, 320, 384), s("idb"), R(t - 1, 0), False, False)
+        mm(P(2, 320, 384), s("nb6"), s("ex", 0, 64), False, False)
+        mm(P(2, 320, 384), s("nb6"), s("ex", 64, 128), False, True)
+        mm(P(2, 192, 320), s("bo6"), s("ex"), True, True)
+        act(s("C%d" % t), P(2, 192, 384))
         if t == 0:
-            act(s("cb"), P(7, 192, 384))
-            mm(P(7, 384, 448), dg("c_l"), s("cb", 0, 64), True, False)
-            mm(P(7, 384, 448), dg("c_r"), s("cb", 64, 128), False, True)
-            act(s("cut"), P(7, 384, 448))
+            act(s("cb"), P(2, 192, 384))
+            mm(P(2, 384, 448), dg("c_l"), s("cb", 0, 64), True, False)
+            mm(P(2, 384, 448), dg("c_r"), s("cb", 64, 128), False, True)
+            act(s("cut"), P(2, 384, 448))
             act(s("La2"), s("Lw", 0, 4))
             act(s("xb"), s(e8, 0, 4), scale=1.0 / 64)
             tt(s("xb"), s("xb"), s("c21w", 4, 8), A.add)
@@ -667,23 +676,20 @@ def rank_program(g, core, T, topo):
     for ih in range(2):
         ts(s("l_f", ih, 256, 4), p5(256, ih), float(ZC), A.min)
     o = OFF["YO"][1]
-    cuts = (0, 1280, 2560, 3584, 4096)
-    for c in range(4):
-        a, b = cuts[c], cuts[c + 1]
-        act(s("YO", a, b), ind(s("numb"), s("l_f", a // 16, b // 16))); seq("yo")
-        cp(s("G", a, b), ind(s("xb_"), s("l_f", a // 16, b // 16))); seq("y")
-        dma("s", T.y[:, a:b], s("G", a, b)[0], "so", 1.9 + (b - a) / 1500, r=[s("G", a, b)])
-        if c == 2:
-            dma("s", T.yo[:, 0:b], T.F[0:128:16, o:o + b], "so", 2.5, r=[s("YO", 0, b)])
-    dma("a", T.yo[:, a:b], T.F[0:128:16, o + a:o + b], "so", 2.0, r=[s("YO", a, b)])
+    for f, a, b in ((act, 0, 1024), (act, 1024, 2048), (act, 2048, 3072), (cp, 3072, 4096)):
+        f(s("YO", a, b), ind(s("numb"), s("l_f", a // 16, b // 16)))
+    dma("s", T.yo[:, :], T.F[0:128:16, o:o + 4096], "so", 2.5, r=[s("YO")])
+    for f, a, b in YC:
+        (cp if f else act)(s("G", a, b), ind(s("xb_"), s("l_f", a // 16, b // 16)))
+        dma("s" if f else "a", T.y[:, a:b], s("G", a, b)[0], "so", 1.9 + (b - a) / 1500, r=[s("G", a, b)])
 
     n = len(ops)
     if "order" not in MEMO:
         def gap(j, i):
             if not ops[i][2][j]: return ops[j][3]
             if ops[j][0] == ops[i][0] and ops[j][5] == "c":
-                return ops[j][4] + (0.0 if ops[i][0] == "t" else 0.03)
-            return ops[j][4] + (0.0 if ops[i][5] == "x" else 0.06)
+                return ops[j][4] + (0.0 if ops[i][0] == "t" else 0.07)
+            return ops[j][4] + (0.0 if ops[i][5] == "x" else 0.12)
         pre = [[(j, gap(j, i)) for j in o[2]] for i, o in enumerate(ops)]
         suc = [[] for _ in range(n)]
         for i in range(n):

@@ -11,8 +11,8 @@ H16, M26 = 65536.0, 2.0 ** 26
 NK = (14, 14, 4)
 CB = (0, 2, 6, 10, 14, 18, 22, 26, 28, 30, 31, 32)
 CG = (0, 6, 14, 22, 26, 28, 30, 31, 32)
-YC = ((1, 0, 1280), (1, 1280, 2304), (1, 2304, 2944), (0, 2944, 3584), (0, 3584, 4096))
-SAMEQ = True
+YC = ((1, 0, 1280), (1, 1280, 2304), (1, 2304, 2816), (1, 2816, 3072), (0, 3072, 3712), (0, 3712, 4096))
+ZB = (4, 6, 3)
 
 COLS = {
     "s_i": {4: 1, 5: -1, 6: -1, 7: 1, 8: 2, 14: -2, 10: 256, 11: 256, 12: -256, 13: -256},
@@ -29,6 +29,7 @@ COLS = {
     "i_k": {4: 1, 5: -1, 7: 1, 8: 2, 14: -2, 12: -256, 13: -256}, "n_b": {4: -1, 5: 1, 7: -1, 12: 1, 13: 1}, "n_s": {5: 1, 7: -1},
     "i_one": {4: 1, 5: -2, 7: 3, 8: 1, 10: -256, 12: -1, 13: -1}, "i_na": {7: 2048},
     "m_d": {3: 1, 4: 1, 5: 1, 7: 1, 10: 1, 12: 256}, "m_l": {4: 1, 5: -1, 8: 1}, "m_e": {13: 256, 0: 1}, "m_r": {5: 1, 4: -1},
+    "d_l": {1: 1, 10: -1, 11: 1, 8: -256}, "d_r": {0: 1, 12: -1, 13: 1, 14: -256},
     "c_l": {4: -1, 6: 1, 8: -1, 14: 1, 12: 256, 13: 256}, "c_r": {5: -1, 7: 1, 8: 1, 14: -1, 10: 256, 11: 256},
 }
 for _k in ("L", "R"):
@@ -37,29 +38,29 @@ _to = {8: 12, 12: 8, 9: 10, 10: 9}
 COLS = {n: {_to.get(f, f): c for f, c in d.items()} for n, d in COLS.items()}
 CN = list(COLS)
 NE, NC_ = 4, len(CN)
-DN = ["i_k", "i_b", "i_as", "i_la", "i_j", "i_one", "i_na", "i_e", "c_l", "c_r", "mix", "m_n"]
+DN = ["i_k", "i_b", "i_as", "i_la", "i_j", "i_one", "i_na", "i_e", "c_l", "c_r", "mix", "m_n", "m_p", "d_l", "d_r", "e_1"]
 
 SIZES = {"F": {}, "B": {}, "I": {}, "U": {}}
 def _a(ar, **kw):
     SIZES[ar].update(kw)
 _a("F", stat=16 + U, T1=16 + U + 256, T2=16 + U + 512, spos=U, numb=ZC + 16, cp2=672, YO=4096, op_=192, ot=192,
    pcol=16, g8=8, x144=144, pat=256, r16=272, sgm=256, rt=16 * NC_, seg=16 * NC_, cw=16 * NC_, sb=8,
-   idf=128, cdf=256, cdt=256, pm=4 * 128, gp=320, ks=768, zb=768, red=8, rep=128, he=64, gid=128, m2=128, r2f=8,
+   idf=128, cdf=256, cdt=256, pm=4 * 128, gp=320, ks=768, red=8, rep=128, he=64, gid=128,
    jc=64, tq=4 * 80, best=4, wm=64, ones=128, ac0=64, cnt=2, j32=64, j256=64,
    mm=64, ms=64, o1=64, val=64, sw=1184, Fs=256, F2=256, cap=256, m64=256, U1=64, U5=64,
-   kkw=16, vq=4, vx=8, vm=4, cs=4, et=8, e80=8, e81=8, e82=8, c8=8, Lw=8, La2=4,
+   kkw=16, vq=4, vx=8, vm=4, cs=4, et=8, e80=8, e81=8, e82=8, c8=8, La2=4,
    dy2=128, cut=64,
-   wr=12, xa=4, xb=4, xc=4, xd=4, xe_=4, xf=4, xg=4, xh=4, xi=4, c21w=8, y1=68, xP=136, xt=136, xm=136, xu=136,
-   c21=128, bc=16, fa=128, fb=128, fc=128, fd=128, ff=128, fg=128, fh=128, ga=64, gb=64, ge=64, gg=64,
-   ha=64, hb=64, hf=64, hm=128, hn=128, hq=128, hr=128, C0=192, C1=192, C2=192)
-_a("B", xc_=16 + U + 512, xb_=ZC + 16, ad=U + 32, G=4096, MN=4096, XV=XVN + 16, bo=128, bo6=128, bom=128, mo=80, ifl=256, nb6=128,
+   wr=12, xb=4, xd=4, xe_=4, xf=4, xh=4, xi=4, c21w=8, y1=68, xP=136, xt=136, xm=136, xu=136,
+   c21=128, bc=16, fa=128, fb=128, fc=128, fd=128, ff=128, fg=128, fh=128, fj=128, fk=128, fe=128, ga=64, gb=64,
+   ha=64, hb=64, hf=64, hn=128, hq=128, hr=128, C0=192, C1=192, C2=192)
+_a("B", xc_=16 + U + 512, xb_=ZC + 16, ad=U + 32, G=4096, MN=4096, XV=XVN + 16, bo=128, bo6=128, g8n=8, mo=80, ifl=256, nb6=128,
    idb=128, nid=128, qz=144, q1=144, q14=144, q16=144, dg=128 * len(DN), ds=3 * 128, pt=3 * 336, fR=128, fL=128, fZ=128,
-   w0=320, w1=320, sm=320, wc=1536, wf=16, wa=16, wh1=32, wh2=32, rs=3 * 128, R0=192, R1=192, R2=128, na=64,
+   w0=320, w1=320, sm=320, wc=1536, wf=16, wa=16, wh1=16, wh2=16, wz=16, zb=768, nM=128, rs=3 * 128, R0=192, R1=192, na=64,
    onb=128, jb=64, kb=256, eo0=128, eo1=256, eo2=256, el0=640, el1=640, el2=640, W=256, q_gn=64, g2=128, g2a=64,
-   po0=NS, po1=NS, po2=256, mo0=128, mo1=128, mo2=128, dl0=192, dl1=192, dl2=192, ex=128, lr=64, c1b=64, cb=192, nad=272)
-_a("I", oc=168, cd=256, pi=4, mi=256, mj=256, ri=8, rj=8, Hi=64, vf=64, dm=64, g16=64, mu=64, hd=64, pl=64, d64=64,
+   po0=NS, po1=272, po2=256, mo0=128, mo1=128, mo2=128, dl0=192, dl1=192, dl2=192, ex=128, lr=64, xa=12, c1b=64, cb=192, nad=272)
+_a("I", oc=168, cd=256, pi=4, mi=256, mj=256, ri=8, rj=8, rk=8, Hi=64, vf=64, dm=64, g16=64, mu=64, hd=64, pl=64, d64=64,
    Fw=16, cc=16, ww=16, bi=4, bx=4, bm=4, bd=4, e8i=8)
-_a("U", ocu=168, cl=168, ml=256, l_rep=8, l_r2=8, l_p0=8, l_off=4, l_pos=16, wl_=16, l_end=8, l_xv=136, l_f=256)
+_a("U", ocu=168, cl=168, ml=256, l_rep=8, l_p0=8, l_off=4, l_pos=16, wl_=16, l_end=8, l_xv=136, l_f=256)
 OFF = {}
 TOT = {}
 for _ar, _d in SIZES.items():
@@ -78,13 +79,29 @@ SEMAPHORES = ["cv", "ca", "ct", "cg", "ls", "lx0", "lx1", "loc", "lcd", "so", "l
     ["%s%d" % (n, t) for n in ("ae", "ad", "ap") for t in range(RO)]
 
 MEMO = {}
-BOOST = {526: -8, 394: 2, 1087: 1, 882: 1, 614: -2, 575: 4, 695: -1, 696: -1, 697: -1, 698: -1, 699: -1, 700: -1, 701: -1, 702: -2,
-         1161: -0.5, 704: -0.2, 1132: -0.5, 158: 0.5, 173: 0.5, 180: 0.5, 580: -4, 386: 1, 261: 4, 126: -1, 383: 0.2, 946: -8, 344: 1,
-         951: -0.5, 893: 0.2, 924: -2, 82: 1.3, 913: -1, 887: -0.5, 870: -0.5, 947: -4, 298: 4, 299: 4, 300: 4, 301: 4, 302: 4, 303: 4,
-         304: 4, 318: -4, 588: -4, 554: 0.2, 581: -4, 9: -0.5, 674: 4, 1213: 1, 1212: 0.2, 658: 0.5, 662: 0.5, 666: 0.5, 670: 0.5,
-         862: 0.2, 753: 2, 841: -8, 945: 1, 790: 1, 848: 4, 872: 8, 825: -1, 830: -1, 840: -1, 873: 1, 894: -8, 974: 1, 282: -4,
-         313: -2, 624: 0.2, 625: 0.2, 673: 2, 843: 6, 84: -0.5, 1285: 2, 1204: -0.2, 1288: -8, 1290: -8, 1229: 0.5, 898: 0.2, 975: 2,
-         1202: 1, 877: 8, 821: 1.0}
+DIGITS = "0123456789abcdefghijklmnopqrstuvwxyzABCDEFGHIJKLMNOPQRSTUVWXYZ"
+ORDER = (
+    "00010409020305060k0e080d0n1y0j0M0m1A0U1R160A0W1z0V0o121a1007140Z0u0g0G0b151W0J1g0r1h0H1i110Y18171j0S0y0I1l0E0p1b1n0a0h0s1d0l1k0f0z0t"
+    "1T1f1r130X0B1o0x1S0q391U1e1P0v1p0Q0C0i1c1m1B1s1D0c1V1F0w1t1C1q1E1J0F1w1H1Q1I1x1G3c1X1Y1K3J1L1M3z221Z27282a3b1O2e2f292h3y3d2n202g2b4o"
+    "2c1N3G2q2u3B2d2i2j3e2o0N3H213E2l2x2v2D2k2E3a2p2G3A2m23242r2w2s252K2L2t2y3C2T192F2z2B2U2N2A2H2I0L3t300T2M312C2W0K3f2O2P2J4M3g4l3L334j"
+    "2R3o523h2Q4m3i3O2V3j4u0O5L0D2S3K2X322Y6l4i260P0R2Z344w356n3M1u6p3X37563s4v4c365R5S5T5U5V5W5X5Y5Z3U6061626364653x4h1v666q3I6o3k6m384x"
+    "3l53594G6j3F6a4L6b69674t68586e6c5k6d3p6k6f6h6g4d6i3u3v6s6r6x6t4n4r6H6G6u6v6w6y6z6A6B6C6D6E6F576Q6I4s714k706J6K6L6M6N5C6O6P6R6S6T6U6V"
+    "6W6X6Y4S7a727k4y737j7475767778797b7c7d7e7f7g7h7i4q7u7t7l7m7n7o7p7C7q7r7s7B7v7w7x4V7y7I7H7M7D7E7F7L7G7J5a7K6Z3T7N7O7z4W5l555m5n3Y7P5o"
+    "7A5D5p3W7Y5q5E5r7Z3S5s5F5t803nbv3m9w4U3Z5u5G5v5d3r813P3q3V5M5w5I3w5x825y5N5H5z835A864z8t844Q85878w4T895O888e8o8P8L8f8a8j8g8p5P8b8k8q"
+    "4B8u8l8c8r8h4O8m8d8M5Q4D8K8i8v8n8s8N4P8x8O4N8Q8y8R8S408V8T5c8z8W488U478B4e9g8A8X9f4g9h8Z8C8D4X9i919j4f8E8F93499k3D908G9l3R4H8H968I45"
+    "9m9s925b9n949o8J959q979p989r994A9a9v9K8Y3Q9t9e9b3N5J9x9y9z4Y9c5B9d9L9Aa95K9B9M9Q9J9R9Saf9C7Q9T7R7S7T7U9U4R7V7W467Xagah4aaiajakal9Eam"
+    "anaoapaqarasat9F50au9Navawa0a1a2a3a49uaya5ax9Gft9HaDaAbyaIaEaQ4pazaCaM4EaF9OaS4KaBaJ4CaNaR9D4baP51fwaHaT9XaL9Wfu9Y9PaKaafva64F9Za79V"
+    "abac4Jb1a8aUb2b3b4b5b64Ib7b8b9babbbc4ZbdbebfaObgbDbtadbhbibw9IbjbzbkbublbmbBbnbCbxboaebpbAbqbraGbFbsbEbMbGc0bIbHbKbObRbUbXbJbZbLbNbP"
+    "bQbSbTbVbWbYcdc1cuc3c4c6c2c5c7c9caccctc8cbcfcecgciclcochcjckcmcncpaVcHcvcVcwczcCcFcJcMcPcScxcycAcBcDcEcUcGcIcKcLcNd9cOcQcRcTcXd0d3d6"
+    "dld8dbdecWcYcZd1d2d4cqd5d7dkdndqdadcdtdddfcrdsdydmdodvdxdpdgdrdudwdAcs54dzdCdBdhaW42hh44didD43dEdjaXfjdFfkdGdIdHdJdV41dKdL5f5edW5hdM"
+    "5idX5gdNdYdZe0eokLene1lje8dOe3dP5je2eieddQe4eje9exeeaYe5eadRefdSdTe6eteuekdUfVebege7eleseceyehewemeDevezeqlkeCeAlieEeFaZeBeJeHeGeKeI"
+    "f3epf4eLerf5f2b0eNf6ePf7eQf8ffeRf9eSfaeOfdfbeUeTeWfcfeeVeXeYeMfifgeZllflfmf0fnf1fofpfqfxfCg1fDfEfyfFfsg2g3g4g5g6g7log8g9gagblpgchngd"
+    "gelsgfggghgilrfzfhfGgjgkfMgCfNfOgmfPfQfRgFfShkgnglgogpgqgugyfAgrgvfrgBgwgzgAfWgDgtfJfHfKfIfBgxfLgsfTgNhfgOgPgQgRgSgTfUgUgVgWgXgYgZgG"
+    "h0h1h2hofXgEfYh4h6hgh8fZh3hahih7hlh9g0h5hphjhbhmlmhchdkPhrkQhehqhyhshMhuhvhxhthwhAhDhGhLhJhzhBhChEhFhHhIhKhZhNighPhQhShThVhOhRhWhYif"
+    "hUhXi1i4i0i2i3i5i6i8i9ibi7iaitihiHijikiminipiqisiiilioiGiriviyiBiEiuiwixiziAiCiDiViFiJiMiPiSiUj7iIiKiLiNiOiQiRiTiXj6j0iciWiYiZj1j9jc"
+    "jfjeidjkj8jajbjjjdjhjgj2jiiejmjljngHjoj3kMgIltjpj4gJjqj5kFjrkGjsjtkNgKlCjulykRjvjwjWgLjzjxjyk6jAjMjYjBjCjHjNjDjRjOgMjIjSjZjEjJjPjTjF"
+    "jKjUk0jGjLjQk2jVjXkOk1kgkTk3k5kSk7k4kUk8k9kVkckakWkhkdkXkbkskjkikekYktknkrkklnkulxlqkvlvlzkwklkpkxkokmlukylAkzkqlwlDkAkEkfkBlBlEkZkH"
+    "kIkJlHl0l1l2lIl3kKkClFlJlGl5lKl6l4l9lLl7l8lOlPlMlalNlblclUlQlRlSlVldlWlXlYlTlem0lZlfm1lglhm3m2kDm7m6m9m5mhmbmam4mdmcmimjmfm8memgmk")
 
 
 def rank_program(g, core, T, topo):
@@ -97,7 +114,6 @@ def rank_program(g, core, T, topo):
     ops = []
     lw, lr = {}, {}
     bank = {}
-    last_ = {}
 
     def width(n):
         w = 1
@@ -110,9 +126,10 @@ def rank_program(g, core, T, topo):
         b = z if b is None else b
         x = T[ar][:, o + a:o + b] if st == 1 else T[ar][:, o + a:o + b:st]
         return (x, [(ar, np.arange(o + a, o + b, st))])
-    def row0(n, a, b):
+    def row0(n, a, b, st=1):
         ar, o, z = OFF[n]
-        return (T[ar][0:1, o + a:o + b], [(ar, np.arange(o + a, o + b))])
+        x = T[ar][0:1, o + a:o + b] if st == 1 else T[ar][0:1, o + a:o + b:st]
+        return (x, [(ar, np.arange(o + a, o + b, st))])
     def col(n, j): return s(n, j, j + 1)
     def P(b, a=0, e=512, st=1):
         n = "P%d" % b
@@ -124,11 +141,10 @@ def rank_program(g, core, T, topo):
         return (T[n][:, i, a:b], [(n, ids[i, a:b])])
     def ind(w, off): return (w[0].indirect(off[0]), w[1], off[1])
     def ap(x): return x[0] if isinstance(x, tuple) else x
-    def size(x): return 16 * len(x[2][0][1]) if len(x) > 2 else len(x[1][0][1])
 
-    def add(q, fn, r, w, cost, lat=None, kind="c", sem=None, after=()):
+    def add(q, fn, r, w, kind="c", sem=None):
         i = len(ops)
-        pre = {}
+        pre = set()
         rd = []
         for x in r:
             if isinstance(x, tuple):
@@ -141,19 +157,17 @@ def rank_program(g, core, T, topo):
             if n not in lw:
                 lw[n] = np.full(width(n), -1); lr[n] = {}
         for n, c in rd + wt:
-            for j in np.unique(lw[n][c]):
-                if j >= 0: pre[int(j)] = True
+            pre.update(int(j) for j in np.unique(lw[n][c]) if j >= 0)
         for n, c in wt:
-            for j, a in lr[n].items():
-                if a[c].any(): pre[j] = pre.get(j, False) or ops[j][0] != q or ops[j][5] != "c" or kind != "c" or SAMEQ
+            pre.update(j for j, a in lr[n].items() if a[c].any())
         for n, c in rd + wt:
             if n[0] == "P":
                 for k, js in bank.setdefault(n, {}).items():
                     if k != q or q == "t":
-                        for j in js: pre[j] = True
+                        pre.update(js)
         for n, c in rd + wt:
             if n[0] == "P":
-                bank[n] = {"t": [i]} if q == "t" else {q: bank[n].get(q, []) + [i]}
+                bank[n] = {"t": [i]} if q == "t" else dict(bank[n], **{q: bank[n].get(q, []) + [i]})
         for n, c in wt:
             lw[n][c] = i
             for j in list(lr[n]):
@@ -162,54 +176,34 @@ def rank_program(g, core, T, topo):
         for n, c in rd:
             if i not in lr[n]: lr[n][i] = np.zeros(width(n), bool)
             lr[n][i][c] = True
-        for j in after: pre[j] = True
-        pre.pop(i, None)
-        ops.append([q, fn, pre, cost, cost if lat is None else lat, kind, sem])
-        return i
-    def seq(tag):
-        i = len(ops) - 1
-        if tag in last_: ops[i][2].setdefault(last_[tag], False)
-        last_[tag] = i
+        pre.discard(i)
+        ops.append([q, fn, sorted(pre), kind, sem])
 
-    CY, GA, SC = 0.0008715, 1.5, 3.0
-    def vc(o, ins, two=False):
-        if len(o) > 2: return 0.05 + size(o) * SC * CY
-        if any(len(x) > 2 for x in ins): return 0.05 + size(o) * GA * CY
-        n = size(ins[0]) if ins else size(o)
-        if two and not any(x[1][0][0][0] == "P" for x in ins): n *= 2
-        elif all(x[1][0][0] in ("B", "U") for x in [o] + ins): n /= 2
-        return max(64, n) * CY
     V = g.vector
-    def cp(o, i): add("v", lambda: V.tensor_copy(o[0], i[0]), [i], [o], vc(o, [i]))
-    def tt(o, a, b, f): add("v", lambda: V.tensor_tensor(o[0], a[0], b[0], f), [a, b], [o], vc(o, [a, b], True))
-    def ts(o, a, s1, f): add("v", lambda: V.tensor_scalar(o[0], a[0], ap(s1), None, f), [a, s1], [o], vc(o, [a]))
-    def t2(o, a, s1, f, s2, f2): add("v", lambda: V.tensor_scalar(o[0], a[0], ap(s1), ap(s2), f, f2), [a, s1, s2], [o], vc(o, [a]))
-    def red(o, a, f): add("v", lambda: V.tensor_reduce(o[0], a[0], AxisListType.X, f), [a], [o], max(64, size(a)) * CY)
-    def scan(o, a, b, ini, f, f2): add("v", lambda: V.tensor_tensor_scan(o[0], a[0], b[0], ini, f, f2), [a, b], [o], vc(o, [a, b]))
-    def ms(o, c): add("v", lambda: V.memset(o[0], c), [], [o], vc(o, []))
+    def cp(o, i): add("v", lambda: V.tensor_copy(o[0], i[0]), [i], [o])
+    def tt(o, a, b, f): add("v", lambda: V.tensor_tensor(o[0], a[0], b[0], f), [a, b], [o])
+    def ts(o, a, s1, f): add("v", lambda: V.tensor_scalar(o[0], a[0], ap(s1), None, f), [a, s1], [o])
+    def t2(o, a, s1, f, s2, f2): add("v", lambda: V.tensor_scalar(o[0], a[0], ap(s1), ap(s2), f, f2), [a, s1, s2], [o])
+    def red(o, a, f): add("v", lambda: V.tensor_reduce(o[0], a[0], AxisListType.X, f), [a], [o])
+    def scan(o, a, b, ini, f, f2): add("v", lambda: V.tensor_tensor_scan(o[0], a[0], b[0], ini, f, f2), [a, b], [o])
+    def ms(o, c): add("v", lambda: V.memset(o[0], c), [], [o])
     def act(o, i, f=AF.Identity, **kw):
-        add("a", lambda: g.scalar.activation(o[0], i[0], f, **{k: ap(x) for k, x in kw.items()}), [i] + list(kw.values()), [o],
-            0.065 + size(i) * CY * (GA if len(i) > 2 else 1))
-    def mm(o, l, rh, st, sp):
-        add("t", lambda: g.tensor.matmul(o[0], l[0], rh[0], st, sp), [l, rh], [o],
-            max(64, size(rh)) * CY * (1 if l[1][0][0] == "B" else 4))
+        add("a", lambda: g.scalar.activation(o[0], i[0], f, **{k: ap(x) for k, x in kw.items()}), [i] + list(kw.values()), [o])
+    def mm(o, l, rh, st, sp): add("t", lambda: g.tensor.matmul(o[0], l[0], rh[0], st, sp), [l, rh], [o])
     def io_(o, pat, base, cm=0):
         if o[1][0][0] == "I":
-            add("g", lambda: g.iota(o[0], pat, base, cm), [], [o], 0.1344 + 2 * size(o) * CY)
+            add("g", lambda: g.iota(o[0], pat, base, cm), [], [o])
         else:
-            add("g", lambda: g.iota(o[0], pat, base, cm, allow_small_or_imprecise_dtypes=True), [], [o], 0.1344 + 2 * size(o) * CY)
-    def fill(o, c): io_(o, [[0, size(o)]], c)
-    def dma(q, o, i, sem, lat, r=(), w=()):
-        add(q, lambda: Q[q].dma_start(o, i), list(r), list(w), 0.05, lat, "d", sem)
+            add("g", lambda: g.iota(o[0], pat, base, cm, allow_small_or_imprecise_dtypes=True), [], [o])
+    def fill(o, c): io_(o, [[0, len(o[1][0][1])]], c)
+    def dma(q, o, i, sem, r=(), w=()): add(q, lambda: Q[q].dma_start(o, i), list(r), list(w), "d", sem)
     eng = [e for e in topo.engines(T.cores[0], T.cores[1])
            if all(e in topo.engines(a, b) for a in T.cores for b in T.cores if a != b)]
     emask = sum(1 << e for e in eng)
-    def send(dst, o, i, sem, first=False):
+    def send(dst, o, i, sem):
         rid, pid, _e = topo.addr(dst)
-        j = add("g", lambda: g.remote_dma(o[0], i[0], T.sem[sem], T.sem.ls, pid, rid, emask), [i], [], 2.6 if first else 0.3,
-                4.3 if first else 2.0, "r", "ls")
-        c = 0.5 + size(i) * 0.0026
-        add("x", None, [], [o], c, c + 0.3, "x", sem, [j])
+        add("g", lambda: g.remote_dma(o[0], i[0], T.sem[sem], T.sem.ls, pid, rid, emask), [i], [], "r", "ls")
+        add("x", None, [], [o], "x", sem)
 
     def victim(t): return T.cores[(rank + 1 + t % (NR - 1)) % NR]
     def attacker(t): return T.cores[(rank - 1 - t % (NR - 1)) % NR]
@@ -220,10 +214,10 @@ def rank_program(g, core, T, topo):
         return s("R%d" % t, 64 * k, 64 * k + 64) if k < 2 else s("dl%d" % t, 128, 192)
     def dl(t): return s("dl%d" % t, 64, 128)
 
-    dma("s", s("oc")[0], T.oc[:], "loc", 2.2, w=[s("oc")]); seq("ld")
-    dma("a", s("cd")[0], T.cd[:], "lcd", 2.5, w=[s("cd")]); seq("la")
-    dma("a", s("xc_", 16, 16 + U // 2)[0], T.x[:, 0:U // 2], "lx0", 4.0, w=[s("xc_", 16, 16 + U // 2)]); seq("la")
-    dma("s", s("xc_", 16 + U // 2, 16 + U)[0], T.x[:, U // 2:U], "lx1", 4.6, w=[s("xc_", 16 + U // 2, 16 + U)]); seq("ld")
+    dma("s", s("oc")[0], T.oc[:], "loc", w=[s("oc")])
+    dma("a", s("xc_", 16, 16 + U // 2)[0], T.x[:, 0:U // 2], "lx0", w=[s("xc_", 16, 16 + U // 2)])
+    dma("s", s("xc_", 16 + U // 2, 16 + U)[0], T.x[:, U // 2:U], "lx1", w=[s("xc_", 16 + U // 2, 16 + U)])
+    dma("s", s("cd")[0], T.cd[:], "lcd", w=[s("cd")])
 
     HW = 336
     ms(s("ones"), 1.0)
@@ -260,7 +254,7 @@ def rank_program(g, core, T, topo):
     ts(s("g8"), s("x144", 0, 8), gc_, A.is_equal)
     ts(s("idb"), s("x144", 0, 128), pc, A.is_equal)
     t2(s("nid"), s("x144", 0, 128), pc, A.is_equal, -1.0, A.mult)
-    cp(P(6, 0, 192), s("r16", 0, 192))
+    cp(P(6, 0, 208), s("r16", 0, 208))
     for a, b in ((0, NE), (NE, NE + 12), (NE + 12, NC_)):
         tt(s("seg", 16 * a, 16 * b), P(6, 0, 16 * (b - a)), s("rt", 16 * a, 16 * b), A.mult)
         scan(s("cw", 16 * a, 16 * b), s("sgm", 0, 16 * (b - a)), s("seg", 16 * a, 16 * b), 0.0, A.mult, A.add)
@@ -283,17 +277,14 @@ def rank_program(g, core, T, topo):
 
     xw = s("xc_", 16, 16 + U)
     for c, (a, b) in enumerate(((0, 22), (22, 42), (42, 84), (84, 126), (126, 146), (146, 168))):
-        (cp if c in (0, 2, 4) else act)(s("xb_", 16 * a, 16 * b), ind(xw, s("ocu", a, b)))
+        (cp if c in (0, 2, 3) else act)(s("xb_", 16 * a, 16 * b), ind(xw, s("ocu", a, b)))
     act(s("eo0", 0, 128, 2), s("xb_", 0, U, 42))
     act(s("eo0", 1, 128, 2), s("xb_", 20, U, 42))
-    send(victim(0), s("el0", 128, 256), s("eo0"), "ae0", True)
+    send(victim(0), s("el0", 128, 256), s("eo0"), "ae0")
     for h in range(8):
         lo = max(HW * h, 1); hi = HW * h + HW; b = (0, 1, 4)[h % 3]
-        if h in (1, 3, 5):
-            tt(P(b, 0, hi - lo), s("xb_", lo, hi), s("xb_", lo - 1, hi - 1), A.subtract)
-        else:
-            mm(P(b, 0, hi - lo), s("idb"), s("xb_", lo, hi), True, False)
-            mm(P(b, 0, hi - lo), s("nid"), s("xb_", lo - 1, hi - 1), False, True)
+        mm(P(b, 0, hi - lo), s("idb"), s("xb_", lo, hi), True, False)
+        mm(P(b, 0, hi - lo), s("nid"), s("xb_", lo - 1, hi - 1), False, True)
         act(s("ad", 15 + lo, 15 + hi), P(b, 0, hi - lo), AF.Abs)
         lo = HW * h; b = (2, 3, 5)[h % 3]
         mm(P(b, 0, HW), s("fZ"), s("xb_", lo, hi), True, False)
@@ -309,9 +300,9 @@ def rank_program(g, core, T, topo):
             k = 2 * kh + j1
             add("g", lambda k=k, kh=kh, j1=j1: g.affine_select(
                 s("pm", 128 * k, 128 * k + 128)[0], s("ones")[0], [[32, 4], [1000 - 2000 * j1, 2], [2, 16]], A.is_equal, 0.0,
-                kh + 1000 * j1, -1), [s("ones")], [s("pm", 128 * k, 128 * k + 128)], 0.4032)
+                kh + 1000 * j1, -1), [s("ones")], [s("pm", 128 * k, 128 * k + 128)])
     cp(s("cdf"), s("cd"))
-    add("v", lambda: V.transpose(s("cdt")[0], s("cdf")[0]), [s("cdf")], [s("cdt")], 256 * CY)
+    add("v", lambda: V.transpose(s("cdt")[0], s("cdf")[0]), [s("cdf")], [s("cdt")])
     act(c3("TR", None, 0, 32), s("cdt"))
     for k in range(4):
         mm(P(7, 128 * (k // 2), 128 * (k // 2) + 128), s("pm", 128 * k, 128 * k + 128), c3("TR", None, 16 * (k % 2), 16 * (k % 2) + 16), k % 2 == 0, k % 2 == 1)
@@ -323,13 +314,11 @@ def rank_program(g, core, T, topo):
         act(s("wa", lr_, 16, 2), s("g8"), scale=cw(("aL", "aR")[lr_]))
         act(s("wh1", lr_, 16, 2), s("g8"), scale=cw(("hL", "hR")[lr_]))
         act(s("wh2", lr_, 16, 2), s("g8"), scale=col("cw", lr_))
-        act(s("wh1", 16 + lr_, 32, 2), s("g8"), scale=col("r16", 4 + lr_))
-        act(s("wh2", 16 + lr_, 32, 2), s("g8"), scale=col("r16", 4 + lr_))
+        act(s("wz", lr_, 16, 2), s("g8"), scale=col("r16", 4 + lr_))
     K0 = (0, NK[0], NK[0] + NK[1])
     for b in range(3):
         nk = NK[b]
         io_(s("wc", 512 * b, 512 * b + 16 * nk), [[0, 8], [1024, 2], [-2048, nk]], (31 - K0[b]) * 2048)
-        fill(s("wc", 512 * b + 16 * nk, 512 * b + 32 * nk), 0)
     for b in (0, 2):
         nk = NK[b]; a = 128 * b; e = a + 16 * nk
         io_(s("gp", a, e), [[1, 8], [0, 2 * nk]], 0)
@@ -337,17 +326,19 @@ def rank_program(g, core, T, topo):
         act(s("w1", a, e), s("w0", a, e), scale=-1.0 / H16)
         io_(s("sm", a, e), [[0, 8], [1, 2 * nk]], 0)
         act(s("sm", a, e), s("sm", a, e), AF.Sign)
-    act(s("onb"), s("ones")); act(s("idf"), s("idb"))
+    act(s("onb"), s("ones")); act(s("idf"), s("idb")); act(s("nM"), s("idb"), scale=-M26)
     io_(s("gid"), [[1, 8], [0, 16]], 0)
     ts(s("bo"), s("gid"), gc_, A.is_equal)
     act(s("bo6"), s("bo"), scale=1.0 / 64); act(s("nb6"), s("bo"), scale=-1.0 / 64)
     for n, w, c in (("i_k", "idb", cw("i_k")), ("i_b", "idb", cw("n_b")), ("i_as", "idb", cw("n_s")), ("i_la", "idb", col("r16", 4)),
                     ("i_j", "idb", col("r16", 3)), ("i_one", "idb", cw("i_one")), ("i_na", "idb", cw("i_na")), ("i_e", "idb", col("r16", 0)),
-                    ("mix", "idb", cw("m_d")), ("m_n", "nid", cw("mDe")), ("c_l", "idb", cw("c_l")), ("c_r", "idb", cw("c_r"))):
+                    ("mix", "idb", cw("m_d")), ("m_n", "nid", cw("mDe")), ("m_p", "idb", cw("mDe")), ("d_l", "bo", cw("d_l")),
+                    ("d_r", "bo", cw("d_r")), ("c_l", "idb", cw("c_l")), ("c_r", "idb", cw("c_r"))):
         act(dg(n), s(w), scale=c)
     for f, n in ((12, "m_l"), (13, "m_e"), (14, "m_r")):
         act(s("dg", 128 * DN.index("mix") + f, 128 * DN.index("mix") + 128, 16), s("g8"), scale=cw(n))
-    act(s("bom"), s("bo"), scale=0.0); act(s("bom", 11, 128, 16), s("g8")); act(s("bom", 13, 128, 16), s("g8"))
+    fill(dg("e_1"), 0); act(s("dg", 128 * DN.index("e_1"), 128 * DN.index("e_1") + 128, 16), s("g8"), scale=col("r16", 11))
+    act(s("g8n"), s("g8"), scale=-128.0); act(col("pcol", 6), rc, bias=31 * 128.0)
     for k, c in enumerate((cw("r_s"), col("r16", 10), cw("r_n"))):
         act(s("rs", 128 * k, 128 * k + 128), s("bo"), scale=c)
     io_(s("xt", 0, 68), [[1, 17], [672, 4]], 21)
@@ -366,14 +357,10 @@ def rank_program(g, core, T, topo):
     io_(s("xP", 0, 68), [[1, 17], [0, 4]], 0)
     io_(s("y1"), [[1, 17], [0, 4]], 1)
     io_(s("c21"), [[21, 2], [42, 64]], 0)
-    io_(s("m2"), [[0, 4], [1, 16], [0, 2]], 0)
-    io_(s("r2f"), [[1, 4], [0, 2]], 0)
-    cp(s("l_r2"), s("r2f"))
-    ts(s("m2"), s("m2"), rc, A.is_equal)
     fill(s("T1", 0, 16), 100); fill(s("T2", 0, 16), 100); fill(s("T2", 16 + U, 16 + U + 256), 100)
-    fill(s("dl0", 0, 64), 128); fill(s("dy2", 64, 128), 0); fill(s("xb_", ZC, ZC + 16), 0)
+    fill(s("dl0", 0, 64), 128); fill(s("dy2", 64, 128), 0); fill(s("xb_", ZC, ZC + 16), 0); fill(s("xb_", Z1 - 64, Z1), 0)
     fill(s("numb", ZC, ZC + 16), -1); fill(s("nad", 0, 16), 0); fill(s("nad", 256, 272), 0)
-    fill(s("xa"), 21); fill(s("xe_"), 20); fill(s("xh"), TH - 4096 * 21); fill(s("xc"), 21); fill(s("Lw", 4, 8), 0)
+    fill(s("xa", 0, 4), 21); fill(s("xa", 4, 8), 0); fill(s("xa", 8, 12), -21); fill(s("xe_"), 20); fill(s("xh"), TH - 4096 * 21)
     for a in range(0, U, 384): fill(s("numb", a, a + 384), 0)
     for t in range(RO - 1): io_(s("numb", U + NS * t, U + NS * t + NS), [[1, NS]], U + NEWC * t)
     io_(s("numb", Z1, ZC), [[1, NEWC]], U + 2 * NEWC)
@@ -391,22 +378,15 @@ def rank_program(g, core, T, topo):
     tt(s("j256"), s("j256"), s("r16", 0, 64), A.mult)
     for k, (m, b) in enumerate(((1, 0), (1, U + NS - 1), (1, Z1 - 1), (4096, TH), (8192, 4096), (-2, -1))):
         act(s("bc", 2 * k, 2 * k + 2), s("kkw", 0, 2), scale=float(m), bias=float(b))
-    add("g", lambda: g.dma_start(s("ad", 16, 16 + U)[0], s("stat", 16, 16 + U)[0]), [s("stat", 16, 16 + U)], [s("ad", 16, 16 + U)], 1.5, 6.0, "d", "lc")
+    dma("g", s("ad", 16, 16 + U)[0], s("stat", 16, 16 + U)[0], "lc", r=[s("stat", 16, 16 + U)], w=[s("ad", 16, 16 + U)])
     for r in range(16):
         mm(P(7, 0, 168), s("q14", 15 - r, 143 - r), s("ad", 16 + r, 16 + U, 16), r == 0, r == 15)
     cp(s("cl"), P(7, 0, 168))
     fill(s("op_"), 0)
     for u in range(6): cp(s("op_", 32 * u, 32 * u + 28), s("oc", u, 168, 6))
     tt3 = (T.TT[:, :, :], [("TT", np.arange(192))])
-    add("v", lambda: V.transpose(s("ot")[0], s("op_")[0]), [s("op_")], [s("ot")], 192 * CY)
+    add("v", lambda: V.transpose(s("ot")[0], s("op_")[0]), [s("op_")], [s("ot")])
     act(tt3, s("ot"))
-
-    def unpack(t):
-        for k in range(3 if t < RO - 1 else 2):
-            mm(P(4, 64 * k, 64 * k + 64), s("rs", 128 * k, 128 * k + 128), dl(t), True, True)
-        act(s("R%d" % t, 0, 128), P(4, 0, 128))
-        if t < RO - 1:
-            act(s("na"), P(4, 128, 192), bias=1.0)
 
     cp(P(5, 448, 512), s("jc"))
     for t in range(RO):
@@ -421,15 +401,18 @@ def rank_program(g, core, T, topo):
                 tt(s("dy2", 0, 64), dl(1), s("cut"), A.add)
                 win = s("dy2")
             for a in range(0, 168, 42):
-                tt(s(tab, 16 + 16 * a, 16 + 16 * a + 672), ind(win, s("cl", a, a + 42)), s("stat", 16 + 16 * a, 16 + 16 * a + 672), A.add); seq("u")
-            unpack(t - 1)
+                tt(s(tab, 16 + 16 * a, 16 + 16 * a + 672), ind(win, s("cl", a, a + 42)), s("stat", 16 + 16 * a, 16 + 16 * a + 672), A.add)
+            for k in range(3):
+                mm(P(4, 64 * k, 64 * k + 64), s("rs", 128 * k, 128 * k + 128), dl(t - 1), True, True)
+            act(s("R%d" % (t - 1), 0, 128), P(4, 0, 128))
+            act(s("na"), P(4, 128, 192), bias=1.0)
             act(s("xc_", n0, n0 + 256), s("xb_", z0, z0 + 256))
             cp(s("wl_"), s("xb_", z0 + 256, z0 + 272))
             mm(P(3, 0, 255), s("idb"), s("xb_", z0 + 1, z0 + 256), True, False)
             mm(P(3, 0, 255), s("nid"), s("xb_", z0, z0 + 255), False, True)
             act(s("nad", 1, 256), P(3, 0, 255), AF.Abs)
             lst = [("i_as", R(t - 1, 0)), ("i_la", s("lr") if t == 1 else s("cb", 128, 192)), ("i_j", s("jb")), ("i_one", s("onb", 0, 64)),
-                   ("i_na", s("na")), ("i_b", R(t - 1, 2)), ("i_e", s("xb_", z0 + 272, z0 + 336))]
+                   ("i_na", s("na")), ("i_b", R(t - 1, 2)), ("i_e", s("xb_", z0 + 272, z0 + 336)) if t == 1 else ("e_1", dl(1))]
             for k, (w, x) in enumerate(lst):
                 mm(P(4, 192, 256), dg(w), x, k == 0, k == len(lst) - 1)
             act(s("mo", 0, 64), P(4, 192, 256))
@@ -442,16 +425,14 @@ def rank_program(g, core, T, topo):
             act(s(tab, n0, n0 + 256), P(7, 256, 512))
             act(s("R%d" % (t - 1), 128, 192), R(t - 1, 2))
             for r in range(16):
-                mm(P(1, 256, 268), s("q16", 15 - r, 143 - r), s("R%d" % (t - 1), r, 192, 16), r == 0, r == 15)
-            act(s("wr"), P(1, 256, 268))
+                mm(P(1, 256, 268), s("q16", 15 - r, 143 - r), s("R%d" % (t - 1), r, 192, 16), r == 0, False)
+            mm(P(1, 256, 268), s("idb"), s("xa"), False, True)
+            act(s("wr", 0, 8), P(1, 256, 264)); act(s("xd"), P(1, 264, 268), bias=float(z0 - 1))
             act(s("xf"), s("wr", 4, 8), scale=-2.0, bias=1.0)
-            tt(s("xc"), s("xa"), s("wr", 0, 4), A.add)
-            tt(s("xd"), s("wr", 8, 12), s("xa"), A.subtract)
-            tt(s("xg"), s("xe_"), s("wr", 4, 8), A.mult)
-            tt(s("xi"), s("xg"), s("c21w", 0, 4) if t == 1 else s("xb"), A.add)
-            act(s("xd"), s("xd"), bias=float(z0 - 1))
             for q in range(4):
-                act(s("xP", 68 + q, 136, 4), s("y1", q, 68, 4), scale=-1.0, bias=col("xc", q))
+                act(col("xi", q), col("xe_", q), scale=col("wr", 4 + q), bias=col("c21w" if t == 1 else "xb", q))
+            for q in range(4):
+                act(s("xP", 68 + q, 136, 4), s("y1", q, 68, 4), scale=-1.0, bias=col("wr", q))
                 act(s("xm", q, 136, 4), s("xP", q, 136, 4), scale=4096.0, bias=col("xh", q))
                 act(s("xt", q, 136, 4), s("xP", q, 136, 4), scale=col("xf", q), bias=col("xi", q))
                 act(s("xu", q, 136, 4), s("xP", q, 136, 4), bias=col("xd", q))
@@ -461,7 +442,7 @@ def rank_program(g, core, T, topo):
         else:
             cp(s("l_xv"), s("xu"))
         for a, b in (((0, 24), (24, 48), (68, 92), (92, 116)) if t == 0 else ((0, 34), (34, 68), (68, 102), (102, 136))):
-            act(s("XV", 16 * a, 16 * b), ind(s("xb_", 0, U + NS * t), s("l_xv", a, b))); seq("xv")
+            act(s("XV", 16 * a, 16 * b), ind(s("xb_", 0, U + NS * t), s("l_xv", a, b)))
         for r in range(16):
             mm(P(6, 0, 8), s("qz", 15 - r, 143 - r), s(el, 128 + r, 256, 16), r == 0, r == 15)
         for B in range(8):
@@ -470,19 +451,18 @@ def rank_program(g, core, T, topo):
             ts(s("mj", a, b), s("mi", a, b), 4095, A.bitwise_and)
             t2(s("ml", a, b), s("mj", a, b), float(4096 - lim - 16), A.subtract, 0.0, A.max)
         act(s(el, 256, 384), s(el, 128, 256)); act(s(el, 384, 640), s(el, 128, 384))
-        nn = 16 if t == 0 else 32
         for b in range(3):
             nk = NK[b]; o = 256 * (b // 2)
-            mm(P(b, 0, nn * nk), row0("onb", 0, 128), row0("wc", 512 * b, 512 * b + nn * nk), True, False)
+            mm(P(b, 0, 16 * nk), row0("onb", 0, 128), row0("wc", 512 * b, 512 * b + 16 * nk), True, False)
             mm(P(b, 0, 16 * nk), s(el, 128, 256), s("w0", o, o + 16 * nk), False, False)
             if t > 0:
-                mm(P(b, 16 * nk, 32 * nk), s(el, 0, 128), s("w1", o, o + 16 * nk), False, False)
+                mm(P(ZB[b], 0, 16 * nk), s(el, 0, 128), s("w1", o, o + 16 * nk), True, False)
         for c in range(len(CB) - 1):
             a, e = 128 * CB[c], 128 * CB[c + 1]
-            tt(s("MN", a, e), ind(s("xc_", 0, 16 + lim), s("ml", a // 16, e // 16)), s(el, 128, 128 + e - a), A.min); seq("mn")
+            tt(s("MN", a, e), ind(s("xc_", 0, 16 + lim), s("ml", a // 16, e // 16)), s(el, 128, 128 + e - a), A.min)
             if CB[c] in CG:
                 e2 = 128 * CG[CG.index(CB[c]) + 1]
-                act(s("G", a, e2), ind(s(tab, 0, 16 + lim), s("ml", a // 16, e2 // 16)), AF.Relu); seq("g")
+                act(s("G", a, e2), ind(s(tab, 0, 16 + lim), s("ml", a // 16, e2 // 16)), AF.Relu)
             for k in range(CB[c], CB[c + 1]):
                 b = 0 if k < K0[1] else (1 if k < K0[2] else 2)
                 nk = NK[b]; last = k - K0[b] == nk - 1
@@ -491,13 +471,13 @@ def rank_program(g, core, T, topo):
                 if t == 0:
                     mm(o, s("G", 128 * k, 128 * k + 128), s("wa"), False, last)
                 else:
-                    mm(P(b, k - K0[b], 32 * nk, nk), s("G", 128 * k, 128 * k + 128), s("wh%d" % t), False, last)
+                    mm(P(ZB[b], k - K0[b], 16 * nk, nk), s("G", 128 * k, 128 * k + 128), s("wz"), False, last)
+                    mm(o, s("G", 128 * k, 128 * k + 128), s("wh%d" % t), False, False)
                 if last:
                     o = 256 * (b // 2)
                     if t > 0:
-                        if b < 2: act(s("zb", 256 * b, 256 * b + 16 * nk), P(b, 16 * nk, 32 * nk), scale=-M26, bias=31.5 * M26)
-                        else: t2(s("zb", 256 * b, 256 * b + 16 * nk), P(b, 16 * nk, 32 * nk), -M26, A.mult, 31.5 * M26, A.add)
-                        tt(P(b, 0, 16 * nk), P(b, 0, 16 * nk), s("zb", 256 * b, 256 * b + 16 * nk), A.min)
+                        act(s("zb", 256 * b, 256 * b + 16 * nk), P(ZB[b], 0, 16 * nk), AF.Relu, bias=-31.0)
+                        mm(P(b, 0, 16 * nk), s("nM"), s("zb", 256 * b, 256 * b + 16 * nk), False, True)
                     scan(s("ks", 256 * b, 256 * b + 16 * nk), s("sm", o, o + 16 * nk), P(b, 0, 16 * nk), 0.0, A.mult, A.max)
                     if b == 1:
                         tt(s("red"), s("ks", 2 * nk - 1, 16 * nk, 2 * nk), s("ks", 256 + 2 * nk - 1, 256 + 16 * nk, 2 * nk), A.max)
@@ -505,11 +485,22 @@ def rank_program(g, core, T, topo):
             o = OFF["numb"][1]
             for k in range(8):
                 dma("s", T.F[16 * k:16 * k + 1, o:o + U], T.TT[32 * (k // 2):32 * (k // 2) + 28, :, 16 * (k % 2):16 * (k % 2) + 16],
-                    "ln%d" % k, 3.0, r=[tt3, s("MN", 0, 16)], w=[s("numb", k, U, 8)]); seq("ln")
+                    "ln%d" % k, r=[tt3, s("MN", 0, 16)], w=[s("numb", k, U, 8)])
         tt(s("ri"), s("red"), s("ks", 512 + 2 * nk - 1, 512 + 16 * nk, 2 * nk), A.max)
         ts(s("rj"), s("ri"), 0xFF07FF, A.bitwise_and)
         ts(s("rep"), ind(s("rj"), s("l_rep")), col("pcol", 5), A.add)
-        add("t", lambda: g.tensor.transpose(P(3, 0, 128)[0], s("rep")[0], s("idf")[0]), [s("rep"), s("idf")], [P(3, 0, 128)], 512 * CY)
+        if t == 1:
+            t2(s("rk"), s("ri"), 11, A.logical_shift_right, 31, A.bitwise_and)
+            tt(s("g2"), ind(s("rk"), s("l_rep")), s("r16", 0, 128), A.mult)
+            mm(P(6, 64, 72), s("g2"), s("g8n"), True, False)
+            mm(P(6, 64, 72), row0("onb", 0, 128), row0("kb", 0, 128, 16), False, True)
+            ts(s("l_p0"), P(6, 64, 72), col("pcol", 6), A.add)
+            act(s("ex"), ind(s("G"), s("l_p0")))
+            mm(P(7, 0, 128), dg("d_l"), s("ex"), True, True); mm(P(7, 128, 256), dg("d_r"), s("ex"), True, True)
+            act(s("ifl"), P(7, 0, 256), AF.Relu)
+            for k, (w, a) in enumerate((("m_p", 0), ("m_p", 128), ("m_n", 1), ("m_n", 129))):
+                mm(P(6, 128, 192), dg(w), s("ifl", a, 128 + a - a % 2, 2), k == 0, k == 3)
+        add("t", lambda: g.tensor.transpose(P(3, 0, 128)[0], s("rep")[0], s("idf")[0]), [s("rep"), s("idf")], [P(3, 0, 128)])
         cp(s("he"), P(3, 0, 128, 2))
         tt(s("Hi"), P(3, 1, 128, 2), s("he"), A.max)
         Hi = s("Hi")
@@ -530,7 +521,11 @@ def rank_program(g, core, T, topo):
         t2(s("d64"), Hi, 4, A.logical_shift_right, 64, A.bitwise_and)
         tt(P(5, 128, 192), s("pl"), s("d64"), A.add)
         po = "po%d" % t
-        if t < RO - 1:
+        if t == 1:
+            ts(s("q_gn"), s("g16"), 1.0 / H16, A.mult)
+            for k, (w, x) in enumerate((("m_p", s("ifl", 1, 128, 2)), ("m_p", s("ifl", 129, 256, 2)), ("m_n", s("q_gn")))):
+                mm(P(3, 128, 192), dg(w), x, k == 0, k == 2)
+        if t == 0:
             tt(s("mm"), P(5, 128, 192), s("r16", 0, 64), A.mult)
             scan(s("ms"), s("sgm", 0, 64), s("mm"), 0.0, A.mult, A.add)
             cp(s("l_p0", 0, 4), s("ms", 15, 64, 16))
@@ -542,12 +537,13 @@ def rank_program(g, core, T, topo):
             act(s("g2a"), P(6, 64, 128), AF.Abs)
             mm(P(6, 128, 192), s("bo"), s("g2a"), True, False)
             mm(P(6, 128, 192), s("nid"), s("q_gn"), False, True)
-            if t == 1:
-                mm(P(3, 128, 192), s("bom"), s("g2a"), True, False)
-                mm(P(3, 128, 192), dg("m_n"), s("q_gn"), False, True)
             act(s(po, 272, 336), P(6, 128, 192))
         t2(s("U1"), s("mu"), cw("ua1"), A.mult, cw("ub1"), A.add)
-        t2(P(5, 192, 256), s("mu"), cw("ua2"), A.mult, cw("ub2"), A.add)
+        if t == 1:
+            t2(s("wm"), s("mu"), cw("ua2"), A.mult, cw("ub2"), A.add)
+            tt(P(5, 192, 256), P(6, 128, 192), s("wm"), A.add)
+        else:
+            t2(P(5, 192, 256), s("mu"), cw("ua2"), A.mult, cw("ub2"), A.add)
         tt(P(5, 192, 256), P(5, 192, 256), s("hd"), A.mult)
         tt(s("U1"), P(5, 192, 256), s("U1"), A.add)
         if t == 1: tt(s("U1"), P(3, 128, 192), s("U1"), A.add)
@@ -578,13 +574,9 @@ def rank_program(g, core, T, topo):
             eo = "eo%d" % (t + 1)
             tt(s("e8i"), s(e8), s("c8"), A.add)
             cp(s("l_end"), s("e8i"))
-            cp(s(eo, 128, 256, 2), ind(s("XV", 0, XVN), s("l_end", 0, 4)))
+            act(s(eo, 128, 256, 2), ind(s("XV", 0, XVN), s("l_end", 0, 4)))
             act(s(eo, 129, 256, 2), ind(s("XV", 0, XVN), s("l_end", 4, 8)))
-            t2(s("cs"), s("bm"), -1.0, A.mult, -1.0, A.add)
-            tt(s("cs"), s("cs"), s("vx", 0, 4), A.mult)
-            tt(s("Lw", 0, 4), s("cs"), s("xc"), A.add)
-            tt(s(eo, 0, 128), ind(s("Lw"), s("l_r2")), s("m2"), A.mult)
-            send(victim(t + 1), s("el%d" % (t + 1), 0, 256), s(eo), "ae%d" % (t + 1))
+            if t == 0: tt(s("cs"), s(e8, 0, 4), s(e8, 4, 8), A.add)
         tt(s("val"), P(5, 128, 192), s("j32"), A.add)
         tt(s("mm"), P(5, 384, 448), s("j256"), A.min)
         scan(s("ms"), s("sgm", 0, 64), s("mm"), 0.0, A.mult, A.add)
@@ -600,24 +592,27 @@ def rank_program(g, core, T, topo):
             ts(s("ww"), s("Fw"), 15, A.arith_shift_right)
             t2(s(po, 256, 272), s("ww"), -1.0, A.mult, 63.0, A.add)
             fill(s("sw", 0, 272), 2 ** 23)
-        send(attacker(t), s("xb_", U + NS * t, U + NS * t + NS) if t < RO - 1 else s("xb_", Z1, ZC), s(po), "ap%d" % t)
+        send(attacker(t), s("xb_", U + NS * t, U + NS * t + OFF[po][2]), s(po), "ap%d" % t)
         tt(s("ex"), ind(s(e8), s("l_rep")), s("r16", 0, 128), A.mult)
         mm(P(2, 320, 384), s("idb"), s("lr") if t < 2 else s("cb", 128, 192), True, False)
         if t > 0: mm(P(2, 320, 384), s("idb"), R(t - 1, 0), False, False)
         mm(P(2, 320, 384), s("nb6"), s("ex", 0, 64), False, False)
         mm(P(2, 320, 384), s("nb6"), s("ex", 64, 128), False, True)
         mm(P(2, 192, 320), s("bo6"), s("ex"), True, True)
+        if t < RO - 1:
+            act(s(eo, 0, 128, 2), P(2, 320, 384), scale=1.0 / 16); act(s(eo, 1, 128, 2), P(2, 320, 384), scale=1.0 / 16)
+            send(victim(t + 1), s("el%d" % (t + 1), 0, 256), s(eo), "ae%d" % (t + 1))
         act(s("C%d" % t), P(2, 192, 384))
         if t == 0:
             act(s("cb"), P(2, 192, 384))
             mm(P(2, 384, 448), dg("c_l"), s("cb", 0, 64), True, False)
             mm(P(2, 384, 448), dg("c_r"), s("cb", 64, 128), False, True)
             act(s("cut"), P(2, 384, 448))
-            act(s("La2"), s("Lw", 0, 4))
+            act(s("La2"), s("cs"), scale=-1.0 / 64, bias=21.0)
             act(s("xb"), s(e8, 0, 4), scale=1.0 / 64)
             tt(s("xb"), s("xb"), s("c21w", 4, 8), A.add)
         if t == 1:
-            act(s("xa"), s("La2"))
+            act(s("xa", 0, 4), s("La2")); act(s("xa", 8, 12), s("La2"), scale=-1.0)
             act(s("xe_"), s("La2"), bias=-1.0)
             act(s("xh"), s("La2"), scale=-4096.0, bias=float(TH))
 
@@ -626,23 +621,23 @@ def rank_program(g, core, T, topo):
     def bc(k, ih): return col("bc", 2 * k + ih)
     act(s("gb"), C(0, 2), bias=-1.0)
     act(s("ga"), R(1, 1), scale=-2.0, bias=1.0)
-    tt(s("ge"), s("c21", 64, 128), C(0, 0), A.add)
     tt(s("gb"), s("gb"), R(1, 1), A.mult)
-    tt(s("ge"), s("ge"), s("gb"), A.add)
     for ih in range(2):
         act(h("fd", ih), s("ga"), scale=bc(0, ih))
-        tt(h("fd", ih), h("fd", ih), s("ge"), A.add)
+        for k, x in enumerate((s("c21", 64, 128), C(0, 0), s("gb"), h("fd", ih))):
+            mm(P(7, 64 * ih, 64 * ih + 64), s("idf"), x, k == 0, k == 3)
+    act(s("fd"), P(7, 0, 128))
     mm(P(3, 64, 128), s("bo6"), s("ex", 0, 64), True, False); mm(P(3, 64, 128), s("nid"), s("cb", 128, 192), False, True)
     mm(P(3, 128, 192), s("bo6"), s("ex", 0, 64), True, False); mm(P(3, 128, 192), s("nid"), s("cb", 128, 192), False, False)
     mm(P(3, 128, 192), s("idb"), R(1, 2), False, True)
-    tt(s("gg"), s("ga"), C(2, 0), A.mult)
+    tt(P(5, 384, 448), s("ga"), C(2, 0), A.mult)
     for ih in range(2):
         act(h("fa", ih), P(3, 64, 128), scale=4096.0, bias=bc(3, ih))
         act(h("fb", ih), P(3, 128, 192), bias=bc(1, ih))
-        act(h("fc", ih), C(2, 2), scale=-8192.0, bias=bc(4, ih))
-        tt(p5(0, ih), h("fd", ih), s("gg"), A.add)
+        act(h("fe", ih), C(2, 2), scale=-8192.0, bias=bc(4, ih))
+        tt(p5(0, ih), P(5, 384, 448), h("fd", ih), A.add)
     tt(s("fa"), s("fa"), s("fb"), A.min)
-    tt(P(5, 0, 128), P(5, 0, 128), s("fc"), A.max)
+    tt(P(5, 0, 128), P(5, 0, 128), s("fe"), A.max)
     tt(P(5, 0, 128), P(5, 0, 128), s("fa"), A.max)
     for ih in range(2):
         ts(s("l_f", 2 + ih, 256, 4), p5(0, ih), float(ZC), A.min)
@@ -652,80 +647,55 @@ def rank_program(g, core, T, topo):
     tt(s("hb"), s("hb"), s("c21", 0, 64), A.add)
     act(s("c1b"), C(1, 2))
     for ih in range(2):
-        act(h("hm", ih), C(1, 2), scale=-4096.0, bias=bc(3, ih))
+        act(P(7, 64 * ih, 64 * ih + 64), C(1, 2), scale=-4096.0, bias=bc(3, ih))
         act(h("hq", ih), C(1, 2), bias=bc(5, ih))
         act(h("hr", ih), C(1, 0), bias=bc(0, ih))
-    unpack(2)
+    for k, n in enumerate(("fj", "fk")):
+        if k: tt(s("fh"), s("hq"), s("hr"), A.add)
+        x = "fh" if k else "hr"
+        act(s("fg"), s(x), scale=4096.0, bias=float(TH - 4096 * 21))
+        for ih in range(2):
+            tt(p5(128, ih), h(x, ih), s("ha"), A.mult)
+            tt(p5(256, ih), h(x, ih), s("hf"), A.add)
+            tt(h("ff", ih), p5(128, ih), s("hb"), A.add)
+        tt(P(5, 256, 384), P(5, 256, 384), s("fg"), A.min)
+        tt(s(n), P(5, 256, 384), s("ff"), A.max)
+    tt(s("fk"), s("fk"), s("fj"), A.subtract)
+    mm(P(4, 0, 64), s("rs", 128, 256), dl(2), True, True)
     mm(P(6, 0, 64), s("rs", 0, 128), dl(2), True, False); mm(P(6, 0, 64), s("idb"), s("c1b"), False, True)
     mm(P(3, 0, 64), s("idb"), R(2, 2), True, False); mm(P(3, 0, 64), s("nid"), s("c1b"), False, True)
     for ih in range(2):
-        tt(p5(128, ih), h("hq", ih), R(2, 1), A.mult)
+        tt(p5(128, ih), P(4, 0, 64), h("fk", ih), A.mult)
         act(h("hn", ih), P(3, 0, 64), bias=bc(2, ih))
         act(h("fc", ih), P(6, 0, 64), scale=-8192.0, bias=bc(4, ih))
-    tt(s("fh"), P(5, 128, 256), s("hr"), A.add)
-    tt(P(5, 256, 384), s("hn"), s("hm"), A.min)
-    act(s("fg"), s("fh"), scale=4096.0, bias=float(TH - 4096 * 21))
-    for ih in range(2):
-        tt(p5(128, ih), h("fh", ih), s("ha"), A.mult)
-        tt(p5(0, ih), h("fh", ih), s("hf"), A.add)
-        tt(h("ff", ih), p5(128, ih), s("hb"), A.add)
-    tt(P(5, 256, 384), P(5, 256, 384), s("fc"), A.max)
-    tt(s("fd"), P(5, 0, 128), s("fg"), A.min)
-    tt(P(5, 256, 384), P(5, 256, 384), s("ff"), A.max)
-    tt(P(5, 256, 384), P(5, 256, 384), s("fd"), A.max)
+    tt(P(5, 128, 256), P(5, 128, 256), s("fj"), A.add)
+    tt(s("hn"), P(7, 0, 128), s("hn"), A.min)
+    tt(P(5, 128, 256), P(5, 128, 256), s("fc"), A.max)
+    tt(P(5, 256, 384), P(5, 128, 256), s("hn"), A.max)
     for ih in range(2):
         ts(s("l_f", ih, 256, 4), p5(256, ih), float(ZC), A.min)
     o = OFF["YO"][1]
     for f, a, b in ((act, 0, 1024), (act, 1024, 2048), (act, 2048, 3072), (cp, 3072, 4096)):
         f(s("YO", a, b), ind(s("numb"), s("l_f", a // 16, b // 16)))
-    dma("s", T.yo[:, :], T.F[0:128:16, o:o + 4096], "so", 2.5, r=[s("YO")])
+    dma("s", T.yo[:, :], T.F[0:128:16, o:o + 4096], "so", r=[s("YO")])
     for f, a, b in YC:
         (cp if f else act)(s("G", a, b), ind(s("xb_"), s("l_f", a // 16, b // 16)))
-        dma("s" if f else "a", T.y[:, a:b], s("G", a, b)[0], "so", 1.9 + (b - a) / 1500, r=[s("G", a, b)])
+        dma("s" if f else "a", T.y[:, a:b], s("G", a, b)[0], "so", r=[s("G", a, b)])
 
-    n = len(ops)
-    if "order" not in MEMO:
-        def gap(j, i):
-            if not ops[i][2][j]: return ops[j][3]
-            if ops[j][0] == ops[i][0] and ops[j][5] == "c":
-                return ops[j][4] + (0.0 if ops[i][0] == "t" else 0.07)
-            return ops[j][4] + (0.0 if ops[i][5] == "x" else 0.12)
-        pre = [[(j, gap(j, i)) for j in o[2]] for i, o in enumerate(ops)]
-        suc = [[] for _ in range(n)]
-        for i in range(n):
-            for j, d in pre[i]: suc[j].append((i, d - ops[j][3] + ops[i][3]))
-        MEMO["g"] = (ops, pre, suc, BOOST)
-        prio = [0.0] * n
-        for i in range(n - 1, -1, -1):
-            prio[i] = max([d + prio[k] for k, d in suc[i]] + [ops[i][4] - ops[i][3]]) + BOOST.get(i, 0.0)
-            for k, d in suc[i]:
-                if prio[i] + ops[i][3] <= prio[k] + ops[k][3]: prio[i] = prio[k] + ops[k][3] - ops[i][3] + 1e-6
-        at = [0.0] * n
-        busy = {q: [] for q in "vatgsx"}
-        for i in sorted(range(n), key=lambda i: (-prio[i] - ops[i][3], i)):
-            r = max([at[j] + d for j, d in pre[i]] + [0.0])
-            c = ops[i][3]; b = busy[ops[i][0]]
-            lo = 0
-            while lo < len(b) and b[lo][1] <= r: lo += 1
-            while lo < len(b) and b[lo][0] < r + c - 1e-9:
-                r = max(r, b[lo][1]); lo += 1
-            at[i] = r
-            a = max(r - 1.0, b[lo - 1][1] if lo else 0.0) if ops[i][5] == "r" else r
-            b.insert(lo, (a, r + c))
-        MEMO["span"] = max(at[i] + ops[i][4] for i in range(n))
-        MEMO["order"] = sorted(range(n), key=lambda i: (at[i], i))
+    order = [62 * DIGITS.index(ORDER[i]) + DIGITS.index(ORDER[i + 1]) for i in range(0, len(ORDER), 2)]
+    assert sorted(order) == list(range(len(ops)))
     cnt = {}
     ev = {}
     know = {q: {} for q in Q}
-    for i in MEMO["order"]:
-        q, fn, pre, _c, _l, kind, sem = ops[i]
+    for i in order:
+        q, fn, pre, kind, sem = ops[i]
         if kind == "x":
             cnt[sem] = len(eng); ev[i] = (sem, len(eng), {})
             continue
         need = {}
-        for j, must in pre.items():
-            if not must or (q == "t" and ops[j][0] == q): continue
+        for j in pre:
             sm, c, kn = ev[j]
+            if q == "t" and ops[j][0] == q: continue
             if need.get(sm, (0,))[0] < c: need[sm] = (c, kn)
         for sm, (c, kn) in sorted(need.items(), key=lambda e: -len(e[1][1])):
             if know[q].get(sm, 0) < c:

import numpy as np
from concourse.mybir import AluOpType as A, AxisListType, ActivationFunctionType as AF

U, NEWC, RO = 2688, 256, 3
XVN = 34 * 64
NS = 336
Z1 = U + 2 * NS
ZC = Z1 + NEWC
TH = 4000
H16, M26 = 65536.0, 2.0 ** 26
NK = (14, 14, 4)
CB = (0, 2, 6, 10, 14, 18, 22, 26, 28, 30, 31, 32)
CG = (0, 6, 14, 22, 26, 28, 30, 31, 32)
YC = ((1, 0, 1280), (1, 1280, 2304), (1, 2304, 2816), (1, 2816, 3072), (0, 3072, 3712), (0, 3712, 4096))
ZB = (4, 6, 3)

COLS = {
    "s_i": {4: 1, 5: -1, 6: -1, 7: 1, 8: 2, 14: -2, 10: 256, 11: 256, 12: -256, 13: -256},
    "s_e": {15: 64}, "s_j": {3: 1},
    "s_c": {5: 20, 6: 1, 7: -19, 8: -19, 14: 20, 10: -5120, 11: -5120},
    "aL": {1: H16, 2: -H16, 6: -M26, 7: -M26, 8: -M26, 15: -M26, 4: 64, 3: 1},
    "aR": {0: H16, 2: -H16, 6: -M26, 7: -M26, 14: -M26, 15: -M26, 5: 64, 3: 1},
    "ua1": {5: 1, 8: -1, 14: 1}, "ub1": {5: 1, 7: -1, 8: -1, 14: 1},
    "ua2": {4: 1, 5: -1, 8: 2, 14: -2}, "ub2": {4: 1, 5: -1, 6: -1, 7: 1, 8: 1, 14: -1, 9: 1},
    "hL": {1: H16, 10: -H16, 11: H16, 2: -H16, 6: -M26, 7: -M26, 8: -M26},
    "hR": {0: H16, 12: -H16, 13: H16, 2: -H16, 6: -M26, 7: -M26, 14: -M26},
    "lL": {4: 64, 3: 1, 9: 1024}, "lR": {5: 64, 3: 1, 9: -1024},
    "mDe": {11: 1, 13: 1}, "r_s": {4: 1, 5: 1}, "r_n": {9: -1, 7: 1}, "q_c": {3: 1, 15: 1},
    "i_k": {4: 1, 5: -1, 7: 1, 8: 2, 14: -2, 12: -256, 13: -256}, "n_b": {4: -1, 5: 1, 7: -1, 12: 1, 13: 1}, "n_s": {5: 1, 7: -1},
    "i_one": {4: 1, 5: -2, 7: 3, 8: 1, 10: -256, 12: -1, 13: -1}, "i_na": {7: 2048},
    "m_d": {3: 1, 4: 1, 5: 1, 7: 1, 10: 1, 12: 256}, "m_l": {4: 1, 5: -1, 8: 1}, "m_e": {13: 256, 0: 1}, "m_r": {5: 1, 4: -1},
    "d_l": {1: 1, 10: -1, 11: 1, 8: -256}, "d_r": {0: 1, 12: -1, 13: 1, 14: -256},
    "c_l": {4: -1, 6: 1, 8: -1, 14: 1, 12: 256, 13: 256}, "c_r": {5: -1, 7: 1, 8: 1, 14: -1, 10: 256, 11: 256},
}
for _k in ("L", "R"):
    COLS["h" + _k].update(COLS.pop("l" + _k))
_to = {8: 12, 12: 8, 9: 10, 10: 9}
COLS = {n: {_to.get(f, f): c for f, c in d.items()} for n, d in COLS.items()}
CN = list(COLS)
NE, NC_ = 4, len(CN)
DN = ["i_k", "i_b", "i_as", "i_la", "i_j", "i_one", "i_na", "i_e", "c_l", "c_r", "mix", "m_n", "m_p", "d_l", "d_r", "e_1"]

SIZES = {"F": {}, "B": {}, "I": {}, "U": {}}
def _a(ar, **kw):
    SIZES[ar].update(kw)
_a("F", stat=16 + U, T1=16 + U + 256, T2=16 + U + 512, spos=U, numb=ZC + 16, cp2=672, YO=4096, op_=192, ot=192,
   pcol=16, g8=8, x144=144, pat=256, r16=272, sgm=256, rt=16 * NC_, seg=16 * NC_, cw=16 * NC_, sb=8,
   idf=128, cdf=256, cdt=256, pm=4 * 128, gp=320, ks=768, red=8, rep=128, he=64, gid=128,
   jc=64, tq=4 * 80, best=4, wm=64, ones=128, ac0=64, cnt=2, j32=64, j256=64,
   mm=64, ms=64, o1=64, val=64, sw=1184, Fs=256, F2=256, cap=256, m64=256, U1=64, U5=64,
   kkw=16, vq=4, vx=8, vm=4, cs=4, et=8, e80=8, e81=8, e82=8, c8=8, La2=4,
   dy2=128, cut=64,
   wr=12, xb=4, xd=4, xe_=4, xf=4, xh=4, xi=4, c21w=8, y1=68, xP=136, xt=136, xm=136, xu=136,
   c21=128, bc=16, fa=128, fb=128, fc=128, fd=128, ff=128, fg=128, fh=128, fj=128, fk=128, fe=128, ga=64, gb=64,
   ha=64, hb=64, hf=64, hn=128, hq=128, hr=128, C0=192, C1=192, C2=192)
_a("B", xc_=16 + U + 512, xb_=ZC + 16, ad=U + 32, G=4096, MN=4096, XV=XVN + 16, bo=128, bo6=128, g8n=8, mo=80, ifl=256, nb6=128,
   idb=128, nid=128, qz=144, q1=144, q14=144, q16=144, dg=128 * len(DN), ds=3 * 128, pt=3 * 336, fR=128, fL=128, fZ=128,
   w0=320, w1=320, sm=320, wc=1536, wf=16, wa=16, wh1=16, wh2=16, wz=16, zb=768, nM=128, rs=3 * 128, R0=192, R1=192, na=64,
   onb=128, jb=64, kb=256, eo0=128, eo1=256, eo2=256, el0=640, el1=640, el2=640, W=256, q_gn=64, g2=128, g2a=64,
   po0=NS, po1=272, po2=256, mo0=128, mo1=128, mo2=128, dl0=192, dl1=192, dl2=192, ex=128, lr=64, xa=12, c1b=64, cb=192, nad=272)
_a("I", oc=168, cd=256, pi=4, mi=256, mj=256, ri=8, rj=8, rk=8, Hi=64, vf=64, dm=64, g16=64, mu=64, hd=64, pl=64, d64=64,
   Fw=16, cc=16, ww=16, bi=4, bx=4, bm=4, bd=4, e8i=8)
_a("U", ocu=168, cl=168, ml=256, l_rep=8, l_p0=8, l_off=4, l_pos=16, wl_=16, l_end=8, l_xv=136, l_f=256)
OFF = {}
TOT = {}
for _ar, _d in SIZES.items():
    _o = 0
    for _n, _s in _d.items():
        OFF[_n] = (_ar, _o, _s)
        _o += (_s + 15) // 16 * 16
    TOT[_ar] = _o
SCRATCH = {"F": ("sbuf", [128, TOT["F"]], "float32"), "B": ("sbuf", [128, TOT["B"]], "bfloat16"),
           "I": ("sbuf", [128, TOT["I"]], "int32"), "U": ("sbuf", [128, TOT["U"]], "uint16"),
           "TR": ("sbuf", [128, 8, 32], "float32"), "CT": ("sbuf", [128, 8, 32], "float32"),
           "TT": ("sbuf", [128, 6, 32], "float32")}
for _b in range(8):
    SCRATCH["P%d" % _b] = ("psum", [128, 512], "float32")
SEMAPHORES = ["cv", "ca", "ct", "cg", "ls", "lx0", "lx1", "loc", "lcd", "so", "lc"] + ["ln%d" % k for k in range(8)] + \
    ["%s%d" % (n, t) for n in ("ae", "ad", "ap") for t in range(RO)]

MEMO = {}
DIGITS = "0123456789abcdefghijklmnopqrstuvwxyzABCDEFGHIJKLMNOPQRSTUVWXYZ"
ORDER = (
    "00010409020305060k0e080d0n1y0j0M0m1A0U1R160A0W1z0V0o121a1007140Z0u0g0G0b151W0J1g0r1h0H1i110Y18171j0S0y0I1l0E0p1b1n0a0h0s1d0l1k0f0z0t"
    "1T1f1r130X0B1o0x1S0q391U1e1P0v1p0Q0C0i1c1m1B1s1D0c1V1F0w1t1C1q1E1J0F1w1H1Q1I1x1G3c1X1Y1K3J1L1M3z221Z27282a3b1O2e2f292h3y3d2n202g2b4o"
    "2c1N3G2q2u3B2d2i2j3e2o0N3H213E2l2x2v2D2k2E3a2p2G3A2m23242r2w2s252K2L2t2y3C2T192F2z2B2U2N2A2H2I0L3t300T2M312C2W0K3f2O2P2J4M3g4l3L334j"
    "2R3o523h2Q4m3i3O2V3j4u0O5L0D2S3K2X322Y6l4i260P0R2Z344w356n3M1u6p3X37563s4v4c365R5S5T5U5V5W5X5Y5Z3U6061626364653x4h1v666q3I6o3k6m384x"
    "3l53594G6j3F6a4L6b69674t68586e6c5k6d3p6k6f6h6g4d6i3u3v6s6r6x6t4n4r6H6G6u6v6w6y6z6A6B6C6D6E6F576Q6I4s714k706J6K6L6M6N5C6O6P6R6S6T6U6V"
    "6W6X6Y4S7a727k4y737j7475767778797b7c7d7e7f7g7h7i4q7u7t7l7m7n7o7p7C7q7r7s7B7v7w7x4V7y7I7H7M7D7E7F7L7G7J5a7K6Z3T7N7O7z4W5l555m5n3Y7P5o"
    "7A5D5p3W7Y5q5E5r7Z3S5s5F5t803nbv3m9w4U3Z5u5G5v5d3r813P3q3V5M5w5I3w5x825y5N5H5z835A864z8t844Q85878w4T895O888e8o8P8L8f8a8j8g8p5P8b8k8q"
    "4B8u8l8c8r8h4O8m8d8M5Q4D8K8i8v8n8s8N4P8x8O4N8Q8y8R8S408V8T5c8z8W488U478B4e9g8A8X9f4g9h8Z8C8D4X9i919j4f8E8F93499k3D908G9l3R4H8H968I45"
    "9m9s925b9n949o8J959q979p989r994A9a9v9K8Y3Q9t9e9b3N5J9x9y9z4Y9c5B9d9L9Aa95K9B9M9Q9J9R9Saf9C7Q9T7R7S7T7U9U4R7V7W467Xagah4aaiajakal9Eam"
    "anaoapaqarasat9F50au9Navawa0a1a2a3a49uaya5ax9Gft9HaDaAbyaIaEaQ4pazaCaM4EaF9OaS4KaBaJ4CaNaR9D4baP51fwaHaT9XaL9Wfu9Y9PaKaafva64F9Za79V"
    "abac4Jb1a8aUb2b3b4b5b64Ib7b8b9babbbc4ZbdbebfaObgbDbtadbhbibw9IbjbzbkbublbmbBbnbCbxboaebpbAbqbraGbFbsbEbMbGc0bIbHbKbObRbUbXbJbZbLbNbP"
    "bQbSbTbVbWbYcdc1cuc3c4c6c2c5c7c9caccctc8cbcfcecgciclcochcjckcmcncpaVcHcvcVcwczcCcFcJcMcPcScxcycAcBcDcEcUcGcIcKcLcNd9cOcQcRcTcXd0d3d6"
    "dld8dbdecWcYcZd1d2d4cqd5d7dkdndqdadcdtdddfcrdsdydmdodvdxdpdgdrdudwdAcs54dzdCdBdhaW42hh44didD43dEdjaXfjdFfkdGdIdHdJdV41dKdL5f5edW5hdM"
    "5idX5gdNdYdZe0eokLene1lje8dOe3dP5je2eieddQe4eje9exeeaYe5eadRefdSdTe6eteuekdUfVebege7eleseceyehewemeDevezeqlkeCeAlieEeFaZeBeJeHeGeKeI"
    "f3epf4eLerf5f2b0eNf6ePf7eQf8ffeRf9eSfaeOfdfbeUeTeWfcfeeVeXeYeMfifgeZllflfmf0fnf1fofpfqfxfCg1fDfEfyfFfsg2g3g4g5g6g7log8g9gagblpgchngd"
    "gelsgfggghgilrfzfhfGgjgkfMgCfNfOgmfPfQfRgFfShkgnglgogpgqgugyfAgrgvfrgBgwgzgAfWgDgtfJfHfKfIfBgxfLgsfTgNhfgOgPgQgRgSgTfUgUgVgWgXgYgZgG"
    "h0h1h2hofXgEfYh4h6hgh8fZh3hahih7hlh9g0h5hphjhbhmlmhchdkPhrkQhehqhyhshMhuhvhxhthwhAhDhGhLhJhzhBhChEhFhHhIhKhZhNighPhQhShThVhOhRhWhYif"
    "hUhXi1i4i0i2i3i5i6i8i9ibi7iaitihiHijikiminipiqisiiilioiGiriviyiBiEiuiwixiziAiCiDiViFiJiMiPiSiUj7iIiKiLiNiOiQiRiTiXj6j0iciWiYiZj1j9jc"
    "jfjeidjkj8jajbjjjdjhjgj2jiiejmjljngHjoj3kMgIltjpj4gJjqj5kFjrkGjsjtkNgKlCjulykRjvjwjWgLjzjxjyk6jAjMjYjBjCjHjNjDjRjOgMjIjSjZjEjJjPjTjF"
    "jKjUk0jGjLjQk2jVjXkOk1kgkTk3k5kSk7k4kUk8k9kVkckakWkhkdkXkbkskjkikekYktknkrkklnkulxlqkvlvlzkwklkpkxkokmlukylAkzkqlwlDkAkEkfkBlBlEkZkH"
    "kIkJlHl0l1l2lIl3kKkClFlJlGl5lKl6l4l9lLl7l8lOlPlMlalNlblclUlQlRlSlVldlWlXlYlTlem0lZlfm1lglhm3m2kDm7m6m9m5mhmbmam4mdmcmimjmfm8memgmk")


def rank_program(g, core, T, topo):
    rank = T.rank_of(core)
    if rank is None:
        return
    NR = len(T.cores)
    Q = {"v": g.vector, "a": g.scalar, "t": g.tensor, "g": g, "s": g.sync}
    SEM = {"v": "cv", "a": "ca", "t": "ct", "g": "cg"}
    ops = []
    lw, lr = {}, {}
    bank = {}

    def width(n):
        w = 1
        for d in SCRATCH[n][1][1:]:
            w *= d
        return w

    def s(n, a=0, b=None, st=1):
        ar, o, z = OFF[n]
        b = z if b is None else b
        x = T[ar][:, o + a:o + b] if st == 1 else T[ar][:, o + a:o + b:st]
        return (x, [(ar, np.arange(o + a, o + b, st))])
    def row0(n, a, b, st=1):
        ar, o, z = OFF[n]
        x = T[ar][0:1, o + a:o + b] if st == 1 else T[ar][0:1, o + a:o + b:st]
        return (x, [(ar, np.arange(o + a, o + b, st))])
    def col(n, j): return s(n, j, j + 1)
    def P(b, a=0, e=512, st=1):
        n = "P%d" % b
        return (T[n][:, a:e] if st == 1 else T[n][:, a:e:st], [(n, np.arange(a, e, st))])
    def c3(n, i, a, b):
        ids = np.arange(256).reshape(8, 32)
        if i is None:
            return (T[n][:, :, a:b], [(n, ids[:, a:b].reshape(-1))])
        return (T[n][:, i, a:b], [(n, ids[i, a:b])])
    def ind(w, off): return (w[0].indirect(off[0]), w[1], off[1])
    def ap(x): return x[0] if isinstance(x, tuple) else x

    def add(q, fn, r, w, kind="c", sem=None):
        i = len(ops)
        pre = set()
        rd = []
        for x in r:
            if isinstance(x, tuple):
                rd += x[1] + (x[2] if len(x) > 2 else [])
        wt = []
        for x in w:
            wt += x[1]
            rd += x[2] if len(x) > 2 else []
        for n, c in rd + wt:
            if n not in lw:
                lw[n] = np.full(width(n), -1); lr[n] = {}
        for n, c in rd + wt:
            pre.update(int(j) for j in np.unique(lw[n][c]) if j >= 0)
        for n, c in wt:
            pre.update(j for j, a in lr[n].items() if a[c].any())
        for n, c in rd + wt:
            if n[0] == "P":
                for k, js in bank.setdefault(n, {}).items():
                    if k != q or q == "t":
                        pre.update(js)
        for n, c in rd + wt:
            if n[0] == "P":
                bank[n] = {"t": [i]} if q == "t" else dict(bank[n], **{q: bank[n].get(q, []) + [i]})
        for n, c in wt:
            lw[n][c] = i
            for j in list(lr[n]):
                lr[n][j][c] = False
                if not lr[n][j].any(): del lr[n][j]
        for n, c in rd:
            if i not in lr[n]: lr[n][i] = np.zeros(width(n), bool)
            lr[n][i][c] = True
        pre.discard(i)
        ops.append([q, fn, sorted(pre), kind, sem])

    V = g.vector
    def cp(o, i): add("v", lambda: V.tensor_copy(o[0], i[0]), [i], [o])
    def tt(o, a, b, f): add("v", lambda: V.tensor_tensor(o[0], a[0], b[0], f), [a, b], [o])
    def ts(o, a, s1, f): add("v", lambda: V.tensor_scalar(o[0], a[0], ap(s1), None, f), [a, s1], [o])
    def t2(o, a, s1, f, s2, f2): add("v", lambda: V.tensor_scalar(o[0], a[0], ap(s1), ap(s2), f, f2), [a, s1, s2], [o])
    def red(o, a, f): add("v", lambda: V.tensor_reduce(o[0], a[0], AxisListType.X, f), [a], [o])
    def scan(o, a, b, ini, f, f2): add("v", lambda: V.tensor_tensor_scan(o[0], a[0], b[0], ini, f, f2), [a, b], [o])
    def ms(o, c): add("v", lambda: V.memset(o[0], c), [], [o])
    def act(o, i, f=AF.Identity, **kw):
        add("a", lambda: g.scalar.activation(o[0], i[0], f, **{k: ap(x) for k, x in kw.items()}), [i] + list(kw.values()), [o])
    def mm(o, l, rh, st, sp): add("t", lambda: g.tensor.matmul(o[0], l[0], rh[0], st, sp), [l, rh], [o])
    def io_(o, pat, base, cm=0):
        if o[1][0][0] == "I":
            add("g", lambda: g.iota(o[0], pat, base, cm), [], [o])
        else:
            add("g", lambda: g.iota(o[0], pat, base, cm, allow_small_or_imprecise_dtypes=True), [], [o])
    def fill(o, c): io_(o, [[0, len(o[1][0][1])]], c)
    def dma(q, o, i, sem, r=(), w=()): add(q, lambda: Q[q].dma_start(o, i), list(r), list(w), "d", sem)
    eng = [e for e in topo.engines(T.cores[0], T.cores[1])
           if all(e in topo.engines(a, b) for a in T.cores for b in T.cores if a != b)]
    emask = sum(1 << e for e in eng)
    def send(dst, o, i, sem):
        rid, pid, _e = topo.addr(dst)
        add("g", lambda: g.remote_dma(o[0], i[0], T.sem[sem], T.sem.ls, pid, rid, emask), [i], [], "r", "ls")
        add("x", None, [], [o], "x", sem)

    def victim(t): return T.cores[(rank + 1 + t % (NR - 1)) % NR]
    def attacker(t): return T.cores[(rank - 1 - t % (NR - 1)) % NR]
    def cw(n): return col("cw", 16 * CN.index(n) + 15)
    def dg(n): k = DN.index(n); return s("dg", 128 * k, 128 * k + 128)
    def C(t, k): return s("C%d" % t, 64 * k, 64 * k + 64)
    def R(t, k):
        return s("R%d" % t, 64 * k, 64 * k + 64) if k < 2 else s("dl%d" % t, 128, 192)
    def dl(t): return s("dl%d" % t, 64, 128)

    dma("s", s("oc")[0], T.oc[:], "loc", w=[s("oc")])
    dma("a", s("xc_", 16, 16 + U // 2)[0], T.x[:, 0:U // 2], "lx0", w=[s("xc_", 16, 16 + U // 2)])
    dma("s", s("xc_", 16 + U // 2, 16 + U)[0], T.x[:, U // 2:U], "lx1", w=[s("xc_", 16 + U // 2, 16 + U)])
    dma("s", s("cd")[0], T.cd[:], "lcd", w=[s("cd")])

    HW = 336
    ms(s("ones"), 1.0)
    ms(s("rt", 0, 16 * NE), 0.0)
    ms(s("rt", 16 * NE, 16 * NC_), 0.0)
    io_(col("pi", 0), [[0, 1]], 0, 1)
    io_(s("pat"), [[0, 16], [1, 16]], 0)
    io_(s("x144"), [[1, 144]], 0)
    io_(s("pt", 0, HW), [[0, 16], [1, 21]], 0)
    io_(s("pt", HW, 2 * HW), [[0, 8], [-1, 2], [0, 21]], 1)
    io_(s("pt", 2 * HW, 3 * HW), [[1, 8], [0, 42]], 0)
    if "runs" not in MEMO:
        MEMO["runs"] = []
        for a, b in ((0, NE), (NE, NC_)):
            todo = {16 * k + f: c for k in range(a, b) for f, c in COLS[CN[k]].items()}
            while todo:
                run = max(([p0 + d * i for i in range(m)] for p0 in sorted(todo) for d in range(1, 16 * (b - a)) for m in (6, 5, 4, 3, 2, 1)
                           if all(todo.get(p0 + d * i) == todo[p0] for i in range(m))), key=len)
                MEMO["runs"].append((run, float(todo[run[0]])))
                for p0 in run: del todo[p0]
    for k, (run, c) in enumerate(MEMO["runs"]):
        o = s("rt", run[0], run[-1] + 1, run[1] - run[0] if len(run) > 1 else 1)
        if k % 6 == 5: ms(o, c)
        else: act(o, s("ones", 0, len(run)), scale=c)
    ts(col("pi", 1), col("pi", 0), 15, A.bitwise_and)
    ts(col("pi", 2), col("pi", 0), 4, A.arith_shift_right)
    ts(col("pi", 3), col("pi", 0), 1, A.bitwise_and)
    cp(s("pcol", 0, 4), s("pi"))
    rc, gc_, pc = col("pcol", 1), col("pcol", 2), col("pcol", 0)
    cp(s("ocu"), s("oc"))
    ts(s("r16", 0, 256), s("pat"), rc, A.is_equal)
    cp(s("r16", 256, 272), s("r16", 0, 16))
    ts(s("sgm"), s("pat"), 0.5, A.is_gt)
    ts(s("g8"), s("x144", 0, 8), gc_, A.is_equal)
    ts(s("idb"), s("x144", 0, 128), pc, A.is_equal)
    t2(s("nid"), s("x144", 0, 128), pc, A.is_equal, -1.0, A.mult)
    cp(P(6, 0, 208), s("r16", 0, 208))
    for a, b in ((0, NE), (NE, NE + 12), (NE + 12, NC_)):
        tt(s("seg", 16 * a, 16 * b), P(6, 0, 16 * (b - a)), s("rt", 16 * a, 16 * b), A.mult)
        scan(s("cw", 16 * a, 16 * b), s("sgm", 0, 16 * (b - a)), s("seg", 16 * a, 16 * b), 0.0, A.mult, A.add)
    ms(s("fR"), 0.0); ms(s("fL"), 0.0); ms(s("fZ"), 0.0)
    for n, fs in (("fR", (1, 9)), ("fL", (0, 8)), ("fZ", (2,))):
        for f in fs:
            act(s(n, f, 128, 16), s("g8"))
    for k, n in enumerate(("s_i", "s_e", "s_j")):
        act(s("ds", 128 * k, 128 * k + 128), s("idb"), scale=cw(n))
    t2(s("sb"), s("x144", 0, 64, 8), cw("s_j"), A.mult, cw("s_c"), A.add)
    for k in range(3):
        mm(P(7, 0, HW), s("ds", 128 * k, 128 * k + 128), s("pt", HW * k, HW * k + HW), k == 0, k == 2)
    act(s("cp2", 0, HW), P(7, 0, HW)); act(s("cp2", HW, 2 * HW), P(7, 0, HW))
    ms(s("ad", 0, 16), 0.0); ms(s("xc_", 0, 16), 0.0); ms(s("stat", 0, 16), 100.0)
    t2(col("pcol", 4), gc_, 16.0, A.mult, 15.0, A.add)
    t2(col("pcol", 5), col("pcol", 3), -2048.0, A.mult, 2048.0, A.add)
    ts(col("pcol", 7), rc, 42.0, A.mult)
    t2(s("qz"), s("x144"), col("pcol", 4), A.is_equal, 61.0, A.mult)
    cp(s("l_rep"), s("x144", 0, 8))

    xw = s("xc_", 16, 16 + U)
    for c, (a, b) in enumerate(((0, 22), (22, 42), (42, 84), (84, 126), (126, 146), (146, 168))):
        (cp if c in (0, 2, 3) else act)(s("xb_", 16 * a, 16 * b), ind(xw, s("ocu", a, b)))
    act(s("eo0", 0, 128, 2), s("xb_", 0, U, 42))
    act(s("eo0", 1, 128, 2), s("xb_", 20, U, 42))
    send(victim(0), s("el0", 128, 256), s("eo0"), "ae0")
    for h in range(8):
        lo = max(HW * h, 1); hi = HW * h + HW; b = (0, 1, 4)[h % 3]
        mm(P(b, 0, hi - lo), s("idb"), s("xb_", lo, hi), True, False)
        mm(P(b, 0, hi - lo), s("nid"), s("xb_", lo - 1, hi - 1), False, True)
        act(s("ad", 15 + lo, 15 + hi), P(b, 0, hi - lo), AF.Abs)
        lo = HW * h; b = (2, 3, 5)[h % 3]
        mm(P(b, 0, HW), s("fZ"), s("xb_", lo, hi), True, False)
        mm(P(b, 0, HW - 1), s("fR"), s("ad", 16 + lo, 15 + hi), False, False)
        mm(P(b, 0, HW), s("fL"), s("ad", 15 + lo, 15 + hi), False, True)
        act(s("spos", lo, hi), P(b, 0, HW), bias=col("sb", h))
        if h % 2:
            for a, b in ((0, 20), (20, 42)):
                o = 42 * (h // 2)
                tt(ind(s("stat", 16, 16 + U), s("ocu", o + a, o + b)), s("spos", 16 * (o + a), 16 * (o + b)), s("cp2", 16 * a, 16 * b), A.add)
    for kh in range(2):
        for j1 in range(2):
            k = 2 * kh + j1
            add("g", lambda k=k, kh=kh, j1=j1: g.affine_select(
                s("pm", 128 * k, 128 * k + 128)[0], s("ones")[0], [[32, 4], [1000 - 2000 * j1, 2], [2, 16]], A.is_equal, 0.0,
                kh + 1000 * j1, -1), [s("ones")], [s("pm", 128 * k, 128 * k + 128)])
    cp(s("cdf"), s("cd"))
    add("v", lambda: V.transpose(s("cdt")[0], s("cdf")[0]), [s("cdf")], [s("cdt")])
    act(c3("TR", None, 0, 32), s("cdt"))
    for k in range(4):
        mm(P(7, 128 * (k // 2), 128 * (k // 2) + 128), s("pm", 128 * k, 128 * k + 128), c3("TR", None, 16 * (k % 2), 16 * (k % 2) + 16), k % 2 == 0, k % 2 == 1)
    for kh in range(2):
        act(c3("CT", None, 16 * kh, 16 * kh + 16), P(7, 128 * kh, 128 * kh + 128))
    act(col("cw", 0), col("r16", 15), scale=-M26, bias=cw("hL")); act(col("cw", 1), col("r16", 15), scale=-M26, bias=cw("hR"))
    for lr_ in range(2):
        act(s("wf", lr_, 16, 2), s("g8"), scale=2 * H16)
        act(s("wa", lr_, 16, 2), s("g8"), scale=cw(("aL", "aR")[lr_]))
        act(s("wh1", lr_, 16, 2), s("g8"), scale=cw(("hL", "hR")[lr_]))
        act(s("wh2", lr_, 16, 2), s("g8"), scale=col("cw", lr_))
        act(s("wz", lr_, 16, 2), s("g8"), scale=col("r16", 4 + lr_))
    K0 = (0, NK[0], NK[0] + NK[1])
    for b in range(3):
        nk = NK[b]
        io_(s("wc", 512 * b, 512 * b + 16 * nk), [[0, 8], [1024, 2], [-2048, nk]], (31 - K0[b]) * 2048)
    for b in (0, 2):
        nk = NK[b]; a = 128 * b; e = a + 16 * nk
        io_(s("gp", a, e), [[1, 8], [0, 2 * nk]], 0)
        t2(s("w0", a, e), s("gp", a, e), gc_, A.is_equal, -H16, A.mult)
        act(s("w1", a, e), s("w0", a, e), scale=-1.0 / H16)
        io_(s("sm", a, e), [[0, 8], [1, 2 * nk]], 0)
        act(s("sm", a, e), s("sm", a, e), AF.Sign)
    act(s("onb"), s("ones")); act(s("idf"), s("idb")); act(s("nM"), s("idb"), scale=-M26)
    io_(s("gid"), [[1, 8], [0, 16]], 0)
    ts(s("bo"), s("gid"), gc_, A.is_equal)
    act(s("bo6"), s("bo"), scale=1.0 / 64); act(s("nb6"), s("bo"), scale=-1.0 / 64)
    for n, w, c in (("i_k", "idb", cw("i_k")), ("i_b", "idb", cw("n_b")), ("i_as", "idb", cw("n_s")), ("i_la", "idb", col("r16", 4)),
                    ("i_j", "idb", col("r16", 3)), ("i_one", "idb", cw("i_one")), ("i_na", "idb", cw("i_na")), ("i_e", "idb", col("r16", 0)),
                    ("mix", "idb", cw("m_d")), ("m_n", "nid", cw("mDe")), ("m_p", "idb", cw("mDe")), ("d_l", "bo", cw("d_l")),
                    ("d_r", "bo", cw("d_r")), ("c_l", "idb", cw("c_l")), ("c_r", "idb", cw("c_r"))):
        act(dg(n), s(w), scale=c)
    for f, n in ((12, "m_l"), (13, "m_e"), (14, "m_r")):
        act(s("dg", 128 * DN.index("mix") + f, 128 * DN.index("mix") + 128, 16), s("g8"), scale=cw(n))
    fill(dg("e_1"), 0); act(s("dg", 128 * DN.index("e_1"), 128 * DN.index("e_1") + 128, 16), s("g8"), scale=col("r16", 11))
    act(s("g8n"), s("g8"), scale=-128.0); act(col("pcol", 6), rc, bias=31 * 128.0)
    for k, c in enumerate((cw("r_s"), col("r16", 10), cw("r_n"))):
        act(s("rs", 128 * k, 128 * k + 128), s("bo"), scale=c)
    io_(s("xt", 0, 68), [[1, 17], [672, 4]], 21)
    io_(s("xt", 68, 136), [[-1, 17], [672, 4]], 41)
    io_(s("jc"), [[-32, 64]], 127 * 32)
    io_(s("j256"), [[1, 64]], 1100)
    io_(s("j32"), [[1, 64]], 0)
    io_(s("c8"), [[1088, 2], [16, 4]], 0)
    io_(s("jb"), [[1, 64]], 0)
    fill(s("tq", 64, 320, 80), 32768)
    io_(s("kkw"), [[16, 16]], 0)
    fill(s("XV", 16 * 116, XVN + 16), 0); fill(s("XV", 16 * 48, 16 * 68), 0); fill(s("lr"), 21); fill(s("mo", 64, 80), 100)
    for a in range(0, 1184, 296): fill(s("sw", a, a + 296), 2 ** 23)
    io_(s("kb"), [[1, 256]], 0)
    io_(s("c21w"), [[21, 2], [672, 4]], 0)
    io_(s("xP", 0, 68), [[1, 17], [0, 4]], 0)
    io_(s("y1"), [[1, 17], [0, 4]], 1)
    io_(s("c21"), [[21, 2], [42, 64]], 0)
    fill(s("T1", 0, 16), 100); fill(s("T2", 0, 16), 100); fill(s("T2", 16 + U, 16 + U + 256), 100)
    fill(s("dl0", 0, 64), 128); fill(s("dy2", 64, 128), 0); fill(s("xb_", ZC, ZC + 16), 0); fill(s("xb_", Z1 - 64, Z1), 0)
    fill(s("numb", ZC, ZC + 16), -1); fill(s("nad", 0, 16), 0); fill(s("nad", 256, 272), 0)
    fill(s("xa", 0, 4), 21); fill(s("xa", 4, 8), 0); fill(s("xa", 8, 12), -21); fill(s("xe_"), 20); fill(s("xh"), TH - 4096 * 21)
    for a in range(0, U, 384): fill(s("numb", a, a + 384), 0)
    for t in range(RO - 1): io_(s("numb", U + NS * t, U + NS * t + NS), [[1, NS]], U + NEWC * t)
    io_(s("numb", Z1, ZC), [[1, NEWC]], U + 2 * NEWC)
    act(s("vq"), s("x144", 0, 64, 16), bias=rc)
    act(s("xu"), s("xt"), bias=col("pcol", 7))
    act(s("kkw"), s("kkw"), bias=rc)
    act(s("j32"), s("j32"), scale=-32768.0, bias=63 * 32768.0)
    act(s("c8"), s("c8"), bias=rc)
    fill(s("m64"), -64)
    act(s("q1"), s("qz"), AF.Sign)
    act(s("cap"), s("r16", 1, 257), scale=-2e9, bias=1e9)
    act(s("q14"), s("q1"), scale=cw("q_c"))
    act(s("q16"), s("q1"), scale=1.0 / 16)
    act(s("c21w"), s("c21w"), bias=col("pcol", 7))
    tt(s("j256"), s("j256"), s("r16", 0, 64), A.mult)
    for k, (m, b) in enumerate(((1, 0), (1, U + NS - 1), (1, Z1 - 1), (4096, TH), (8192, 4096), (-2, -1))):
        act(s("bc", 2 * k, 2 * k + 2), s("kkw", 0, 2), scale=float(m), bias=float(b))
    dma("g", s("ad", 16, 16 + U)[0], s("stat", 16, 16 + U)[0], "lc", r=[s("stat", 16, 16 + U)], w=[s("ad", 16, 16 + U)])
    for r in range(16):
        mm(P(7, 0, 168), s("q14", 15 - r, 143 - r), s("ad", 16 + r, 16 + U, 16), r == 0, r == 15)
    cp(s("cl"), P(7, 0, 168))
    fill(s("op_"), 0)
    for u in range(6): cp(s("op_", 32 * u, 32 * u + 28), s("oc", u, 168, 6))
    tt3 = (T.TT[:, :, :], [("TT", np.arange(192))])
    add("v", lambda: V.transpose(s("ot")[0], s("op_")[0]), [s("op_")], [s("ot")])
    act(tt3, s("ot"))

    cp(P(5, 448, 512), s("jc"))
    for t in range(RO):
        lim = U + NEWC * t
        el = "el%d" % t
        tab = "stat" if t == 0 else "T%d" % t
        if t > 0:
            z0 = U + NS * (t - 1); n0 = 16 + lim - NEWC
            if t == 1:
                win = s("dl0", 0, 128)
            else:
                tt(s("dy2", 0, 64), dl(1), s("cut"), A.add)
                win = s("dy2")
            for a in range(0, 168, 42):
                tt(s(tab, 16 + 16 * a, 16 + 16 * a + 672), ind(win, s("cl", a, a + 42)), s("stat", 16 + 16 * a, 16 + 16 * a + 672), A.add)
            for k in range(3):
                mm(P(4, 64 * k, 64 * k + 64), s("rs", 128 * k, 128 * k + 128), dl(t - 1), True, True)
            act(s("R%d" % (t - 1), 0, 128), P(4, 0, 128))
            act(s("na"), P(4, 128, 192), bias=1.0)
            act(s("xc_", n0, n0 + 256), s("xb_", z0, z0 + 256))
            cp(s("wl_"), s("xb_", z0 + 256, z0 + 272))
            mm(P(3, 0, 255), s("idb"), s("xb_", z0 + 1, z0 + 256), True, False)
            mm(P(3, 0, 255), s("nid"), s("xb_", z0, z0 + 255), False, True)
            act(s("nad", 1, 256), P(3, 0, 255), AF.Abs)
            lst = [("i_as", R(t - 1, 0)), ("i_la", s("lr") if t == 1 else s("cb", 128, 192)), ("i_j", s("jb")), ("i_one", s("onb", 0, 64)),
                   ("i_na", s("na")), ("i_b", R(t - 1, 2)), ("i_e", s("xb_", z0 + 272, z0 + 336)) if t == 1 else ("e_1", dl(1))]
            for k, (w, x) in enumerate(lst):
                mm(P(4, 192, 256), dg(w), x, k == 0, k == len(lst) - 1)
            act(s("mo", 0, 64), P(4, 192, 256))
            act(s("ifl"), ind(s("mo"), s("wl_")))
            mm(P(7, 256, 512), dg("i_k"), s("kb"), True, False)
            mm(P(7, 256, 512), s("fZ"), s("xb_", z0, z0 + 256), False, False)
            mm(P(7, 256, 512), s("fL"), s("nad", 0, 256), False, False)
            mm(P(7, 256, 512), s("fR"), s("nad", 1, 257), False, False)
            mm(P(7, 256, 512), dg("mix"), s("ifl"), False, True)
            act(s(tab, n0, n0 + 256), P(7, 256, 512))
            act(s("R%d" % (t - 1), 128, 192), R(t - 1, 2))
            for r in range(16):
                mm(P(1, 256, 268), s("q16", 15 - r, 143 - r), s("R%d" % (t - 1), r, 192, 16), r == 0, False)
            mm(P(1, 256, 268), s("idb"), s("xa"), False, True)
            act(s("wr", 0, 8), P(1, 256, 264)); act(s("xd"), P(1, 264, 268), bias=float(z0 - 1))
            act(s("xf"), s("wr", 4, 8), scale=-2.0, bias=1.0)
            for q in range(4):
                act(col("xi", q), col("xe_", q), scale=col("wr", 4 + q), bias=col("c21w" if t == 1 else "xb", q))
            for q in range(4):
                act(s("xP", 68 + q, 136, 4), s("y1", q, 68, 4), scale=-1.0, bias=col("wr", q))
                act(s("xm", q, 136, 4), s("xP", q, 136, 4), scale=4096.0, bias=col("xh", q))
                act(s("xt", q, 136, 4), s("xP", q, 136, 4), scale=col("xf", q), bias=col("xi", q))
                act(s("xu", q, 136, 4), s("xP", q, 136, 4), bias=col("xd", q))
            tt(P(5, 0, 136), s("xm"), s("xu"), A.min)
            tt(P(5, 0, 136), P(5, 0, 136), s("xt"), A.max)
            t2(s("l_xv"), P(5, 0, 136), 0.0, A.max, float(z0 + 255), A.min)
        else:
            cp(s("l_xv"), s("xu"))
        for a, b in (((0, 24), (24, 48), (68, 92), (92, 116)) if t == 0 else ((0, 34), (34, 68), (68, 102), (102, 136))):
            act(s("XV", 16 * a, 16 * b), ind(s("xb_", 0, U + NS * t), s("l_xv", a, b)))
        for r in range(16):
            mm(P(6, 0, 8), s("qz", 15 - r, 143 - r), s(el, 128 + r, 256, 16), r == 0, r == 15)
        for B in range(8):
            t2(s("mi", B, 256, 8), c3("CT", B, 0, 32), P(6, B, B + 1), A.add, float(4096 - lim), A.add)
        for a, b in ((0, 48), (48, 256)):
            ts(s("mj", a, b), s("mi", a, b), 4095, A.bitwise_and)
            t2(s("ml", a, b), s("mj", a, b), float(4096 - lim - 16), A.subtract, 0.0, A.max)
        act(s(el, 256, 384), s(el, 128, 256)); act(s(el, 384, 640), s(el, 128, 384))
        for b in range(3):
            nk = NK[b]; o = 256 * (b // 2)
            mm(P(b, 0, 16 * nk), row0("onb", 0, 128), row0("wc", 512 * b, 512 * b + 16 * nk), True, False)
            mm(P(b, 0, 16 * nk), s(el, 128, 256), s("w0", o, o + 16 * nk), False, False)
            if t > 0:
                mm(P(ZB[b], 0, 16 * nk), s(el, 0, 128), s("w1", o, o + 16 * nk), True, False)
        for c in range(len(CB) - 1):
            a, e = 128 * CB[c], 128 * CB[c + 1]
            tt(s("MN", a, e), ind(s("xc_", 0, 16 + lim), s("ml", a // 16, e // 16)), s(el, 128, 128 + e - a), A.min)
            if CB[c] in CG:
                e2 = 128 * CG[CG.index(CB[c]) + 1]
                act(s("G", a, e2), ind(s(tab, 0, 16 + lim), s("ml", a // 16, e2 // 16)), AF.Relu)
            for k in range(CB[c], CB[c + 1]):
                b = 0 if k < K0[1] else (1 if k < K0[2] else 2)
                nk = NK[b]; last = k - K0[b] == nk - 1
                o = P(b, k - K0[b], 16 * nk, nk)
                mm(o, s("MN", 128 * k, 128 * k + 128), s("wf"), False, False)
                if t == 0:
                    mm(o, s("G", 128 * k, 128 * k + 128), s("wa"), False, last)
                else:
                    mm(P(ZB[b], k - K0[b], 16 * nk, nk), s("G", 128 * k, 128 * k + 128), s("wz"), False, last)
                    mm(o, s("G", 128 * k, 128 * k + 128), s("wh%d" % t), False, False)
                if last:
                    o = 256 * (b // 2)
                    if t > 0:
                        act(s("zb", 256 * b, 256 * b + 16 * nk), P(ZB[b], 0, 16 * nk), AF.Relu, bias=-31.0)
                        mm(P(b, 0, 16 * nk), s("nM"), s("zb", 256 * b, 256 * b + 16 * nk), False, True)
                    scan(s("ks", 256 * b, 256 * b + 16 * nk), s("sm", o, o + 16 * nk), P(b, 0, 16 * nk), 0.0, A.mult, A.max)
                    if b == 1:
                        tt(s("red"), s("ks", 2 * nk - 1, 16 * nk, 2 * nk), s("ks", 256 + 2 * nk - 1, 256 + 16 * nk, 2 * nk), A.max)
        if t == 0:
            o = OFF["numb"][1]
            for k in range(8):
                dma("s", T.F[16 * k:16 * k + 1, o:o + U], T.TT[32 * (k // 2):32 * (k // 2) + 28, :, 16 * (k % 2):16 * (k % 2) + 16],
                    "ln%d" % k, r=[tt3, s("MN", 0, 16)], w=[s("numb", k, U, 8)])
        tt(s("ri"), s("red"), s("ks", 512 + 2 * nk - 1, 512 + 16 * nk, 2 * nk), A.max)
        ts(s("rj"), s("ri"), 0xFF07FF, A.bitwise_and)
        ts(s("rep"), ind(s("rj"), s("l_rep")), col("pcol", 5), A.add)
        if t == 1:
            t2(s("rk"), s("ri"), 11, A.logical_shift_right, 31, A.bitwise_and)
            tt(s("g2"), ind(s("rk"), s("l_rep")), s("r16", 0, 128), A.mult)
            mm(P(6, 64, 72), s("g2"), s("g8n"), True, False)
            mm(P(6, 64, 72), row0("onb", 0, 128), row0("kb", 0, 128, 16), False, True)
            ts(s("l_p0"), P(6, 64, 72), col("pcol", 6), A.add)
            act(s("ex"), ind(s("G"), s("l_p0")))
            mm(P(7, 0, 128), dg("d_l"), s("ex"), True, True); mm(P(7, 128, 256), dg("d_r"), s("ex"), True, True)
            act(s("ifl"), P(7, 0, 256), AF.Relu)
            for k, (w, a) in enumerate((("m_p", 0), ("m_p", 128), ("m_n", 1), ("m_n", 129))):
                mm(P(6, 128, 192), dg(w), s("ifl", a, 128 + a - a % 2, 2), k == 0, k == 3)
        add("t", lambda: g.tensor.transpose(P(3, 0, 128)[0], s("rep")[0], s("idf")[0]), [s("rep"), s("idf")], [P(3, 0, 128)])
        cp(s("he"), P(3, 0, 128, 2))
        tt(s("Hi"), P(3, 1, 128, 2), s("he"), A.max)
        Hi = s("Hi")
        ts(s("vf"), Hi, 63, A.bitwise_and)
        t2(s("dm"), Hi, 6, A.logical_shift_right, 31, A.bitwise_and)
        ts(s("g16"), Hi, 0xFF0000, A.bitwise_and)
        tt(P(5, 64, 128), s("g16"), P(5, 448, 512), A.add)
        tt(P(5, 0, 64), P(5, 64, 128), s("dm"), A.add)
        for q in range(4):
            ts(s("tq", 80 * q, 80 * q + 64), s("vf"), col("vq", q), A.is_equal)
            tt(s("tq", 80 * q, 80 * q + 64), s("tq", 80 * q, 80 * q + 64), P(5, 0, 64), A.mult)
            red(col("best", q), s("tq", 80 * q, 80 * q + 65), A.max)
            ts(s("W", 64 * q, 64 * q + 64), s("tq", 80 * q, 80 * q + 64), col("best", q), A.is_equal)
            mm(P(4, 0, 64), s("bo"), s("W", 64 * q, 64 * q + 64), q == 0, q == 3)
        t2(s("mu"), Hi, 6, A.logical_shift_right, 15, A.bitwise_and)
        t2(s("hd"), Hi, 11, A.logical_shift_right, 1, A.bitwise_and)
        ts(s("pl"), Hi, 2047, A.bitwise_and)
        t2(s("d64"), Hi, 4, A.logical_shift_right, 64, A.bitwise_and)
        tt(P(5, 128, 192), s("pl"), s("d64"), A.add)
        po = "po%d" % t
        if t == 1:
            ts(s("q_gn"), s("g16"), 1.0 / H16, A.mult)
            for k, (w, x) in enumerate((("m_p", s("ifl", 1, 128, 2)), ("m_p", s("ifl", 129, 256, 2)), ("m_n", s("q_gn")))):
                mm(P(3, 128, 192), dg(w), x, k == 0, k == 2)
        if t == 0:
            tt(s("mm"), P(5, 128, 192), s("r16", 0, 64), A.mult)
            scan(s("ms"), s("sgm", 0, 64), s("mm"), 0.0, A.mult, A.add)
            cp(s("l_p0", 0, 4), s("ms", 15, 64, 16))
            ts(s("l_p0", 4, 8), s("ms", 15, 64, 16), 64.0, A.add)
            ts(s("q_gn"), s("g16"), 1.0 / H16, A.mult)
            act(s("g2"), ind(s("XV", 0, XVN + 16), s("l_p0")))
            mm(P(6, 64, 128), s("idb"), s("g2", 0, 64), True, False)
            mm(P(6, 64, 128), s("nid"), s("g2", 64, 128), False, True)
            act(s("g2a"), P(6, 64, 128), AF.Abs)
            mm(P(6, 128, 192), s("bo"), s("g2a"), True, False)
            mm(P(6, 128, 192), s("nid"), s("q_gn"), False, True)
            act(s(po, 272, 336), P(6, 128, 192))
        t2(s("U1"), s("mu"), cw("ua1"), A.mult, cw("ub1"), A.add)
        if t == 1:
            t2(s("wm"), s("mu"), cw("ua2"), A.mult, cw("ub2"), A.add)
            tt(P(5, 192, 256), P(6, 128, 192), s("wm"), A.add)
        else:
            t2(P(5, 192, 256), s("mu"), cw("ua2"), A.mult, cw("ub2"), A.add)
        tt(P(5, 192, 256), P(5, 192, 256), s("hd"), A.mult)
        tt(s("U1"), P(5, 192, 256), s("U1"), A.add)
        if t == 1: tt(s("U1"), P(3, 128, 192), s("U1"), A.add)
        tt(s("wm"), P(4, 0, 64), s("mu"), A.mult)
        ts(s("U5"), s("mu"), 2048.0, A.add)
        tt(s("o1"), P(4, 0, 64), s("U5"), A.mult)
        scan(P(5, 256, 320), P(4, 0, 64), s("wm"), 2048.0, A.add, A.add)
        tt(P(5, 192, 256), P(4, 0, 64), s("U1"), A.mult)
        ts(s("ac0"), P(5, 256, 320), 2304.5, A.is_lt)
        mo = "mo%d" % t
        tt(s(mo, 0, 64), P(5, 192, 256), s("ac0"), A.mult)
        tt(P(5, 384, 448), P(5, 256, 320), s("o1"), A.subtract)
        ts(s(mo, 64, 128), P(5, 384, 448), 256.0, A.min)
        send(attacker(t), s("dl%d" % t, 64, 192), s(mo), "ad%d" % t)
        e8 = "e8%d" % t
        cp(s("bi"), s("best"))
        t2(s("bx"), s("bi"), 5, A.logical_shift_right, 127, A.bitwise_and)
        ts(s("bm"), s("bi"), 15, A.bitwise_and)
        t2(s("bd"), s("bi"), 4, A.logical_shift_right, 1, A.bitwise_and)
        t2(s("vm"), s("bm"), 64.0, A.mult, 64.0, A.add)
        tt(s("et", 4, 8), s("vm"), s("bd"), A.mult)
        tt(s("et", 0, 4), s("vm"), s("et", 4, 8), A.subtract)
        red(col("cnt", 0), s("ac0"), A.add)
        for a in (0, 4):
            t2(s("vx", a, a + 4), s("bx"), col("cnt", 0), A.add, 127.5, A.is_gt)
        tt(s(e8), s("et"), s("vx"), A.mult)
        if t < RO - 1:
            eo = "eo%d" % (t + 1)
            tt(s("e8i"), s(e8), s("c8"), A.add)
            cp(s("l_end"), s("e8i"))
            act(s(eo, 128, 256, 2), ind(s("XV", 0, XVN), s("l_end", 0, 4)))
            act(s(eo, 129, 256, 2), ind(s("XV", 0, XVN), s("l_end", 4, 8)))
            if t == 0: tt(s("cs"), s(e8, 0, 4), s(e8, 4, 8), A.add)
        tt(s("val"), P(5, 128, 192), s("j32"), A.add)
        tt(s("mm"), P(5, 384, 448), s("j256"), A.min)
        scan(s("ms"), s("sgm", 0, 64), s("mm"), 0.0, A.mult, A.add)
        cp(s("l_off"), s("ms", 15, 64, 16))
        cp(ind(s("sw"), s("l_off")), s("val"))
        scan(s("Fs"), s("m64"), s("sw", 1, 257), 63 * 32768.0 + 20000, A.add, A.min)
        scan(s("F2"), s("Fs"), s("cap"), -1e9, A.max, A.min)
        tt(s("Fw"), s("F2", 14, 256, 16), s("F2", 15, 256, 16), A.max)
        ts(s("cc"), s("Fw"), 32767, A.bitwise_and)
        ts(s("l_pos"), s("cc"), float(XVN - 1), A.min)
        act(s(po, 0, 256), ind(s("XV", 0, XVN), s("l_pos")))
        if t < RO - 1:
            ts(s("ww"), s("Fw"), 15, A.arith_shift_right)
            t2(s(po, 256, 272), s("ww"), -1.0, A.mult, 63.0, A.add)
            fill(s("sw", 0, 272), 2 ** 23)
        send(attacker(t), s("xb_", U + NS * t, U + NS * t + OFF[po][2]), s(po), "ap%d" % t)
        tt(s("ex"), ind(s(e8), s("l_rep")), s("r16", 0, 128), A.mult)
        mm(P(2, 320, 384), s("idb"), s("lr") if t < 2 else s("cb", 128, 192), True, False)
        if t > 0: mm(P(2, 320, 384), s("idb"), R(t - 1, 0), False, False)
        mm(P(2, 320, 384), s("nb6"), s("ex", 0, 64), False, False)
        mm(P(2, 320, 384), s("nb6"), s("ex", 64, 128), False, True)
        mm(P(2, 192, 320), s("bo6"), s("ex"), True, True)
        if t < RO - 1:
            act(s(eo, 0, 128, 2), P(2, 320, 384), scale=1.0 / 16); act(s(eo, 1, 128, 2), P(2, 320, 384), scale=1.0 / 16)
            send(victim(t + 1), s("el%d" % (t + 1), 0, 256), s(eo), "ae%d" % (t + 1))
        act(s("C%d" % t), P(2, 192, 384))
        if t == 0:
            act(s("cb"), P(2, 192, 384))
            mm(P(2, 384, 448), dg("c_l"), s("cb", 0, 64), True, False)
            mm(P(2, 384, 448), dg("c_r"), s("cb", 64, 128), False, True)
            act(s("cut"), P(2, 384, 448))
            act(s("La2"), s("cs"), scale=-1.0 / 64, bias=21.0)
            act(s("xb"), s(e8, 0, 4), scale=1.0 / 64)
            tt(s("xb"), s("xb"), s("c21w", 4, 8), A.add)
        if t == 1:
            act(s("xa", 0, 4), s("La2")); act(s("xa", 8, 12), s("La2"), scale=-1.0)
            act(s("xe_"), s("La2"), bias=-1.0)
            act(s("xh"), s("La2"), scale=-4096.0, bias=float(TH))

    def h(n, ih): return s(n, 64 * ih, 64 * ih + 64)
    def p5(a, ih): return P(5, a + 64 * ih, a + 64 * ih + 64)
    def bc(k, ih): return col("bc", 2 * k + ih)
    act(s("gb"), C(0, 2), bias=-1.0)
    act(s("ga"), R(1, 1), scale=-2.0, bias=1.0)
    tt(s("gb"), s("gb"), R(1, 1), A.mult)
    for ih in range(2):
        act(h("fd", ih), s("ga"), scale=bc(0, ih))
        for k, x in enumerate((s("c21", 64, 128), C(0, 0), s("gb"), h("fd", ih))):
            mm(P(7, 64 * ih, 64 * ih + 64), s("idf"), x, k == 0, k == 3)
    act(s("fd"), P(7, 0, 128))
    mm(P(3, 64, 128), s("bo6"), s("ex", 0, 64), True, False); mm(P(3, 64, 128), s("nid"), s("cb", 128, 192), False, True)
    mm(P(3, 128, 192), s("bo6"), s("ex", 0, 64), True, False); mm(P(3, 128, 192), s("nid"), s("cb", 128, 192), False, False)
    mm(P(3, 128, 192), s("idb"), R(1, 2), False, True)
    tt(P(5, 384, 448), s("ga"), C(2, 0), A.mult)
    for ih in range(2):
        act(h("fa", ih), P(3, 64, 128), scale=4096.0, bias=bc(3, ih))
        act(h("fb", ih), P(3, 128, 192), bias=bc(1, ih))
        act(h("fe", ih), C(2, 2), scale=-8192.0, bias=bc(4, ih))
        tt(p5(0, ih), P(5, 384, 448), h("fd", ih), A.add)
    tt(s("fa"), s("fa"), s("fb"), A.min)
    tt(P(5, 0, 128), P(5, 0, 128), s("fe"), A.max)
    tt(P(5, 0, 128), P(5, 0, 128), s("fa"), A.max)
    for ih in range(2):
        ts(s("l_f", 2 + ih, 256, 4), p5(0, ih), float(ZC), A.min)
    act(s("ha"), R(0, 1), scale=-2.0, bias=1.0)
    act(s("hb"), R(0, 1), scale=20.0)
    act(s("hf"), R(0, 2), bias=float(U - 22))
    tt(s("hb"), s("hb"), s("c21", 0, 64), A.add)
    act(s("c1b"), C(1, 2))
    for ih in range(2):
        act(P(7, 64 * ih, 64 * ih + 64), C(1, 2), scale=-4096.0, bias=bc(3, ih))
        act(h("hq", ih), C(1, 2), bias=bc(5, ih))
        act(h("hr", ih), C(1, 0), bias=bc(0, ih))
    for k, n in enumerate(("fj", "fk")):
        if k: tt(s("fh"), s("hq"), s("hr"), A.add)
        x = "fh" if k else "hr"
        act(s("fg"), s(x), scale=4096.0, bias=float(TH - 4096 * 21))
        for ih in range(2):
            tt(p5(128, ih), h(x, ih), s("ha"), A.mult)
            tt(p5(256, ih), h(x, ih), s("hf"), A.add)
            tt(h("ff", ih), p5(128, ih), s("hb"), A.add)
        tt(P(5, 256, 384), P(5, 256, 384), s("fg"), A.min)
        tt(s(n), P(5, 256, 384), s("ff"), A.max)
    tt(s("fk"), s("fk"), s("fj"), A.subtract)
    mm(P(4, 0, 64), s("rs", 128, 256), dl(2), True, True)
    mm(P(6, 0, 64), s("rs", 0, 128), dl(2), True, False); mm(P(6, 0, 64), s("idb"), s("c1b"), False, True)
    mm(P(3, 0, 64), s("idb"), R(2, 2), True, False); mm(P(3, 0, 64), s("nid"), s("c1b"), False, True)
    for ih in range(2):
        tt(p5(128, ih), P(4, 0, 64), h("fk", ih), A.mult)
        act(h("hn", ih), P(3, 0, 64), bias=bc(2, ih))
        act(h("fc", ih), P(6, 0, 64), scale=-8192.0, bias=bc(4, ih))
    tt(P(5, 128, 256), P(5, 128, 256), s("fj"), A.add)
    tt(s("hn"), P(7, 0, 128), s("hn"), A.min)
    tt(P(5, 128, 256), P(5, 128, 256), s("fc"), A.max)
    tt(P(5, 256, 384), P(5, 128, 256), s("hn"), A.max)
    for ih in range(2):
        ts(s("l_f", ih, 256, 4), p5(256, ih), float(ZC), A.min)
    o = OFF["YO"][1]
    for f, a, b in ((act, 0, 1024), (act, 1024, 2048), (act, 2048, 3072), (cp, 3072, 4096)):
        f(s("YO", a, b), ind(s("numb"), s("l_f", a // 16, b // 16)))
    dma("s", T.yo[:, :], T.F[0:128:16, o:o + 4096], "so", r=[s("YO")])
    for f, a, b in YC:
        (cp if f else act)(s("G", a, b), ind(s("xb_"), s("l_f", a // 16, b // 16)))
        dma("s" if f else "a", T.y[:, a:b], s("G", a, b)[0], "so", r=[s("G", a, b)])

    order = [62 * DIGITS.index(ORDER[i]) + DIGITS.index(ORDER[i + 1]) for i in range(0, len(ORDER), 2)]
    assert sorted(order) == list(range(len(ops)))
    cnt = {}
    ev = {}
    know = {q: {} for q in Q}
    for i in order:
        q, fn, pre, kind, sem = ops[i]
        if kind == "x":
            cnt[sem] = len(eng); ev[i] = (sem, len(eng), {})
            continue
        need = {}
        for j in pre:
            sm, c, kn = ev[j]
            if q == "t" and ops[j][0] == q: continue
            if need.get(sm, (0,))[0] < c: need[sm] = (c, kn)
        for sm, (c, kn) in sorted(need.items(), key=lambda e: -len(e[1][1])):
            if know[q].get(sm, 0) < c:
                Q[q].wait_ge(T.sem[sm], c)
                know[q][sm] = c
                for k, x in kn.items():
                    if know[q].get(k, 0) < x: know[q][k] = x
        if kind == "r":
            fn(); cnt["ls"] = cnt.get("ls", 0) + len(eng); ev[i] = ("ls", cnt["ls"], {})
            continue
        sem = SEM[q] if kind == "c" else sem
        inc = 1 if kind == "c" else 16
        fn().then_inc(T.sem[sem], inc)
        cnt[sem] = cnt.get(sem, 0) + inc
        ev[i] = (sem, cnt[sem], dict(know[q]))
    for sem, c in cnt.items():
        g.wait_ge(T.sem[sem], c)
